import numpy as np
import ml_dtypes


def mxq(x, axis, fmt="e4m3"):
    dtype, down = {"e4m3": (ml_dtypes.float8_e4m3fn, 7), "e5m2": (ml_dtypes.float8_e5m2, 14)}[fmt]
    v = np.moveaxis(np.asarray(x, np.float32).astype(ml_dtypes.bfloat16).astype(np.float64), axis, -1)
    blocks = v.reshape(v.shape[:-1] + (-1, 32))
    amax = np.abs(blocks).max(-1, keepdims=True)
    byte = np.maximum(np.where(amax > 0, np.frexp(amax)[1] - 1 + 127, 0) - down, 1)
    scale = np.exp2(byte - 127.0)
    codes = (blocks / scale).astype(np.float32).astype(dtype).astype(np.float64)
    return np.moveaxis((codes * scale).reshape(v.shape), -1, axis)


WIDE = False


def mx_kscale(k):
    if not WIDE:
        return np.ones(k)
    levels = np.array([24, -24, 12, -12, 0])
    if k % 512:
        return np.exp2(np.random.permutation(np.resize(levels, k // 32))).repeat(32)
    a = np.empty((k // 512, 16))
    for p in range(k // 512):
        a[p, :8] = np.random.permutation(np.resize(levels, 8))
        for g in range(8):
            far = levels[np.abs(levels - a[p, g]) >= 10]
            a[p, g + 8] = far[np.random.randint(len(far))]
    return np.exp2(a.ravel()).repeat(32)


def f64(x):
    return np.asarray(x).astype(np.float64)


def striped(idx):
    return np.tile(idx.reshape(-1, 16).T, (8, 1)).astype(np.uint16)


def unstriped(offs):
    return offs[:16].T.reshape(-1).astype(np.int64)


E2M1 = np.array([0.0, 0.5, 1.0, 1.5, 2.0, 3.0, 4.0, 6.0, -0.0, -0.5, -1.0, -1.5, -2.0, -3.0, -4.0, -6.0])


def pack_weight(w, fmt):
    k, n = w.shape
    w = f64(np.asarray(w, np.float32).astype(ml_dtypes.bfloat16)).reshape(k // 32, 32, n)
    amax = np.abs(w).max(1)
    if fmt == "e4m3":
        byte = np.frexp(amax)[1] - 1 + 127 - 7
    else:
        mant, ex = np.frexp(amax / 6.0)
        byte = np.where(mant > 0.5, ex, ex - 1) + 127
    byte = np.clip(np.where(amax > 0, byte, 1), 1, 254)
    scaled = (w * np.exp2(127.0 - byte)[:, None, :]).reshape(k, n).astype(np.float32)
    by_word = np.ascontiguousarray(scaled.reshape(k // 512, 128, 4, n).transpose(0, 1, 3, 2))
    if fmt == "e4m3":
        words = by_word.astype(ml_dtypes.float8_e4m3fn).view(np.uint8)
    else:
        c = by_word.astype(ml_dtypes.float4_e2m1fn).view(np.uint8) & 0xF
        words = (c[..., 0::2] | (c[..., 1::2] << 4)).reshape(k // 512, 128, 2 * n)
    return np.ascontiguousarray(words), np.ascontiguousarray(byte.astype(np.uint8).reshape(k // 512, 16, n))


def unpack_weight(words, scales, fmt):
    g, _, n = scales.shape
    words = np.ascontiguousarray(words).reshape(g, 128, n, -1)
    if fmt == "e4m3":
        vals = words.view(ml_dtypes.float8_e4m3fn).astype(np.float64)
    else:
        nib = np.empty((g, 128, n, 4), np.uint8)
        nib[..., 0::2] = words & 0xF
        nib[..., 1::2] = words >> 4
        vals = E2M1[nib]
    vals = vals * np.repeat(np.exp2(scales.astype(np.float64) - 127.0), 8, axis=1)[..., None]
    return vals.transpose(0, 1, 3, 2).reshape(g * 512, n)


def gelu(f):
    return 0.5 * f * (1.0 + np.tanh(np.sqrt(2.0 / np.pi) * (f + 0.044715 * f**3)))


K, R, N, T, J = 512, 1024, 512, 4096, 2048


def setup_inputs():
    n = np.random.standard_normal
    s = mx_kscale(K)[:, None]
    u = mx_kscale(R)[:, None]
    p_tab = pack_weight(n((K, T)) * s, "e4m3")
    p_wg = pack_weight(n((K, R)) / np.sqrt(K) / s, "e4m3")
    p_wu = pack_weight(n((K, R)) / np.sqrt(K) / s * u.T, "e4m3")
    p_wd = pack_weight(n((R, N)) / np.sqrt(R) / u, "e2m1")
    return {
        "tab_words": p_tab[0],
        "tab_scales": p_tab[1],
        "wg_words": p_wg[0],
        "wg_scales": p_wg[1],
        "wu_words": p_wu[0],
        "wu_scales": p_wu[1],
        "wd_words": p_wd[0],
        "wd_scales": p_wd[1],
        "gT": (n((N, T))).astype(np.float32),
        "offs": striped(np.random.permutation(T)[:J]),
    }


def reference(tab_words, tab_scales, wg_words, wg_scales, wu_words, wu_scales, wd_words, wd_scales, gT, offs):
    idx = unstriped(offs)
    tab_ = unpack_weight(tab_words, tab_scales, "e4m3")[:, idx]
    wg_ = unpack_weight(wg_words, wg_scales, "e4m3")
    wu_ = unpack_weight(wu_words, wu_scales, "e4m3")
    ga = wg_.T @ tab_
    ub = wu_.T @ tab_
    h = gelu(ga) * ub
    h_ = mxq(h, 0, "e4m3")
    wd_ = unpack_weight(wd_words, wd_scales, "e2m1")
    y = wd_.T @ h_
    return y * f64(gT)[:, idx]

@@ -1,0 +1,186 @@
+from contextlib import ExitStack
+
+import concourse.mybir as mybir
+
+K, R, N, T, J = 512, 1024, 512, 4096, 2048
+FLOPS = 2 * K * R * J * 2 + 2 * R * N * J
+
+F32 = mybir.dt.float32
+BF16 = mybir.dt.bfloat16
+I32 = mybir.dt.int32
+U32 = mybir.dt.uint32
+U16 = mybir.dt.uint16
+U8 = mybir.dt.uint8
+FP8X4 = mybir.dt.float8_e4m3fn_x4
+FP4X4 = mybir.dt.float4_e2m1fn_x4
+MULT = mybir.AluOpType.mult
+GELU = mybir.ActivationFunctionType.Gelu_apprx_tanh
+
+P = 128
+PACK = 4
+PASS_ROWS = P * PACK
+R_PASSES = R // PASS_ROWS
+CHUNK = 512
+CHUNKS = J // CHUNK
+SUB = 128
+SUBS = CHUNK // SUB
+N_TILES = N // P
+WU_PLANE = 4
+
+
+def tile_list_gmlpt_gelu_gate_kernel(
+    tc, tab_words, tab_scales, wg_words, wg_scales, wu_words, wu_scales, wd_words, wd_scales, gT, offs, out
+):
+    nc = tc.nc
+    with ExitStack() as ctx:
+        held = ctx.enter_context(tc.tile_pool(name="held", bufs=1))
+        ring = ctx.enter_context(tc.tile_pool(name="ring", bufs=3))
+        psum = ctx.enter_context(tc.psum_pool(name="psum", bufs=1))
+
+        offsets = held.tile([P, J // 16], U16, name="offsets")
+        nc.sync.dma_start(offsets[:], offs)
+
+        tab_plane = held.tile([P, T], U8, name="tab_plane", align_bytes=64)
+        nc.vector.memset(tab_plane[:].bitcast(I32), 0)
+        w_plane_raw = held.tile([P, R], U8, name="w_plane_raw", align_bytes=64)
+        nc.vector.memset(w_plane_raw[:].bitcast(I32), 0)
+        wd_plane = held.tile([P, R_PASSES * N], U8, name="wd_plane", align_bytes=64)
+        nc.vector.memset(wd_plane[:].bitcast(I32), 0)
+
+        warm = held.tile([P, 1], F32, name="warm")
+        nc.vector.memset(warm[:], 0.0)
+        warm_out = held.tile([P, 1], F32, name="warm_out")
+        nc.scalar.activation(warm_out[:], warm[:], GELU)
+
+        raw = []
+        for name, words in (("wg_raw", wg_words), ("wu_raw", wu_words)):
+            w_raw = held.tile([P, R], I32, name=name, align_bytes=64)
+            nc.sync.dma_start(w_raw[:], words[0].rearrange("p n t -> p (n t)").bitcast(I32))
+            raw.append(w_raw)
+        for q in range(4):
+            nc.sync.dma_start(
+                tab_plane[32 * q : 32 * q + 4, :].bitcast(I32), tab_scales[0, 4 * q : 4 * q + 4, :].bitcast(I32)
+            )
+        for q in range(4):
+            for first, scales in ((0, wg_scales), (WU_PLANE, wu_scales)):
+                nc.sync.dma_start(
+                    w_plane_raw[32 * q + first : 32 * q + first + 4, :].bitcast(I32),
+                    scales[0, 4 * q : 4 * q + 4, :].bitcast(I32),
+                )
+        tab = held.tile([P, T], U32, name="tab", align_bytes=64)
+        nc.sync.dma_start(tab[:].bitcast(I32), tab_words[0].rearrange("p n t -> p (n t)").bitcast(I32))
+        wd = held.tile([P, R_PASSES, 2 * N], U8, name="wd", align_bytes=64)
+        nc.sync.dma_start(wd[:].bitcast(I32), wd_words.rearrange("a p n -> p a n").bitcast(I32))
+        for q in range(4):
+            nc.sync.dma_start(
+                wd_plane[32 * q : 32 * q + 4, :].bitcast(I32).rearrange("p (a n) -> p a n", a=R_PASSES),
+                wd_scales[:, 4 * q : 4 * q + 4, :].rearrange("a r n -> r a n").bitcast(I32),
+            )
+        gates = []
+        for n in range(N_TILES):
+            gate = held.tile([P, T], F32, name="gate%d" % n, align_bytes=64)
+            nc.sync.dma_start(gate[:], gT[n * P : (n + 1) * P, :])
+            gates.append(gate)
+
+        dealt = []
+        for name, w_raw in zip(("wg", "wu"), raw):
+            w = held.tile([P, R], I32, name=name, align_bytes=64)
+            nc.vector.tensor_copy(
+                w[:].rearrange("p (a t c i) -> p a c t i", a=R_PASSES, t=PACK, i=4),
+                w_raw[:].rearrange("p (a c i t) -> p a c t i", a=R_PASSES, t=PACK, i=4),
+            )
+            dealt.append(w)
+        wg, wu = dealt
+
+        def chunk_offsets(c):
+            return offsets[:, c * (CHUNK // 16) : (c + 1) * (CHUNK // 16)]
+
+        x_words, x_planes = {}, {}
+
+        def gather_plane(c):
+            x_planes[c] = held.tile([P, CHUNK], U8, name="x_plane%d" % c, align_bytes=64)
+            nc.vector.tensor_copy(x_planes[c][:], tab_plane[:].indirect(chunk_offsets(c)))
+
+        def gather_words(c):
+            x_words[c] = held.tile([P, CHUNK], U32, name="x_words%d" % c, align_bytes=64)
+            nc.vector.tensor_copy(x_words[c][:], tab[:].indirect(chunk_offsets(c)))
+
+        for c in range(CHUNKS):
+            gather_plane(c)
+        w_plane = held.tile([P, R], U8, name="w_plane", align_bytes=64)
+        nc.vector.tensor_copy(
+            w_plane[:].rearrange("p (a t m) -> p a t m", a=R_PASSES, t=PACK),
+            w_plane_raw[:].rearrange("p (a m t) -> p a t m", a=R_PASSES, t=PACK),
+        )
+        gather_words(0)
+
+
+        h_tiles, h_codes, h_planes, y_tiles = {}, {}, {}, {}
+
+        def hidden(c, a, s):
+            if s == 0:
+                h_tiles[c, a] = ring.tile([P, CHUNK * PACK], BF16, name="h", align_bytes=64)
+            cols = slice(s * SUB, (s + 1) * SUB)
+            banks = []
+            for tag, w, first in (("ga", wg, 0), ("ub", wu, WU_PLANE)):
+                bank = psum.tile([P, PACK, SUB], F32, name=tag, bufs=3)
+                for t in range(PACK):
+                    w_cols = slice(a * PASS_ROWS + t * P, a * PASS_ROWS + (t + 1) * P)
+                    nc.tensor.matmul_mx(
+                        out=bank[:, t, :],
+                        lhsT=w[:, w_cols].bitcast(FP8X4),
+                        lhsT_scale=w_plane[first:P, w_cols],
+                        rhs=x_words[c][:, cols].bitcast(FP8X4),
+                        rhs_scale=x_planes[c][:, cols],
+                        start=True,
+                        stop=True,
+                    )
+                banks.append(bank)
+            ga, ub = banks
+            act = ring.tile([P, SUB, PACK], F32, name="act", align_bytes=64)
+            nc.scalar.activation(act[:], ga[:].rearrange("p t j -> p j t"), GELU)
+            nc.vector.tensor_tensor(
+                h_tiles[c, a][:, s * SUB * PACK : (s + 1) * SUB * PACK].rearrange("p (j t) -> p j t", t=PACK),
+                ub[:].rearrange("p t j -> p j t"),
+                act[:],
+                MULT,
+            )
+
+        def quantise(c, a):
+            h_codes[c, a] = ring.tile([P, CHUNK], U32, name="h_codes", align_bytes=64, bufs=4)
+            h_planes[c, a] = ring.tile([P, CHUNK], U8, name="h_plane", align_bytes=64, bufs=4)
+            nc.vector.quantize_mx(out=h_codes[c, a][:].bitcast(FP8X4), scales=h_planes[c, a][:], in_=h_tiles[c, a][:])
+
+        def down(c):
+            for n in range(N_TILES):
+                bank = psum.tile([P, CHUNK], F32, name="y_bank", bufs=2)
+                for a in range(R_PASSES):
+                    nc.tensor.matmul_mx(
+                        out=bank[:],
+                        lhsT=wd[:, a, 2 * n * P : 2 * (n + 1) * P].bitcast(FP4X4),
+                        lhsT_scale=wd_plane[:, a * N + n * P : a * N + (n + 1) * P],
+                        rhs=h_codes[c, a][:].bitcast(FP8X4),
+                        rhs_scale=h_planes[c, a][:],
+                        start=(a == 0),
+                        stop=(a == R_PASSES - 1),
+                    )
+                y_tiles[c, n] = ring.tile([P, CHUNK], F32, name="y", align_bytes=64, bufs=8)
+                nc.scalar.copy(y_tiles[c, n][:], bank[:])
+
+        def gate_and_store(c, n):
+            res = ring.tile([P, CHUNK], F32, name="res", align_bytes=64, bufs=4)
+            nc.vector.tensor_tensor(res[:], gates[n][:].indirect(chunk_offsets(c)), y_tiles[c, n][:], MULT)
+            nc.sync.dma_start(out[n * P : (n + 1) * P, c * CHUNK : (c + 1) * CHUNK], res[:])
+
+        fill = [lambda c=c: gather_words(c) for c in range(1, CHUNKS)]
+        for c in range(CHUNKS):
+            for a in range(R_PASSES):
+                for s in range(SUBS):
+                    hidden(c, a, s)
+                    if s % 2 == 1 and fill:
+                        fill.pop(0)()
+                quantise(c, a)
+            down(c)
+            fill.extend([lambda c=c, n=n: gate_and_store(c, n) for n in range(N_TILES)])
+        for step in fill:
+            step()

@@ -42,7 +42,7 @@ def tile_list_gmlpt_gelu_gate_kernel(
 
         tab_plane = held.tile([P, T], U8, name="tab_plane", align_bytes=64)
         nc.vector.memset(tab_plane[:].bitcast(I32), 0)
-        w_plane_raw = held.tile([P, R], U8, name="w_plane_raw", align_bytes=64)
+        w_plane_raw = held.tile([P, R], U8, name="w_plane_raw", tag="late", align_bytes=64)
         nc.vector.memset(w_plane_raw[:].bitcast(I32), 0)
         wd_plane = held.tile([P, R_PASSES * N], U8, name="wd_plane", align_bytes=64)
         nc.vector.memset(wd_plane[:].bitcast(I32), 0)
@@ -61,18 +61,18 @@ def tile_list_gmlpt_gelu_gate_kernel(
             nc.sync.dma_start(
                 tab_plane[32 * q : 32 * q + 4, :].bitcast(I32), tab_scales[0, 4 * q : 4 * q + 4, :].bitcast(I32)
             )
+        tab = held.tile([P, T], U32, name="tab", align_bytes=64)
+        nc.sync.dma_start(tab[:].bitcast(I32), tab_words[0].rearrange("p n t -> p (n t)").bitcast(I32))
         for q in range(4):
             for first, scales in ((0, wg_scales), (WU_PLANE, wu_scales)):
-                nc.sync.dma_start(
+                nc.gpsimd.dma_start(
                     w_plane_raw[32 * q + first : 32 * q + first + 4, :].bitcast(I32),
                     scales[0, 4 * q : 4 * q + 4, :].bitcast(I32),
                 )
-        tab = held.tile([P, T], U32, name="tab", align_bytes=64)
-        nc.sync.dma_start(tab[:].bitcast(I32), tab_words[0].rearrange("p n t -> p (n t)").bitcast(I32))
         wd = held.tile([P, R_PASSES, 2 * N], U8, name="wd", align_bytes=64)
         nc.sync.dma_start(wd[:].bitcast(I32), wd_words.rearrange("a p n -> p a n").bitcast(I32))
         for q in range(4):
-            nc.sync.dma_start(
+            nc.gpsimd.dma_start(
                 wd_plane[32 * q : 32 * q + 4, :].bitcast(I32).rearrange("p (a n) -> p a n", a=R_PASSES),
                 wd_scales[:, 4 * q : 4 * q + 4, :].rearrange("a r n -> r a n").bitcast(I32),
             )
@@ -95,35 +95,33 @@ def tile_list_gmlpt_gelu_gate_kernel(
         def chunk_offsets(c):
             return offsets[:, c * (CHUNK // 16) : (c + 1) * (CHUNK // 16)]
 
-        x_words, x_planes = {}, {}
-
-        def gather_plane(c):
-            x_planes[c] = held.tile([P, CHUNK], U8, name="x_plane%d" % c, align_bytes=64)
-            nc.vector.tensor_copy(x_planes[c][:], tab_plane[:].indirect(chunk_offsets(c)))
-
-        def gather_words(c):
-            x_words[c] = held.tile([P, CHUNK], U32, name="x_words%d" % c, align_bytes=64)
-            nc.vector.tensor_copy(x_words[c][:], tab[:].indirect(chunk_offsets(c)))
-
-        for c in range(CHUNKS):
-            gather_plane(c)
+        x_words = {}
+        x_plane = held.tile([P, J], U8, name="x_plane", align_bytes=64)
+        nc.vector.tensor_copy(x_plane[:], tab_plane[:].indirect(offsets[:]))
         w_plane = held.tile([P, R], U8, name="w_plane", align_bytes=64)
         nc.vector.tensor_copy(
             w_plane[:].rearrange("p (a t m) -> p a t m", a=R_PASSES, t=PACK),
             w_plane_raw[:].rearrange("p (a m t) -> p a t m", a=R_PASSES, t=PACK),
         )
-        gather_words(0)
+        for c in range(2):
+            x_words[c] = held.tile([P, CHUNK], U32, name="x_words%d" % c, align_bytes=64)[:]
+            nc.vector.tensor_copy(x_words[c], tab[:].indirect(chunk_offsets(c)))
+        late_words = held.tile([P, 2 * CHUNK], U32, name="late_words", tag="late", align_bytes=64)
+        nc.vector.tensor_copy(late_words[:], tab[:].indirect(offsets[:, 2 * (CHUNK // 16) :]))
+        for c in range(2, CHUNKS):
+            x_words[c] = late_words[:, (c - 2) * CHUNK : (c - 1) * CHUNK]
+        hand = [held.tile([P, CHUNK], F32, name="hand%d" % n, align_bytes=64) for n in range(N_TILES)]
 
 
         h_tiles, h_codes, h_planes, y_tiles = {}, {}, {}, {}
 
-        def hidden(c, a, s):
+        def hidden(c, a, s, act):
             if s == 0:
                 h_tiles[c, a] = ring.tile([P, CHUNK * PACK], BF16, name="h", align_bytes=64)
             cols = slice(s * SUB, (s + 1) * SUB)
             banks = []
-            for tag, w, first in (("ga", wg, 0), ("ub", wu, WU_PLANE)):
-                bank = psum.tile([P, PACK, SUB], F32, name=tag, bufs=3)
+            for tag, w, first, bufs in (("ga", wg, 0, 2), ("ub", wu, WU_PLANE, 4)):
+                bank = psum.tile([P, PACK, SUB], F32, name=tag, bufs=bufs)
                 for t in range(PACK):
                     w_cols = slice(a * PASS_ROWS + t * P, a * PASS_ROWS + (t + 1) * P)
                     nc.tensor.matmul_mx(
@@ -131,18 +129,18 @@ def tile_list_gmlpt_gelu_gate_kernel(
                         lhsT=w[:, w_cols].bitcast(FP8X4),
                         lhsT_scale=w_plane[first:P, w_cols],
                         rhs=x_words[c][:, cols].bitcast(FP8X4),
-                        rhs_scale=x_planes[c][:, cols],
+                        rhs_scale=x_plane[:, c * CHUNK + s * SUB : c * CHUNK + (s + 1) * SUB],
                         start=True,
                         stop=True,
                     )
                 banks.append(bank)
             ga, ub = banks
-            act = ring.tile([P, SUB, PACK], F32, name="act", align_bytes=64)
-            nc.scalar.activation(act[:], ga[:].rearrange("p t j -> p j t"), GELU)
+            act = act[:].rearrange("p (j t) -> p j t", t=PACK)
+            nc.scalar.activation(act, ga[:].rearrange("p t j -> p j t"), GELU)
             nc.vector.tensor_tensor(
                 h_tiles[c, a][:, s * SUB * PACK : (s + 1) * SUB * PACK].rearrange("p (j t) -> p j t", t=PACK),
                 ub[:].rearrange("p t j -> p j t"),
-                act[:],
+                act,
                 MULT,
             )
 
@@ -151,36 +149,51 @@ def tile_list_gmlpt_gelu_gate_kernel(
             h_planes[c, a] = ring.tile([P, CHUNK], U8, name="h_plane", align_bytes=64, bufs=4)
             nc.vector.quantize_mx(out=h_codes[c, a][:].bitcast(FP8X4), scales=h_planes[c, a][:], in_=h_tiles[c, a][:])
 
-        def down(c):
-            for n in range(N_TILES):
-                bank = psum.tile([P, CHUNK], F32, name="y_bank", bufs=2)
-                for a in range(R_PASSES):
-                    nc.tensor.matmul_mx(
-                        out=bank[:],
-                        lhsT=wd[:, a, 2 * n * P : 2 * (n + 1) * P].bitcast(FP4X4),
-                        lhsT_scale=wd_plane[:, a * N + n * P : a * N + (n + 1) * P],
-                        rhs=h_codes[c, a][:].bitcast(FP8X4),
-                        rhs_scale=h_planes[c, a][:],
-                        start=(a == 0),
-                        stop=(a == R_PASSES - 1),
-                    )
-                y_tiles[c, n] = ring.tile([P, CHUNK], F32, name="y", align_bytes=64, bufs=8)
-                nc.scalar.copy(y_tiles[c, n][:], bank[:])
+        def down(c, n, y):
+            bank = psum.tile([P, CHUNK], F32, name="y_bank", bufs=2)
+            for a in range(R_PASSES):
+                nc.tensor.matmul_mx(
+                    out=bank[:],
+                    lhsT=wd[:, a, 2 * n * P : 2 * (n + 1) * P].bitcast(FP4X4),
+                    lhsT_scale=wd_plane[:, a * N + n * P : a * N + (n + 1) * P],
+                    rhs=h_codes[c, a][:].bitcast(FP8X4),
+                    rhs_scale=h_planes[c, a][:],
+                    start=(a == 0),
+                    stop=(a == R_PASSES - 1),
+                )
+            nc.scalar.copy(y[:], bank[:])
+            y_tiles[c, n] = y
 
         def gate_and_store(c, n):
             res = ring.tile([P, CHUNK], F32, name="res", align_bytes=64, bufs=4)
             nc.vector.tensor_tensor(res[:], gates[n][:].indirect(chunk_offsets(c)), y_tiles[c, n][:], MULT)
             nc.sync.dma_start(out[n * P : (n + 1) * P, c * CHUNK : (c + 1) * CHUNK], res[:])
 
-        fill = [lambda c=c: gather_words(c) for c in range(1, CHUNKS)]
+        units = R_PASSES * SUBS
         for c in range(CHUNKS):
-            for a in range(R_PASSES):
-                for s in range(SUBS):
-                    hidden(c, a, s)
-                    if s % 2 == 1 and fill:
-                        fill.pop(0)()
-                quantise(c, a)
-            down(c)
-            fill.extend([lambda c=c, n=n: gate_and_store(c, n) for n in range(N_TILES)])
-        for step in fill:
-            step()
+            after = (0, 2, 4, 6) if c < CHUNKS - 1 else (1, 4, 6, 7)
+            waiting = []
+            for u in range(units):
+                a, s = divmod(u, SUBS)
+                if u in after:
+                    act = hand[after.index(u)]
+                else:
+                    act = ring.tile([P, CHUNK], F32, name="act", align_bytes=64)
+                hidden(c, a, s, act)
+                last = c == CHUNKS - 1 and u == units - 1
+                if last:
+                    quantise(c, a)
+                for n in waiting:
+                    gate_and_store(c - 1, n)
+                waiting = []
+                if s == SUBS - 1 and not last:
+                    quantise(c, a)
+                if c > 0 and u in after:
+                    down(c - 1, after.index(u), act)
+                    waiting.append(after.index(u))
+            for n in waiting:
+                gate_and_store(c - 1, n)
+        for n in range(N_TILES):
+            y = ring.tile([P, CHUNK], F32, name="y", align_bytes=64, bufs=4)
+            down(CHUNKS - 1, n, y)
+            gate_and_store(CHUNKS - 1, n)

@@ -42,7 +42,7 @@ def tile_list_gmlpt_gelu_gate_kernel(
 
         tab_plane = held.tile([P, T], U8, name="tab_plane", align_bytes=64)
         nc.vector.memset(tab_plane[:].bitcast(I32), 0)
-        w_plane_raw = held.tile([P, R], U8, name="w_plane_raw", tag="late", align_bytes=64)
+        w_plane_raw = held.tile([P, R], U8, name="w_plane_raw", align_bytes=64)
         nc.vector.memset(w_plane_raw[:].bitcast(I32), 0)
         wd_plane = held.tile([P, R_PASSES * N], U8, name="wd_plane", align_bytes=64)
         nc.vector.memset(wd_plane[:].bitcast(I32), 0)
@@ -52,6 +52,27 @@ def tile_list_gmlpt_gelu_gate_kernel(
         warm_out = held.tile([P, 1], F32, name="warm_out")
         nc.scalar.activation(warm_out[:], warm[:], GELU)
 
+        wd = held.tile([P, R_PASSES, 2 * N], U8, name="wd", align_bytes=64)
+        for a in range(R_PASSES):
+            nc.sync.dma_start(wd[:, a, :].bitcast(I32), wd_words[a].bitcast(I32))
+        for q in range(4):
+            nc.sync.dma_start(
+                tab_plane[32 * q : 32 * q + 4, :].bitcast(I32), tab_scales[0, 4 * q : 4 * q + 4, :].bitcast(I32)
+            )
+
+        def load_w_rows(q, first, scales):
+            nc.sync.dma_start(
+                w_plane_raw[32 * q + first : 32 * q + first + 4, :].bitcast(I32),
+                scales[0, 4 * q : 4 * q + 4, :].bitcast(I32),
+            )
+
+        w_rows = [(q, first, scales) for first, scales in ((0, wg_scales), (WU_PLANE, wu_scales)) for q in range(4)]
+        for rows in w_rows[:3]:
+            load_w_rows(*rows)
+        tab = held.tile([P, T], U32, name="tab", align_bytes=64)
+        nc.sync.dma_start(tab[:].bitcast(I32), tab_words[0].rearrange("p n t -> p (n t)").bitcast(I32))
+        for rows in w_rows[3:]:
+            load_w_rows(*rows)
         raw = []
         for name, words in (("wg_raw", wg_words), ("wu_raw", wu_words)):
             w_raw = held.tile([P, R], I32, name=name, align_bytes=64)
@@ -59,20 +80,6 @@ def tile_list_gmlpt_gelu_gate_kernel(
             raw.append(w_raw)
         for q in range(4):
             nc.sync.dma_start(
-                tab_plane[32 * q : 32 * q + 4, :].bitcast(I32), tab_scales[0, 4 * q : 4 * q + 4, :].bitcast(I32)
-            )
-        tab = held.tile([P, T], U32, name="tab", align_bytes=64)
-        nc.sync.dma_start(tab[:].bitcast(I32), tab_words[0].rearrange("p n t -> p (n t)").bitcast(I32))
-        for q in range(4):
-            for first, scales in ((0, wg_scales), (WU_PLANE, wu_scales)):
-                nc.gpsimd.dma_start(
-                    w_plane_raw[32 * q + first : 32 * q + first + 4, :].bitcast(I32),
-                    scales[0, 4 * q : 4 * q + 4, :].bitcast(I32),
-                )
-        wd = held.tile([P, R_PASSES, 2 * N], U8, name="wd", align_bytes=64)
-        nc.sync.dma_start(wd[:].bitcast(I32), wd_words.rearrange("a p n -> p a n").bitcast(I32))
-        for q in range(4):
-            nc.gpsimd.dma_start(
                 wd_plane[32 * q : 32 * q + 4, :].bitcast(I32).rearrange("p (a n) -> p a n", a=R_PASSES),
                 wd_scales[:, 4 * q : 4 * q + 4, :].rearrange("a r n -> r a n").bitcast(I32),
             )
@@ -82,6 +89,20 @@ def tile_list_gmlpt_gelu_gate_kernel(
             nc.sync.dma_start(gate[:], gT[n * P : (n + 1) * P, :])
             gates.append(gate)
 
+        def chunk_offsets(c):
+            return offsets[:, c * (CHUNK // 16) : (c + 1) * (CHUNK // 16)]
+
+        x_words = {}
+        x_plane = held.tile([P, J], U8, name="x_plane", align_bytes=64)
+        nc.vector.tensor_copy(x_plane[:], tab_plane[:].indirect(offsets[:]))
+        for c in range(2):
+            x_words[c] = held.tile([P, CHUNK], U32, name="x_words%d" % c, align_bytes=64)[:]
+            nc.vector.tensor_copy(x_words[c], tab[:].indirect(chunk_offsets(c)))
+        w_plane = held.tile([P, R], U8, name="w_plane", align_bytes=64)
+        nc.vector.tensor_copy(
+            w_plane[:].rearrange("p (a t m) -> p a t m", a=R_PASSES, t=PACK),
+            w_plane_raw[:].rearrange("p (a m t) -> p a t m", a=R_PASSES, t=PACK),
+        )
         dealt = []
         for name, w_raw in zip(("wg", "wu"), raw):
             w = held.tile([P, R], I32, name=name, align_bytes=64)
@@ -92,21 +113,7 @@ def tile_list_gmlpt_gelu_gate_kernel(
             dealt.append(w)
         wg, wu = dealt
 
-        def chunk_offsets(c):
-            return offsets[:, c * (CHUNK // 16) : (c + 1) * (CHUNK // 16)]
-
-        x_words = {}
-        x_plane = held.tile([P, J], U8, name="x_plane", align_bytes=64)
-        nc.vector.tensor_copy(x_plane[:], tab_plane[:].indirect(offsets[:]))
-        w_plane = held.tile([P, R], U8, name="w_plane", align_bytes=64)
-        nc.vector.tensor_copy(
-            w_plane[:].rearrange("p (a t m) -> p a t m", a=R_PASSES, t=PACK),
-            w_plane_raw[:].rearrange("p (a m t) -> p a t m", a=R_PASSES, t=PACK),
-        )
-        for c in range(2):
-            x_words[c] = held.tile([P, CHUNK], U32, name="x_words%d" % c, align_bytes=64)[:]
-            nc.vector.tensor_copy(x_words[c], tab[:].indirect(chunk_offsets(c)))
-        late_words = held.tile([P, 2 * CHUNK], U32, name="late_words", tag="late", align_bytes=64)
+        late_words = held.tile([P, 2 * CHUNK], U32, name="late_words", tag="wu_raw", align_bytes=64)
         nc.vector.tensor_copy(late_words[:], tab[:].indirect(offsets[:, 2 * (CHUNK // 16) :]))
         for c in range(2, CHUNKS):
             x_words[c] = late_words[:, (c - 2) * CHUNK : (c - 1) * CHUNK]

@@ -26,6 +26,7 @@ SUB = 128
 SUBS = CHUNK // SUB
 N_TILES = N // P
 WU_PLANE = 4
+GPSIMD_SUB = 1
 
 
 def tile_list_gmlpt_gelu_gate_kernel(
@@ -43,18 +44,15 @@ def tile_list_gmlpt_gelu_gate_kernel(
         tab_plane = held.tile([P, T], U8, name="tab_plane", align_bytes=64)
         nc.vector.memset(tab_plane[:].bitcast(I32), 0)
         w_plane_raw = held.tile([P, R], U8, name="w_plane_raw", align_bytes=64)
-        nc.vector.memset(w_plane_raw[:].bitcast(I32), 0)
+        nc.gpsimd.memset(w_plane_raw[:].bitcast(I32), 0)
         wd_plane = held.tile([P, R_PASSES * N], U8, name="wd_plane", align_bytes=64)
-        nc.vector.memset(wd_plane[:].bitcast(I32), 0)
+        nc.gpsimd.memset(wd_plane[:].bitcast(I32), 0)
 
         warm = held.tile([P, 1], F32, name="warm")
-        nc.vector.memset(warm[:], 0.0)
+        nc.gpsimd.memset(warm[:], 0.0)
         warm_out = held.tile([P, 1], F32, name="warm_out")
         nc.scalar.activation(warm_out[:], warm[:], GELU)
 
-        wd = held.tile([P, R_PASSES, 2 * N], U8, name="wd", align_bytes=64)
-        for a in range(R_PASSES):
-            nc.sync.dma_start(wd[:, a, :].bitcast(I32), wd_words[a].bitcast(I32))
         for q in range(4):
             nc.sync.dma_start(
                 tab_plane[32 * q : 32 * q + 4, :].bitcast(I32), tab_scales[0, 4 * q : 4 * q + 4, :].bitcast(I32)
@@ -73,11 +71,16 @@ def tile_list_gmlpt_gelu_gate_kernel(
         nc.sync.dma_start(tab[:].bitcast(I32), tab_words[0].rearrange("p n t -> p (n t)").bitcast(I32))
         for rows in w_rows[3:]:
             load_w_rows(*rows)
-        raw = []
-        for name, words in (("wg_raw", wg_words), ("wu_raw", wu_words)):
-            w_raw = held.tile([P, R], I32, name=name, align_bytes=64)
-            nc.sync.dma_start(w_raw[:], words[0].rearrange("p n t -> p (n t)").bitcast(I32))
-            raw.append(w_raw)
+        raw = {}
+        for a in range(R_PASSES):
+            for name, words in (("wg", wg_words), ("wu", wu_words)):
+                raw[name, a] = held.tile([P, PASS_ROWS], I32, name="%s_raw%d" % (name, a), align_bytes=64)
+                nc.sync.dma_start(
+                    raw[name, a][:],
+                    words[0, :, a * PASS_ROWS : (a + 1) * PASS_ROWS, :].rearrange("p n t -> p (n t)").bitcast(I32),
+                )
+        wd = held.tile([P, R_PASSES, 2 * N], U8, name="wd", align_bytes=64)
+        nc.sync.dma_start(wd[:].bitcast(I32), wd_words.rearrange("a p n -> p a n").bitcast(I32))
         for q in range(4):
             nc.sync.dma_start(
                 wd_plane[32 * q : 32 * q + 4, :].bitcast(I32).rearrange("p (a n) -> p a n", a=R_PASSES),
@@ -95,45 +98,43 @@ def tile_list_gmlpt_gelu_gate_kernel(
         x_words = {}
         x_plane = held.tile([P, J], U8, name="x_plane", align_bytes=64)
         nc.vector.tensor_copy(x_plane[:], tab_plane[:].indirect(offsets[:]))
-        for c in range(2):
-            x_words[c] = held.tile([P, CHUNK], U32, name="x_words%d" % c, align_bytes=64)[:]
-            nc.vector.tensor_copy(x_words[c], tab[:].indirect(chunk_offsets(c)))
+
+        def gather_words(c, tag):
+            x_words[c] = held.tile([P, CHUNK], U32, name="x_words%d" % c, tag=tag, align_bytes=64)
+            nc.vector.tensor_copy(x_words[c][:], tab[:].indirect(chunk_offsets(c)))
+
+        gather_words(0, "x_words0")
         w_plane = held.tile([P, R], U8, name="w_plane", align_bytes=64)
         nc.vector.tensor_copy(
             w_plane[:].rearrange("p (a t m) -> p a t m", a=R_PASSES, t=PACK),
             w_plane_raw[:].rearrange("p (a m t) -> p a t m", a=R_PASSES, t=PACK),
         )
-        dealt = []
-        for name, w_raw in zip(("wg", "wu"), raw):
-            w = held.tile([P, R], I32, name=name, align_bytes=64)
-            nc.vector.tensor_copy(
-                w[:].rearrange("p (a t c i) -> p a c t i", a=R_PASSES, t=PACK, i=4),
-                w_raw[:].rearrange("p (a c i t) -> p a c t i", a=R_PASSES, t=PACK, i=4),
-            )
-            dealt.append(w)
-        wg, wu = dealt
-
-        late_words = held.tile([P, 2 * CHUNK], U32, name="late_words", tag="wu_raw", align_bytes=64)
-        nc.vector.tensor_copy(late_words[:], tab[:].indirect(offsets[:, 2 * (CHUNK // 16) :]))
-        for c in range(2, CHUNKS):
-            x_words[c] = late_words[:, (c - 2) * CHUNK : (c - 1) * CHUNK]
-        hand = [held.tile([P, CHUNK], F32, name="hand%d" % n, align_bytes=64) for n in range(N_TILES)]
+        dealt = {}
+        for a in range(R_PASSES):
+            for name in ("wg", "wu"):
+                dealt[name, a] = held.tile([P, PASS_ROWS], I32, name="%s%d" % (name, a), align_bytes=64)
+                nc.vector.tensor_copy(
+                    dealt[name, a][:].rearrange("p (t c i) -> p c t i", t=PACK, i=4),
+                    raw[name, a][:].rearrange("p (c i t) -> p c t i", t=PACK, i=4),
+                )
+        gather_words(1, "wu_raw1")
+        hand = [held.tile([P, CHUNK], F32, name="hand%d" % i, align_bytes=64) for i in range(6)]
 
 
         h_tiles, h_codes, h_planes, y_tiles = {}, {}, {}, {}
 
         def hidden(c, a, s, act):
             if s == 0:
-                h_tiles[c, a] = ring.tile([P, CHUNK * PACK], BF16, name="h", align_bytes=64)
+                h_tiles[c, a] = ring.tile([P, CHUNK * PACK], BF16, name="h", align_bytes=64, bufs=1)
             cols = slice(s * SUB, (s + 1) * SUB)
             banks = []
-            for tag, w, first, bufs in (("ga", wg, 0, 2), ("ub", wu, WU_PLANE, 4)):
+            for tag, name, first, bufs in (("ga", "wg", 0, 2), ("ub", "wu", WU_PLANE, 4)):
                 bank = psum.tile([P, PACK, SUB], F32, name=tag, bufs=bufs)
                 for t in range(PACK):
                     w_cols = slice(a * PASS_ROWS + t * P, a * PASS_ROWS + (t + 1) * P)
                     nc.tensor.matmul_mx(
                         out=bank[:, t, :],
-                        lhsT=w[:, w_cols].bitcast(FP8X4),
+                        lhsT=dealt[name, a][:, t * P : (t + 1) * P].bitcast(FP8X4),
                         lhsT_scale=w_plane[first:P, w_cols],
                         rhs=x_words[c][:, cols].bitcast(FP8X4),
                         rhs_scale=x_plane[:, c * CHUNK + s * SUB : c * CHUNK + (s + 1) * SUB],
@@ -144,19 +145,20 @@ def tile_list_gmlpt_gelu_gate_kernel(
             ga, ub = banks
             act = act[:].rearrange("p (j t) -> p j t", t=PACK)
             nc.scalar.activation(act, ga[:].rearrange("p t j -> p j t"), GELU)
-            nc.vector.tensor_tensor(
-                h_tiles[c, a][:, s * SUB * PACK : (s + 1) * SUB * PACK].rearrange("p (j t) -> p j t", t=PACK),
-                ub[:].rearrange("p t j -> p j t"),
-                act,
-                MULT,
-            )
+            h = h_tiles[c, a][:, s * SUB * PACK : (s + 1) * SUB * PACK].rearrange("p (j t) -> p j t", t=PACK)
+            if c > 0 and s == GPSIMD_SUB:
+                ub_copy = ring.tile([P, SUB, PACK], F32, name="ub_copy", align_bytes=64, bufs=2)
+                nc.scalar.copy(ub_copy[:], ub[:].rearrange("p t j -> p j t"))
+                nc.gpsimd.tensor_tensor(h, ub_copy[:], act, MULT)
+            else:
+                nc.vector.tensor_tensor(h, ub[:].rearrange("p t j -> p j t"), act, MULT)
 
         def quantise(c, a):
-            h_codes[c, a] = ring.tile([P, CHUNK], U32, name="h_codes", align_bytes=64, bufs=4)
-            h_planes[c, a] = ring.tile([P, CHUNK], U8, name="h_plane", align_bytes=64, bufs=4)
+            h_codes[c, a] = ring.tile([P, CHUNK], U32, name="h_codes", align_bytes=64, bufs=6)
+            h_planes[c, a] = ring.tile([P, CHUNK], U8, name="h_plane", align_bytes=64, bufs=6)
             nc.vector.quantize_mx(out=h_codes[c, a][:].bitcast(FP8X4), scales=h_planes[c, a][:], in_=h_tiles[c, a][:])
 
-        def down(c, n, y):
+        def down(c, n):
             bank = psum.tile([P, CHUNK], F32, name="y_bank", bufs=2)
             for a in range(R_PASSES):
                 nc.tensor.matmul_mx(
@@ -168,39 +170,44 @@ def tile_list_gmlpt_gelu_gate_kernel(
                     start=(a == 0),
                     stop=(a == R_PASSES - 1),
                 )
-            nc.scalar.copy(y[:], bank[:])
-            y_tiles[c, n] = y
+            y_tiles[c, n] = ring.tile([P, CHUNK], F32, name="y", align_bytes=64, bufs=6)
+            nc.scalar.copy(y_tiles[c, n][:], bank[:])
 
-        def gate_and_store(c, n):
-            res = ring.tile([P, CHUNK], F32, name="res", align_bytes=64, bufs=4)
+        def gate_and_store(c, n, res):
             nc.vector.tensor_tensor(res[:], gates[n][:].indirect(chunk_offsets(c)), y_tiles[c, n][:], MULT)
             nc.sync.dma_start(out[n * P : (n + 1) * P, c * CHUNK : (c + 1) * CHUNK], res[:])
 
-        units = R_PASSES * SUBS
+        pending = []
         for c in range(CHUNKS):
-            after = (0, 2, 4, 6) if c < CHUNKS - 1 else (1, 4, 6, 7)
-            waiting = []
-            for u in range(units):
-                a, s = divmod(u, SUBS)
-                if u in after:
-                    act = hand[after.index(u)]
-                else:
-                    act = ring.tile([P, CHUNK], F32, name="act", align_bytes=64)
-                hidden(c, a, s, act)
-                last = c == CHUNKS - 1 and u == units - 1
-                if last:
-                    quantise(c, a)
-                for n in waiting:
-                    gate_and_store(c - 1, n)
-                waiting = []
-                if s == SUBS - 1 and not last:
-                    quantise(c, a)
-                if c > 0 and u in after:
-                    down(c - 1, after.index(u), act)
-                    waiting.append(after.index(u))
-            for n in waiting:
-                gate_and_store(c - 1, n)
-        for n in range(N_TILES):
-            y = ring.tile([P, CHUNK], F32, name="y", align_bytes=64, bufs=4)
-            down(CHUNKS - 1, n, y)
-            gate_and_store(CHUNKS - 1, n)
+            for a in range(R_PASSES):
+                group = c * R_PASSES + a
+                before, behind = hand[2 * (group % 3)], hand[2 * (group % 3) + 1]
+                shared = {SUBS - 2: before, GPSIMD_SUB: behind}
+                if group == 0:
+                    shared = {0: held.tile([P, CHUNK], F32, name="act_first", tag="x_words2", align_bytes=64)}
+                if group == 3:
+                    shared[SUBS - 2] = held.tile([P, CHUNK], F32, name="act_first", tag="x_words3", align_bytes=64)
+                for s in range(SUBS):
+                    if s in shared:
+                        act = shared[s]
+                    else:
+                        act = ring.tile([P, CHUNK], F32, name="act", align_bytes=64)
+                    hidden(c, a, s, act)
+                    if group == 0 and s == 0:
+                        gather_words(2, "x_words2")
+                if c > 0 and a == 0:
+                    pending.extend([(c - 1, n) for n in range(N_TILES)])
+                if group == 3:
+                    gather_words(3, "x_words3")
+                elif pending:
+                    down(*pending[0])
+                    gate_and_store(*pending.pop(0), before)
+                quantise(c, a)
+                if pending:
+                    down(*pending[0])
+                    gate_and_store(*pending.pop(0), behind)
+        pending.extend([(CHUNKS - 1, n) for n in range(N_TILES)])
+        for c, n in pending:
+            down(c, n)
+            res = ring.tile([P, CHUNK], F32, name="res", align_bytes=64, bufs=5)
+            gate_and_store(c, n, res)

@@ -41,8 +41,10 @@ def tile_list_gmlpt_gelu_gate_kernel(
         offsets = held.tile([P, J // 16], U16, name="offsets")
         nc.sync.dma_start(offsets[:], offs)
 
-        tab_plane = held.tile([P, T], U8, name="tab_plane", align_bytes=64)
-        nc.vector.memset(tab_plane[:].bitcast(I32), 0)
+        tab_rows = held.tile([P, T], U8, name="tab_rows", align_bytes=64)
+        nc.vector.memset(tab_rows[:].bitcast(I32), 0)
+        x_plane = held.tile([P, J], U8, name="x_plane", align_bytes=64)
+        nc.vector.memset(x_plane[:].bitcast(I32), 0)
         w_plane_raw = held.tile([P, R], U8, name="w_plane_raw", align_bytes=64)
         nc.gpsimd.memset(w_plane_raw[:].bitcast(I32), 0)
         wd_plane = held.tile([P, R_PASSES * N], U8, name="wd_plane", align_bytes=64)
@@ -53,10 +55,7 @@ def tile_list_gmlpt_gelu_gate_kernel(
         warm_out = held.tile([P, 1], F32, name="warm_out")
         nc.scalar.activation(warm_out[:], warm[:], GELU)
 
-        for q in range(4):
-            nc.sync.dma_start(
-                tab_plane[32 * q : 32 * q + 4, :].bitcast(I32), tab_scales[0, 4 * q : 4 * q + 4, :].bitcast(I32)
-            )
+        nc.sync.dma_start(tab_rows[0:P:8, :].bitcast(I32), tab_scales[0].bitcast(I32))
 
         def load_w_rows(q, first, scales):
             nc.sync.dma_start(
@@ -72,6 +71,8 @@ def tile_list_gmlpt_gelu_gate_kernel(
         for rows in w_rows[3:]:
             load_w_rows(*rows)
         raw = {}
+        x_rows = held.tile([P, J], U8, name="x_rows", align_bytes=64)
+        nc.vector.tensor_copy(x_rows[:], tab_rows[:].indirect(offsets[:]))
         for a in range(R_PASSES):
             for name, words in (("wg", wg_words), ("wu", wu_words)):
                 raw[name, a] = held.tile([P, PASS_ROWS], I32, name="%s_raw%d" % (name, a), align_bytes=64)
@@ -79,6 +80,10 @@ def tile_list_gmlpt_gelu_gate_kernel(
                     raw[name, a][:],
                     words[0, :, a * PASS_ROWS : (a + 1) * PASS_ROWS, :].rearrange("p n t -> p (n t)").bitcast(I32),
                 )
+        for q in range(4):
+            nc.sync.dma_start(
+                x_plane[32 * q : 32 * q + 4, :].bitcast(I32), x_rows[32 * q : 32 * q + 32 : 8, :].bitcast(I32)
+            )
         wd = held.tile([P, R_PASSES, 2 * N], U8, name="wd", align_bytes=64)
         nc.sync.dma_start(wd[:].bitcast(I32), wd_words.rearrange("a p n -> p a n").bitcast(I32))
         for q in range(4):
@@ -96,8 +101,6 @@ def tile_list_gmlpt_gelu_gate_kernel(
             return offsets[:, c * (CHUNK // 16) : (c + 1) * (CHUNK // 16)]
 
         x_words = {}
-        x_plane = held.tile([P, J], U8, name="x_plane", align_bytes=64)
-        nc.vector.tensor_copy(x_plane[:], tab_plane[:].indirect(offsets[:]))
 
         def gather_words(c, tag):
             x_words[c] = held.tile([P, CHUNK], U32, name="x_words%d" % c, tag=tag, align_bytes=64)
@@ -119,13 +122,13 @@ def tile_list_gmlpt_gelu_gate_kernel(
                 )
         gather_words(1, "wu_raw1")
         hand = [held.tile([P, CHUNK], F32, name="hand%d" % i, align_bytes=64) for i in range(6)]
+        h_ring = [held.tile([P, CHUNK * PACK], BF16, name="h%d" % i, align_bytes=64) for i in range(3)]
 
 
         h_tiles, h_codes, h_planes, y_tiles = {}, {}, {}, {}
 
         def hidden(c, a, s, act):
-            if s == 0:
-                h_tiles[c, a] = ring.tile([P, CHUNK * PACK], BF16, name="h", align_bytes=64, bufs=1)
+            h_tiles[c, a] = h_ring[(c * R_PASSES + a) % 3]
             cols = slice(s * SUB, (s + 1) * SUB)
             banks = []
             for tag, name, first, bufs in (("ga", "wg", 0, 2), ("ub", "wu", WU_PLANE, 4)):
@@ -158,7 +161,7 @@ def tile_list_gmlpt_gelu_gate_kernel(
             h_planes[c, a] = ring.tile([P, CHUNK], U8, name="h_plane", align_bytes=64, bufs=6)
             nc.vector.quantize_mx(out=h_codes[c, a][:].bitcast(FP8X4), scales=h_planes[c, a][:], in_=h_tiles[c, a][:])
 
-        def down(c, n):
+        def down(c, n, y):
             bank = psum.tile([P, CHUNK], F32, name="y_bank", bufs=2)
             for a in range(R_PASSES):
                 nc.tensor.matmul_mx(
@@ -170,12 +173,15 @@ def tile_list_gmlpt_gelu_gate_kernel(
                     start=(a == 0),
                     stop=(a == R_PASSES - 1),
                 )
-            y_tiles[c, n] = ring.tile([P, CHUNK], F32, name="y", align_bytes=64, bufs=6)
-            nc.scalar.copy(y_tiles[c, n][:], bank[:])
+            y_tiles[c, n] = y
+            nc.scalar.copy(y, bank[:])
 
         def gate_and_store(c, n, res):
-            nc.vector.tensor_tensor(res[:], gates[n][:].indirect(chunk_offsets(c)), y_tiles[c, n][:], MULT)
+            nc.vector.tensor_tensor(res[:], gates[n][:].indirect(chunk_offsets(c)), y_tiles[c, n], MULT)
             nc.sync.dma_start(out[n * P : (n + 1) * P, c * CHUNK : (c + 1) * CHUNK], res[:])
+
+        def fresh_y():
+            return ring.tile([P, CHUNK], F32, name="y", align_bytes=64, bufs=4)[:]
 
         pending = []
         for c in range(CHUNKS):
@@ -197,17 +203,19 @@ def tile_list_gmlpt_gelu_gate_kernel(
                         gather_words(2, "x_words2")
                 if c > 0 and a == 0:
                     pending.extend([(c - 1, n) for n in range(N_TILES)])
+                first = GPSIMD_SUB * SUB * PACK
+                parked = h_ring[(group + 1) % 3][:, first : first + 2 * CHUNK].bitcast(F32)
                 if group == 3:
                     gather_words(3, "x_words3")
                 elif pending:
-                    down(*pending[0])
+                    down(*pending[0], parked)
                     gate_and_store(*pending.pop(0), before)
                 quantise(c, a)
                 if pending:
-                    down(*pending[0])
+                    down(*pending[0], parked if group == 3 else fresh_y())
                     gate_and_store(*pending.pop(0), behind)
         pending.extend([(CHUNKS - 1, n) for n in range(N_TILES)])
         for c, n in pending:
-            down(c, n)
+            down(c, n, fresh_y())
             res = ring.tile([P, CHUNK], F32, name="res", align_bytes=64, bufs=5)
             gate_and_store(c, n, res)

@@ -25,8 +25,13 @@ CHUNKS = J // CHUNK
 SUB = 128
 SUBS = CHUNK // SUB
 N_TILES = N // P
-WU_PLANE = 4
-GPSIMD_SUB = 1
+GROUPS = CHUNKS * R_PASSES
+CYCLE_STEPS = 7
+HALF = J // 2
+WD_FIRST = HALF + 2 * R
+STAGED_BYTES = WD_FIRST + R_PASSES * N
+PLANE_BYTES = STAGED_BYTES + HALF
+GATE_BYTES = 4 * T
 
 
 def tile_list_gmlpt_gelu_gate_kernel(
@@ -36,6 +41,7 @@ def tile_list_gmlpt_gelu_gate_kernel(
     with ExitStack() as ctx:
         held = ctx.enter_context(tc.tile_pool(name="held", bufs=1))
         ring = ctx.enter_context(tc.tile_pool(name="ring", bufs=3))
+        shared = ctx.enter_context(tc.tile_pool(name="shared", bufs=1))
         psum = ctx.enter_context(tc.psum_pool(name="psum", bufs=1))
 
         offsets = held.tile([P, J // 16], U16, name="offsets")
@@ -43,179 +49,247 @@ def tile_list_gmlpt_gelu_gate_kernel(
 
         tab_rows = held.tile([P, T], U8, name="tab_rows", align_bytes=64)
         nc.vector.memset(tab_rows[:].bitcast(I32), 0)
-        x_plane = held.tile([P, J], U8, name="x_plane", align_bytes=64)
-        nc.vector.memset(x_plane[:].bitcast(I32), 0)
-        w_plane_raw = held.tile([P, R], U8, name="w_plane_raw", align_bytes=64)
-        nc.gpsimd.memset(w_plane_raw[:].bitcast(I32), 0)
-        wd_plane = held.tile([P, R_PASSES * N], U8, name="wd_plane", align_bytes=64)
-        nc.gpsimd.memset(wd_plane[:].bitcast(I32), 0)
+        w_rows = shared.tile([P, 2 * R], U8, name="w_rows", align_bytes=64, offset=GATE_BYTES - R)
+        nc.gpsimd.memset(w_rows[:].bitcast(I32), 0)
+        planes = held.tile([P, PLANE_BYTES], U8, name="planes", align_bytes=64)
+        nc.gpsimd.memset(planes[:].bitcast(I32), 0)
+        staged = shared.tile([P, STAGED_BYTES], U8, name="staged", align_bytes=64, offset=3 * GATE_BYTES - 2 * R)
 
         warm = held.tile([P, 1], F32, name="warm")
-        nc.gpsimd.memset(warm[:], 0.0)
+        nc.vector.memset(warm[:], 0.0)
         warm_out = held.tile([P, 1], F32, name="warm_out")
         nc.scalar.activation(warm_out[:], warm[:], GELU)
 
-        nc.sync.dma_start(tab_rows[0:P:8, :].bitcast(I32), tab_scales[0].bitcast(I32))
-
-        def load_w_rows(q, first, scales):
-            nc.sync.dma_start(
-                w_plane_raw[32 * q + first : 32 * q + first + 4, :].bitcast(I32),
-                scales[0, 4 * q : 4 * q + 4, :].bitcast(I32),
-            )
-
-        w_rows = [(q, first, scales) for first, scales in ((0, wg_scales), (WU_PLANE, wu_scales)) for q in range(4)]
-        for rows in w_rows[:3]:
-            load_w_rows(*rows)
-        tab = held.tile([P, T], U32, name="tab", align_bytes=64)
-        nc.sync.dma_start(tab[:].bitcast(I32), tab_words[0].rearrange("p n t -> p (n t)").bitcast(I32))
-        for rows in w_rows[3:]:
-            load_w_rows(*rows)
         raw = {}
-        x_rows = held.tile([P, J], U8, name="x_rows", align_bytes=64)
-        nc.vector.tensor_copy(x_rows[:], tab_rows[:].indirect(offsets[:]))
-        for a in range(R_PASSES):
-            for name, words in (("wg", wg_words), ("wu", wu_words)):
-                raw[name, a] = held.tile([P, PASS_ROWS], I32, name="%s_raw%d" % (name, a), align_bytes=64)
+
+        def load_w_words(a):
+            for i, (name, words) in enumerate((("wg", wg_words), ("wu", wu_words))):
+                if a == 0:
+                    raw[name, a] = held.tile([P, PASS_ROWS], I32, name="%s_raw0" % name, align_bytes=64)
+                else:
+                    first = GATE_BYTES + HALF // 2 if i else GATE_BYTES - HALF // 2 - 4 * PASS_ROWS
+                    raw[name, a] = shared.tile([P, PASS_ROWS], I32, name="%s_raw1" % name, align_bytes=64, offset=first)
                 nc.sync.dma_start(
                     raw[name, a][:],
                     words[0, :, a * PASS_ROWS : (a + 1) * PASS_ROWS, :].rearrange("p n t -> p (n t)").bitcast(I32),
                 )
-        for q in range(4):
-            nc.sync.dma_start(
-                x_plane[32 * q : 32 * q + 4, :].bitcast(I32), x_rows[32 * q : 32 * q + 32 : 8, :].bitcast(I32)
-            )
-        wd = held.tile([P, R_PASSES, 2 * N], U8, name="wd", align_bytes=64)
-        nc.sync.dma_start(wd[:].bitcast(I32), wd_words.rearrange("a p n -> p a n").bitcast(I32))
-        for q in range(4):
-            nc.sync.dma_start(
-                wd_plane[32 * q : 32 * q + 4, :].bitcast(I32).rearrange("p (a n) -> p a n", a=R_PASSES),
-                wd_scales[:, 4 * q : 4 * q + 4, :].rearrange("a r n -> r a n").bitcast(I32),
-            )
-        gates = []
-        for n in range(N_TILES):
-            gate = held.tile([P, T], F32, name="gate%d" % n, align_bytes=64)
-            nc.sync.dma_start(gate[:], gT[n * P : (n + 1) * P, :])
-            gates.append(gate)
 
-        def chunk_offsets(c):
-            return offsets[:, c * (CHUNK // 16) : (c + 1) * (CHUNK // 16)]
-
-        x_words = {}
-
-        def gather_words(c, tag):
-            x_words[c] = held.tile([P, CHUNK], U32, name="x_words%d" % c, tag=tag, align_bytes=64)
-            nc.vector.tensor_copy(x_words[c][:], tab[:].indirect(chunk_offsets(c)))
-
-        gather_words(0, "x_words0")
-        w_plane = held.tile([P, R], U8, name="w_plane", align_bytes=64)
-        nc.vector.tensor_copy(
-            w_plane[:].rearrange("p (a t m) -> p a t m", a=R_PASSES, t=PACK),
-            w_plane_raw[:].rearrange("p (a m t) -> p a t m", a=R_PASSES, t=PACK),
+        nc.sync.dma_start(tab_rows[0:P:8, :].bitcast(I32), tab_scales[0].bitcast(I32))
+        for i, scales in enumerate((wg_scales, wu_scales)):
+            nc.sync.dma_start(w_rows[0:P:8, i * R : (i + 1) * R].bitcast(I32), scales[0].bitcast(I32))
+        nc.sync.dma_start(
+            staged[0:P:8, WD_FIRST:].bitcast(I32).rearrange("p (a n) -> p a n", a=R_PASSES),
+            wd_scales.rearrange("a r n -> r a n").bitcast(I32),
         )
-        dealt = {}
-        for a in range(R_PASSES):
+        load_w_words(0)
+        tab = held.tile([P, T], U32, name="tab", align_bytes=64)
+        nc.sync.dma_start(tab[:].bitcast(I32), tab_words[0].rearrange("p n t -> p (n t)").bitcast(I32))
+
+        def chunk_offsets(c, count=1):
+            return offsets[:, c * (CHUNK // 16) : (c + count) * (CHUNK // 16)]
+
+        def move_rows(plane, rows):
+            for q in range(4):
+                nc.sync.dma_start(
+                    plane[32 * q : 32 * q + 4, :].bitcast(I32), rows[32 * q : 32 * q + 32 : 8, :].bitcast(I32)
+                )
+
+        x_rows = held.tile([P, HALF], U8, name="x_rows", align_bytes=64)
+        nc.vector.tensor_copy(x_rows[:], tab_rows[:].indirect(chunk_offsets(0, 2)))
+        nc.vector.tensor_copy(staged[:, :HALF].bitcast(I32), x_rows[:].bitcast(I32))
+        nc.gpsimd.tensor_copy(
+            staged[:, HALF:WD_FIRST].rearrange("p (a t m) -> p a t m", a=2 * R_PASSES, t=PACK),
+            w_rows[:].rearrange("p (a m t) -> p a t m", a=2 * R_PASSES, t=PACK),
+        )
+        move_rows(planes[:, :STAGED_BYTES], staged[:])
+        load_w_words(1)
+        x_firsts = [0, CHUNK, STAGED_BYTES, STAGED_BYTES + CHUNK]
+        x_planes = [planes[:, first : first + CHUNK] for first in x_firsts]
+        w_plane, wd_plane = planes[:, HALF:WD_FIRST], planes[:, WD_FIRST:STAGED_BYTES]
+
+        x_words, dealt = {}, {}
+
+        def deal_words(a):
             for name in ("wg", "wu"):
                 dealt[name, a] = held.tile([P, PASS_ROWS], I32, name="%s%d" % (name, a), align_bytes=64)
                 nc.vector.tensor_copy(
                     dealt[name, a][:].rearrange("p (t c i) -> p c t i", t=PACK, i=4),
                     raw[name, a][:].rearrange("p (c i t) -> p c t i", t=PACK, i=4),
                 )
-        gather_words(1, "wu_raw1")
-        hand = [held.tile([P, CHUNK], F32, name="hand%d" % i, align_bytes=64) for i in range(6)]
-        h_ring = [held.tile([P, CHUNK * PACK], BF16, name="h%d" % i, align_bytes=64) for i in range(3)]
 
+        def gather_words(c):
+            x_words[c] = held.tile([P, CHUNK], U32, name="x_words%d" % c, align_bytes=64)
+            nc.vector.tensor_copy(x_words[c][:], tab[:].indirect(chunk_offsets(c)))
 
-        h_tiles, h_codes, h_planes, y_tiles = {}, {}, {}, {}
+        deal_words(0)
+        late_rows = shared.tile([P, HALF], U8, name="late_rows", align_bytes=64, offset=GATE_BYTES - HALF // 2)
+        nc.vector.tensor_copy(late_rows[:], tab_rows[:].indirect(chunk_offsets(2, 2)))
+        move_rows(planes[:, STAGED_BYTES:], late_rows[:])
+        wd = shared.tile([P, R_PASSES, 2 * N], U8, name="wd", align_bytes=64, offset=3 * GATE_BYTES)
+        nc.sync.dma_start(wd[:].bitcast(I32), wd_words.rearrange("a p n -> p a n").bitcast(I32))
+        gather_words(0)
+        deal_words(1)
+        for c in range(1, CHUNKS):
+            gather_words(c)
+        gates = []
 
-        def hidden(c, a, s, act):
-            h_tiles[c, a] = h_ring[(c * R_PASSES + a) % 3]
-            cols = slice(s * SUB, (s + 1) * SUB)
-            banks = []
-            for tag, name, first, bufs in (("ga", "wg", 0, 2), ("ub", "wu", WU_PLANE, 4)):
-                bank = psum.tile([P, PACK, SUB], F32, name=tag, bufs=bufs)
-                for t in range(PACK):
-                    w_cols = slice(a * PASS_ROWS + t * P, a * PASS_ROWS + (t + 1) * P)
-                    nc.tensor.matmul_mx(
-                        out=bank[:, t, :],
-                        lhsT=dealt[name, a][:, t * P : (t + 1) * P].bitcast(FP8X4),
-                        lhsT_scale=w_plane[first:P, w_cols],
-                        rhs=x_words[c][:, cols].bitcast(FP8X4),
-                        rhs_scale=x_plane[:, c * CHUNK + s * SUB : c * CHUNK + (s + 1) * SUB],
-                        start=True,
-                        stop=True,
-                    )
-                banks.append(bank)
-            ga, ub = banks
-            act = act[:].rearrange("p (j t) -> p j t", t=PACK)
-            nc.scalar.activation(act, ga[:].rearrange("p t j -> p j t"), GELU)
-            h = h_tiles[c, a][:, s * SUB * PACK : (s + 1) * SUB * PACK].rearrange("p (j t) -> p j t", t=PACK)
-            if c > 0 and s == GPSIMD_SUB:
-                ub_copy = ring.tile([P, SUB, PACK], F32, name="ub_copy", align_bytes=64, bufs=2)
-                nc.scalar.copy(ub_copy[:], ub[:].rearrange("p t j -> p j t"))
-                nc.gpsimd.tensor_tensor(h, ub_copy[:], act, MULT)
+        def load_gate(n):
+            if n < 3:
+                first = (2, 0, 1)[n] * GATE_BYTES
+                gate = shared.tile([P, T], F32, name="gate%d" % n, align_bytes=64, offset=first)
             else:
-                nc.vector.tensor_tensor(h, ub[:].rearrange("p t j -> p j t"), act, MULT)
+                gate = held.tile([P, T], F32, name="gate%d" % n, tag="x_words0", align_bytes=64)
+            nc.sync.dma_start(gate[:], gT[n * P : (n + 1) * P, :])
+            gates.append(gate)
 
-        def quantise(c, a):
-            h_codes[c, a] = ring.tile([P, CHUNK], U32, name="h_codes", align_bytes=64, bufs=6)
-            h_planes[c, a] = ring.tile([P, CHUNK], U8, name="h_plane", align_bytes=64, bufs=6)
-            nc.vector.quantize_mx(out=h_codes[c, a][:].bitcast(FP8X4), scales=h_planes[c, a][:], in_=h_tiles[c, a][:])
+        for n in range(N_TILES - 1):
+            load_gate(n)
 
-        def down(c, n, y):
-            bank = psum.tile([P, CHUNK], F32, name="y_bank", bufs=2)
-            for a in range(R_PASSES):
-                nc.tensor.matmul_mx(
-                    out=bank[:],
-                    lhsT=wd[:, a, 2 * n * P : 2 * (n + 1) * P].bitcast(FP4X4),
-                    lhsT_scale=wd_plane[:, a * N + n * P : a * N + (n + 1) * P],
-                    rhs=h_codes[c, a][:].bitcast(FP8X4),
-                    rhs_scale=h_planes[c, a][:],
-                    start=(a == 0),
-                    stop=(a == R_PASSES - 1),
-                )
-            y_tiles[c, n] = y
-            nc.scalar.copy(y, bank[:])
+        h = held.tile([P, (SUBS + 1) * CHUNK], BF16, name="h", align_bytes=64)
+        h_codes, h_planes, pair_act, pair_ub, acts, ub_banks, ub_copies, picked = {}, {}, {}, {}, {}, {}, {}, {}
 
-        def gate_and_store(c, n, res):
-            nc.vector.tensor_tensor(res[:], gates[n][:].indirect(chunk_offsets(c)), y_tiles[c, n], MULT)
-            nc.sync.dma_start(out[n * P : (n + 1) * P, c * CHUNK : (c + 1) * CHUNK], res[:])
+        def gpsimd_pieces(group):
+            return [[(0,), (1,)], [(0,), (1,), (2,)]][group] if group < 2 else [(0,), (1, 2)]
 
-        def fresh_y():
-            return ring.tile([P, CHUNK], F32, name="y", align_bytes=64, bufs=4)[:]
+        def interleaved(ap):
+            return ap.rearrange("p (j t) -> p j t", t=PACK)
 
-        pending = []
-        for c in range(CHUNKS):
-            for a in range(R_PASSES):
-                group = c * R_PASSES + a
-                before, behind = hand[2 * (group % 3)], hand[2 * (group % 3) + 1]
-                shared = {SUBS - 2: before, GPSIMD_SUB: behind}
-                if group == 0:
-                    shared = {0: held.tile([P, CHUNK], F32, name="act_first", tag="x_words2", align_bytes=64)}
-                if group == 3:
-                    shared[SUBS - 2] = held.tile([P, CHUNK], F32, name="act_first", tag="x_words3", align_bytes=64)
-                for s in range(SUBS):
-                    if s in shared:
-                        act = shared[s]
-                    else:
-                        act = ring.tile([P, CHUNK], F32, name="act", align_bytes=64)
-                    hidden(c, a, s, act)
-                    if group == 0 and s == 0:
-                        gather_words(2, "x_words2")
-                if c > 0 and a == 0:
-                    pending.extend([(c - 1, n) for n in range(N_TILES)])
-                first = GPSIMD_SUB * SUB * PACK
-                parked = h_ring[(group + 1) % 3][:, first : first + 2 * CHUNK].bitcast(F32)
-                if group == 3:
-                    gather_words(3, "x_words3")
-                elif pending:
-                    down(*pending[0], parked)
-                    gate_and_store(*pending.pop(0), before)
-                quantise(c, a)
-                if pending:
-                    down(*pending[0], parked if group == 3 else fresh_y())
-                    gate_and_store(*pending.pop(0), behind)
-        pending.extend([(CHUNKS - 1, n) for n in range(N_TILES)])
-        for c, n in pending:
-            down(c, n, fresh_y())
-            res = ring.tile([P, CHUNK], F32, name="res", align_bytes=64, bufs=5)
-            gate_and_store(c, n, res)
+        def first_stage(group):
+            c, a = divmod(group, R_PASSES)
+            on_gpsimd = [s for piece in gpsimd_pieces(group) for s in piece]
+            pair_act[group] = held.tile([P, 2 * CHUNK], F32, name="pair_act%d" % group, align_bytes=64)
+            pair_ub[group] = held.tile([P, 2 * CHUNK], F32, name="pair_ub%d" % group, align_bytes=64)
+            for s in range(SUBS):
+                first_token = (s - group % 2) % SUBS * SUB
+                cols = slice(first_token, first_token + SUB)
+                banks = []
+                ub_tag, ub_bufs = ("ub_last", 1) if s == SUBS - 1 else ("ub", 2)
+                for tag, name, first, bufs in (("ga", "wg", 0, 2), (ub_tag, "wu", R, ub_bufs)):
+                    bank = psum.tile([P, PACK, SUB], F32, name=tag, bufs=bufs)
+                    for t in range(PACK):
+                        w_cols = slice(first + a * PASS_ROWS + t * P, first + a * PASS_ROWS + (t + 1) * P)
+                        nc.tensor.matmul_mx(
+                            out=bank[:, t, :],
+                            lhsT=dealt[name, a][:, t * P : (t + 1) * P].bitcast(FP8X4),
+                            lhsT_scale=w_plane[:, w_cols],
+                            rhs=x_words[c][:, cols].bitcast(FP8X4),
+                            rhs_scale=x_planes[c][:, cols],
+                            start=True,
+                            stop=True,
+                        )
+                    banks.append(bank)
+                ga, ub_banks[group, s] = banks
+                if s in (1, 2):
+                    acts[group, s] = pair_act[group][:, (s - 1) * CHUNK : s * CHUNK]
+                    ub_copies[group, s] = pair_ub[group][:, (s - 1) * CHUNK : s * CHUNK]
+                else:
+                    acts[group, s] = ring.tile([P, CHUNK], F32, name="act%d" % s, align_bytes=64, bufs=2)[:]
+                    if s in on_gpsimd:
+                        ub_copies[group, s] = ring.tile([P, CHUNK], F32, name="ub_copy", align_bytes=64, bufs=2)[:]
+                nc.scalar.activation(interleaved(acts[group, s]), ga[:].rearrange("p t j -> p j t"), GELU)
+                if s in on_gpsimd:
+                    nc.scalar.copy(interleaved(ub_copies[group, s]), ub_banks[group, s][:].rearrange("p t j -> p j t"))
+
+        def h_cols(group, s, count=1):
+            place = SUBS if s == 0 and group % 2 else s
+            return h[:, place * CHUNK : (place + count) * CHUNK]
+
+        def product_on_gpsimd(group, piece):
+            if len(piece) == 2:
+                nc.gpsimd.tensor_tensor(h_cols(group, piece[0], 2), pair_ub[group][:], pair_act[group][:], MULT)
+            else:
+                nc.gpsimd.tensor_tensor(h_cols(group, piece[0]), ub_copies[group, piece[0]], acts[group, piece[0]], MULT)
+
+        def product_on_vector(group, s):
+            nc.vector.tensor_tensor(
+                interleaved(h_cols(group, s)),
+                ub_banks[group, s][:].rearrange("p t j -> p j t"),
+                interleaved(acts[group, s]),
+                MULT,
+            )
+
+        def quantise(group):
+            h_codes[group] = held.tile([P, CHUNK], U32, name="h_codes%d" % group, align_bytes=64)
+            h_planes[group] = held.tile([P, CHUNK], U8, name="h_plane%d" % group, align_bytes=64)
+            nc.vector.quantize_mx(out=h_codes[group][:].bitcast(FP8X4), scales=h_planes[group][:], in_=h[:, group % 2 * CHUNK : (group % 2 + SUBS) * CHUNK])
+
+        def gather_gate(c, n, into):
+            picked[c, n] = into
+            nc.vector.tensor_copy(into, gates[n][:].indirect(chunk_offsets(c)))
+
+        def down_pass(c, n, a, bank):
+            nc.tensor.matmul_mx(
+                out=bank[:],
+                lhsT=wd[:, a, 2 * n * P : 2 * (n + 1) * P].bitcast(FP4X4),
+                lhsT_scale=wd_plane[:, a * N + n * P : a * N + (n + 1) * P],
+                rhs=h_codes[c * R_PASSES + a][:].bitcast(FP8X4),
+                rhs_scale=h_planes[c * R_PASSES + a][:],
+                start=(a == 0),
+                stop=(a == R_PASSES - 1),
+            )
+
+        def gate_and_store(c, n, bank=None):
+            if bank is None:
+                bank = psum.tile([P, CHUNK], F32, name="y_bank", bufs=3)
+                down_pass(c, n, 0, bank)
+            down_pass(c, n, 1, bank)
+            nc.vector.tensor_tensor(picked[c, n], bank[:], picked[c, n], MULT)
+            nc.sync.dma_start(out[n * P : (n + 1) * P, c * CHUNK : (c + 1) * CHUNK], picked[c, n])
+
+        units = [(c, n) for c in range(CHUNKS) for n in range(N_TILES)]
+        to_gather, to_gate = list(units), list(units)
+
+        def freed_slices(group):
+            return [pair[group][:, half * CHUNK : (half + 1) * CHUNK] for half in (1, 0) for pair in (pair_ub, pair_act)]
+
+        last_banks = {}
+        first_stage(0)
+        for piece in gpsimd_pieces(0):
+            product_on_gpsimd(0, piece)
+        product_on_vector(0, 2)
+        product_on_vector(0, 3)
+        first_stage(1)
+        load_gate(N_TILES - 1)
+        for group in range(1, GROUPS):
+            free = freed_slices(group - 1)
+            left = CYCLE_STEPS - 1
+            gathers, gated = [], []
+            for c, n in list(to_gate):
+                cost = 3 if (c, n) in to_gather else 1
+                if R_PASSES * (c + 1) <= group and n < group and cost <= left:
+                    if (c, n) in to_gather:
+                        to_gather.remove((c, n))
+                        gathers.append((c, n))
+                    to_gate.remove((c, n))
+                    gated.append((c, n))
+                    left = left - cost
+            for c, n in list(to_gather):
+                if n < group and left >= 1 and len(to_gather) > 1:
+                    to_gather.remove((c, n))
+                    gathers.append((c, n))
+                    left = left - 2
+            first_piece, *later_pieces = gpsimd_pieces(group)
+            product_on_gpsimd(group, first_piece)
+            gather_gate(*gathers[0], free.pop(0))
+            quantise(group - 1)
+            for piece in later_pieces:
+                product_on_gpsimd(group, piece)
+            for unit in gathers[1:2]:
+                gather_gate(*unit, free.pop(0))
+            product_on_vector(group, SUBS - 1)
+            for unit in gated:
+                gate_and_store(*unit)
+            for unit in gathers[2:]:
+                gather_gate(*unit, free.pop(0))
+            if group + 1 < GROUPS:
+                first_stage(group + 1)
+            else:
+                for n, tag in enumerate(("ga", "ub", "ga", "ub")):
+                    last_banks[CHUNKS - 1, n] = psum.tile([P, CHUNK], F32, name="last_bank", tag=tag, bufs=2)
+                    down_pass(CHUNKS - 1, n, 0, last_banks[CHUNKS - 1, n])
+        quantise(GROUPS - 1)
+        free = freed_slices(GROUPS - 1)
+        for unit in to_gather:
+            gather_gate(*unit, free.pop(0))
+        for unit in to_gate:
+            gate_and_store(*unit, last_banks.get(unit))

@@ -26,11 +26,10 @@ SUB = 128
 SUBS = CHUNK // SUB
 N_TILES = N // P
 GROUPS = CHUNKS * R_PASSES
-CYCLE_STEPS = 7
-HALF = J // 2
-WD_FIRST = HALF + 2 * R
+EARLY = J - CHUNK
+WD_FIRST = EARLY + 2 * R
 STAGED_BYTES = WD_FIRST + R_PASSES * N
-PLANE_BYTES = STAGED_BYTES + HALF
+PLANE_BYTES = STAGED_BYTES + CHUNK
 GATE_BYTES = 4 * T
 
 
@@ -53,7 +52,7 @@ def tile_list_gmlpt_gelu_gate_kernel(
         nc.gpsimd.memset(w_rows[:].bitcast(I32), 0)
         planes = held.tile([P, PLANE_BYTES], U8, name="planes", align_bytes=64)
         nc.gpsimd.memset(planes[:].bitcast(I32), 0)
-        staged = shared.tile([P, STAGED_BYTES], U8, name="staged", align_bytes=64, offset=3 * GATE_BYTES - 2 * R)
+        staged = held.tile([P, STAGED_BYTES], U8, name="staged", tag="gate1", align_bytes=64)
 
         warm = held.tile([P, 1], F32, name="warm")
         nc.vector.memset(warm[:], 0.0)
@@ -64,11 +63,8 @@ def tile_list_gmlpt_gelu_gate_kernel(
 
         def load_w_words(a):
             for i, (name, words) in enumerate((("wg", wg_words), ("wu", wu_words))):
-                if a == 0:
-                    raw[name, a] = held.tile([P, PASS_ROWS], I32, name="%s_raw0" % name, align_bytes=64)
-                else:
-                    first = GATE_BYTES + HALF // 2 if i else GATE_BYTES - HALF // 2 - 4 * PASS_ROWS
-                    raw[name, a] = shared.tile([P, PASS_ROWS], I32, name="%s_raw1" % name, align_bytes=64, offset=first)
+                tag = "gate%d" % (2 + i) if a else name
+                raw[name, a] = held.tile([P, PASS_ROWS], I32, name="%s_raw%d" % (name, a), tag=tag, align_bytes=64)
                 nc.sync.dma_start(
                     raw[name, a][:],
                     words[0, :, a * PASS_ROWS : (a + 1) * PASS_ROWS, :].rearrange("p n t -> p (n t)").bitcast(I32),
@@ -81,9 +77,10 @@ def tile_list_gmlpt_gelu_gate_kernel(
             staged[0:P:8, WD_FIRST:].bitcast(I32).rearrange("p (a n) -> p a n", a=R_PASSES),
             wd_scales.rearrange("a r n -> r a n").bitcast(I32),
         )
-        load_w_words(0)
         tab = held.tile([P, T], U32, name="tab", align_bytes=64)
         nc.sync.dma_start(tab[:].bitcast(I32), tab_words[0].rearrange("p n t -> p (n t)").bitcast(I32))
+        load_w_words(0)
+        load_w_words(1)
 
         def chunk_offsets(c, count=1):
             return offsets[:, c * (CHUNK // 16) : (c + count) * (CHUNK // 16)]
@@ -94,78 +91,75 @@ def tile_list_gmlpt_gelu_gate_kernel(
                     plane[32 * q : 32 * q + 4, :].bitcast(I32), rows[32 * q : 32 * q + 32 : 8, :].bitcast(I32)
                 )
 
-        x_rows = held.tile([P, HALF], U8, name="x_rows", align_bytes=64)
-        nc.vector.tensor_copy(x_rows[:], tab_rows[:].indirect(chunk_offsets(0, 2)))
-        nc.vector.tensor_copy(staged[:, :HALF].bitcast(I32), x_rows[:].bitcast(I32))
+        x_rows = held.tile([P, EARLY], U8, name="x_rows", align_bytes=64)
+        nc.vector.tensor_copy(x_rows[:], tab_rows[:].indirect(chunk_offsets(0, CHUNKS - 1)))
+        nc.vector.tensor_copy(staged[:, :EARLY].bitcast(I32), x_rows[:].bitcast(I32))
         nc.gpsimd.tensor_copy(
-            staged[:, HALF:WD_FIRST].rearrange("p (a t m) -> p a t m", a=2 * R_PASSES, t=PACK),
+            staged[:, EARLY:WD_FIRST].rearrange("p (a t m) -> p a t m", a=2 * R_PASSES, t=PACK),
             w_rows[:].rearrange("p (a m t) -> p a t m", a=2 * R_PASSES, t=PACK),
         )
         move_rows(planes[:, :STAGED_BYTES], staged[:])
-        load_w_words(1)
-        x_firsts = [0, CHUNK, STAGED_BYTES, STAGED_BYTES + CHUNK]
+        x_firsts = [0, CHUNK, 2 * CHUNK, STAGED_BYTES]
         x_planes = [planes[:, first : first + CHUNK] for first in x_firsts]
-        w_plane, wd_plane = planes[:, HALF:WD_FIRST], planes[:, WD_FIRST:STAGED_BYTES]
+        w_plane, wd_plane = planes[:, EARLY:WD_FIRST], planes[:, WD_FIRST:STAGED_BYTES]
 
         x_words, dealt = {}, {}
 
         def deal_words(a):
             for name in ("wg", "wu"):
                 dealt[name, a] = held.tile([P, PASS_ROWS], I32, name="%s%d" % (name, a), align_bytes=64)
-                nc.vector.tensor_copy(
+                nc.gpsimd.tensor_copy(
                     dealt[name, a][:].rearrange("p (t c i) -> p c t i", t=PACK, i=4),
                     raw[name, a][:].rearrange("p (c i t) -> p c t i", t=PACK, i=4),
                 )
 
-        def gather_words(c):
-            x_words[c] = held.tile([P, CHUNK], U32, name="x_words%d" % c, align_bytes=64)
+        def gather_words(c, tag):
+            x_words[c] = held.tile([P, CHUNK], U32, name="x_words%d" % c, tag=tag, align_bytes=64)
             nc.vector.tensor_copy(x_words[c][:], tab[:].indirect(chunk_offsets(c)))
 
         deal_words(0)
-        late_rows = shared.tile([P, HALF], U8, name="late_rows", align_bytes=64, offset=GATE_BYTES - HALF // 2)
-        nc.vector.tensor_copy(late_rows[:], tab_rows[:].indirect(chunk_offsets(2, 2)))
-        move_rows(planes[:, STAGED_BYTES:], late_rows[:])
-        wd = shared.tile([P, R_PASSES, 2 * N], U8, name="wd", align_bytes=64, offset=3 * GATE_BYTES)
-        nc.sync.dma_start(wd[:].bitcast(I32), wd_words.rearrange("a p n -> p a n").bitcast(I32))
-        gather_words(0)
         deal_words(1)
-        for c in range(1, CHUNKS):
-            gather_words(c)
+        wd = shared.tile([P, R_PASSES, 2 * N], U8, name="wd", align_bytes=64, offset=GATE_BYTES)
+        nc.sync.dma_start(wd[:].bitcast(I32), wd_words.rearrange("a p n -> p a n").bitcast(I32))
+        gather_words(0, "x_words0")
+        late_rows = held.tile([P, CHUNK], U8, name="late_rows", tag="wg", align_bytes=64)
+        nc.vector.tensor_copy(late_rows[:], tab_rows[:].indirect(chunk_offsets(CHUNKS - 1)))
+        gather_words(1, "x_words1")
         gates = []
-
-        def load_gate(n):
-            if n < 3:
-                first = (2, 0, 1)[n] * GATE_BYTES
-                gate = shared.tile([P, T], F32, name="gate%d" % n, align_bytes=64, offset=first)
+        for n in range(N_TILES):
+            if n == 0:
+                gate = shared.tile([P, T], F32, name="gate0", align_bytes=64, offset=0)
             else:
-                gate = held.tile([P, T], F32, name="gate%d" % n, tag="x_words0", align_bytes=64)
+                gate = held.tile([P, T], F32, name="gate%d" % n, align_bytes=64)
             nc.sync.dma_start(gate[:], gT[n * P : (n + 1) * P, :])
             gates.append(gate)
+            if n == 1:
+                move_rows(planes[:, STAGED_BYTES:], late_rows[:])
 
-        for n in range(N_TILES - 1):
-            load_gate(n)
+        h_tiles = [held.tile([P, SUBS * CHUNK], BF16, name="h%d" % i, align_bytes=64) for i in range(3)]
 
-        h = held.tile([P, (SUBS + 1) * CHUNK], BF16, name="h", align_bytes=64)
-        h_codes, h_planes, pair_act, pair_ub, acts, ub_banks, ub_copies, picked = {}, {}, {}, {}, {}, {}, {}, {}
+        def h_of(group):
+            return h_tiles[group % 3]
 
-        def gpsimd_pieces(group):
-            return [[(0,), (1,)], [(0,), (1,), (2,)]][group] if group < 2 else [(0,), (1, 2)]
+        h_codes, h_planes, pair_act, pair_ub, acts, ub_banks, picked, last_banks, ga_banks = {}, {}, {}, {}, {}, {}, {}, {}, {}
+
+        def gpsimd_subs(group):
+            return (0, 0, 1, 2, 2, 2, 2, 1)[group]
 
         def interleaved(ap):
             return ap.rearrange("p (j t) -> p j t", t=PACK)
 
         def first_stage(group):
             c, a = divmod(group, R_PASSES)
-            on_gpsimd = [s for piece in gpsimd_pieces(group) for s in piece]
-            pair_act[group] = held.tile([P, 2 * CHUNK], F32, name="pair_act%d" % group, align_bytes=64)
+            tag = "x_words3" if group == 1 else "pair_act%d" % group
+            pair_act[group] = held.tile([P, 2 * CHUNK], F32, name="pair_act%d" % group, tag=tag, align_bytes=64)
             pair_ub[group] = held.tile([P, 2 * CHUNK], F32, name="pair_ub%d" % group, align_bytes=64)
             for s in range(SUBS):
-                first_token = (s - group % 2) % SUBS * SUB
-                cols = slice(first_token, first_token + SUB)
+                cols = slice(s * SUB, (s + 1) * SUB)
+                on_gpsimd = s < gpsimd_subs(group)
                 banks = []
-                ub_tag, ub_bufs = ("ub_last", 1) if s == SUBS - 1 else ("ub", 2)
-                for tag, name, first, bufs in (("ga", "wg", 0, 2), (ub_tag, "wu", R, ub_bufs)):
-                    bank = psum.tile([P, PACK, SUB], F32, name=tag, bufs=bufs)
+                for tag, name, first in (("ga", "wg", 0), ("ub" if s < 2 else "ub_held", "wu", R)):
+                    bank = psum.tile([P, PACK, SUB], F32, name=tag, bufs=4 if tag == "ga" else 2)
                     for t in range(PACK):
                         w_cols = slice(first + a * PASS_ROWS + t * P, first + a * PASS_ROWS + (t + 1) * P)
                         nc.tensor.matmul_mx(
@@ -179,47 +173,39 @@ def tile_list_gmlpt_gelu_gate_kernel(
                         )
                     banks.append(bank)
                 ga, ub_banks[group, s] = banks
-                if s in (1, 2):
-                    acts[group, s] = pair_act[group][:, (s - 1) * CHUNK : s * CHUNK]
-                    ub_copies[group, s] = pair_ub[group][:, (s - 1) * CHUNK : s * CHUNK]
+                ga_banks[group, s] = ga
+                if s < 2:
+                    acts[group, s] = pair_act[group][:, s * CHUNK : (s + 1) * CHUNK]
                 else:
-                    acts[group, s] = ring.tile([P, CHUNK], F32, name="act%d" % s, align_bytes=64, bufs=2)[:]
-                    if s in on_gpsimd:
-                        ub_copies[group, s] = ring.tile([P, CHUNK], F32, name="ub_copy", align_bytes=64, bufs=2)[:]
+                    acts[group, s] = ring.tile([P, CHUNK], F32, name="act", align_bytes=64, bufs=4)[:]
                 nc.scalar.activation(interleaved(acts[group, s]), ga[:].rearrange("p t j -> p j t"), GELU)
-                if s in on_gpsimd:
-                    nc.scalar.copy(interleaved(ub_copies[group, s]), ub_banks[group, s][:].rearrange("p t j -> p j t"))
+                if on_gpsimd:
+                    nc.scalar.copy(
+                        interleaved(pair_ub[group][:, s * CHUNK : (s + 1) * CHUNK]),
+                        ub_banks[group, s][:].rearrange("p t j -> p j t"),
+                    )
 
-        def h_cols(group, s, count=1):
-            place = SUBS if s == 0 and group % 2 else s
-            return h[:, place * CHUNK : (place + count) * CHUNK]
+        def products_on_gpsimd(group):
+            cols = slice(0, gpsimd_subs(group) * CHUNK)
+            nc.gpsimd.tensor_tensor(h_of(group)[:, cols], pair_ub[group][:, cols], pair_act[group][:, cols], MULT)
 
-        def product_on_gpsimd(group, piece):
-            if len(piece) == 2:
-                nc.gpsimd.tensor_tensor(h_cols(group, piece[0], 2), pair_ub[group][:], pair_act[group][:], MULT)
-            else:
-                nc.gpsimd.tensor_tensor(h_cols(group, piece[0]), ub_copies[group, piece[0]], acts[group, piece[0]], MULT)
-
-        def product_on_vector(group, s):
-            nc.vector.tensor_tensor(
-                interleaved(h_cols(group, s)),
-                ub_banks[group, s][:].rearrange("p t j -> p j t"),
-                interleaved(acts[group, s]),
-                MULT,
-            )
+        def products_on_vector(group):
+            for s in range(gpsimd_subs(group), SUBS):
+                nc.vector.tensor_tensor(
+                    interleaved(h_of(group)[:, s * CHUNK : (s + 1) * CHUNK]),
+                    ub_banks[group, s][:].rearrange("p t j -> p j t"),
+                    interleaved(acts[group, s]),
+                    MULT,
+                )
 
         def quantise(group):
             h_codes[group] = held.tile([P, CHUNK], U32, name="h_codes%d" % group, align_bytes=64)
             h_planes[group] = held.tile([P, CHUNK], U8, name="h_plane%d" % group, align_bytes=64)
-            nc.vector.quantize_mx(out=h_codes[group][:].bitcast(FP8X4), scales=h_planes[group][:], in_=h[:, group % 2 * CHUNK : (group % 2 + SUBS) * CHUNK])
-
-        def gather_gate(c, n, into):
-            picked[c, n] = into
-            nc.vector.tensor_copy(into, gates[n][:].indirect(chunk_offsets(c)))
+            nc.vector.quantize_mx(out=h_codes[group][:].bitcast(FP8X4), scales=h_planes[group][:], in_=h_of(group)[:])
 
         def down_pass(c, n, a, bank):
             nc.tensor.matmul_mx(
-                out=bank[:],
+                out=bank,
                 lhsT=wd[:, a, 2 * n * P : 2 * (n + 1) * P].bitcast(FP4X4),
                 lhsT_scale=wd_plane[:, a * N + n * P : a * N + (n + 1) * P],
                 rhs=h_codes[c * R_PASSES + a][:].bitcast(FP8X4),
@@ -228,68 +214,60 @@ def tile_list_gmlpt_gelu_gate_kernel(
                 stop=(a == R_PASSES - 1),
             )
 
-        def gate_and_store(c, n, bank=None):
-            if bank is None:
-                bank = psum.tile([P, CHUNK], F32, name="y_bank", bufs=3)
-                down_pass(c, n, 0, bank)
-            down_pass(c, n, 1, bank)
-            nc.vector.tensor_tensor(picked[c, n], bank[:], picked[c, n], MULT)
-            nc.sync.dma_start(out[n * P : (n + 1) * P, c * CHUNK : (c + 1) * CHUNK], picked[c, n])
+        def down(c, n, y, bank):
+            for a in range(R_PASSES):
+                down_pass(c, n, a, bank)
+            nc.scalar.copy(y, bank)
 
-        units = [(c, n) for c in range(CHUNKS) for n in range(N_TILES)]
-        to_gather, to_gate = list(units), list(units)
+        def store(c, n, res):
+            nc.sync.dma_start(out[n * P : (n + 1) * P, c * CHUNK : (c + 1) * CHUNK], res)
 
-        def freed_slices(group):
-            return [pair[group][:, half * CHUNK : (half + 1) * CHUNK] for half in (1, 0) for pair in (pair_ub, pair_act)]
+        def gate_fused(c, n, y, res):
+            nc.vector.tensor_tensor(res, gates[n][:].indirect(chunk_offsets(c)), y, MULT)
+            store(c, n, res)
 
-        last_banks = {}
+        last = CHUNKS - 1
+        fused = [(c, n) for c in range(last) for n in range(N_TILES)]
         first_stage(0)
-        for piece in gpsimd_pieces(0):
-            product_on_gpsimd(0, piece)
-        product_on_vector(0, 2)
-        product_on_vector(0, 3)
-        first_stage(1)
-        load_gate(N_TILES - 1)
-        for group in range(1, GROUPS):
-            free = freed_slices(group - 1)
-            left = CYCLE_STEPS - 1
-            gathers, gated = [], []
-            for c, n in list(to_gate):
-                cost = 3 if (c, n) in to_gather else 1
-                if R_PASSES * (c + 1) <= group and n < group and cost <= left:
-                    if (c, n) in to_gather:
-                        to_gather.remove((c, n))
-                        gathers.append((c, n))
-                    to_gate.remove((c, n))
-                    gated.append((c, n))
-                    left = left - cost
-            for c, n in list(to_gather):
-                if n < group and left >= 1 and len(to_gather) > 1:
-                    to_gather.remove((c, n))
-                    gathers.append((c, n))
-                    left = left - 2
-            first_piece, *later_pieces = gpsimd_pieces(group)
-            product_on_gpsimd(group, first_piece)
-            gather_gate(*gathers[0], free.pop(0))
-            quantise(group - 1)
-            for piece in later_pieces:
-                product_on_gpsimd(group, piece)
-            for unit in gathers[1:2]:
-                gather_gate(*unit, free.pop(0))
-            product_on_vector(group, SUBS - 1)
-            for unit in gated:
-                gate_and_store(*unit)
-            for unit in gathers[2:]:
-                gather_gate(*unit, free.pop(0))
+        for group in range(GROUPS):
+            steps = [fused.pop(0) for i in range(2)] if group > R_PASSES else []
+            if group == GROUPS - 1:
+                steps.extend(fused)
+            ys = []
+            for i in range(len(steps)):
+                if i == len(steps) - 1 and group + 1 < GROUPS:
+                    ys.append(h_of(group + 1)[:, : 2 * CHUNK].bitcast(F32))
+                else:
+                    ys.append(ring.tile([P, CHUNK], F32, name="y", align_bytes=64, bufs=4)[:])
+            for i, (unit, y) in enumerate(zip(steps, ys)):
+                down(*unit, y, ga_banks[group, (2 + i) % SUBS][:].rearrange("p t j -> p (t j)"))
+            if gpsimd_subs(group):
+                products_on_gpsimd(group)
+            if group == 0:
+                gather_words(2, "x_words2")
+            elif group == 2:
+                gather_words(3, "x_words3")
+            elif 2 < group < GROUPS - 1:
+                n = group - 3
+                picked[n] = pair_act[group - 1][:, :CHUNK]
+                nc.vector.tensor_copy(picked[n], gates[n][:].indirect(chunk_offsets(last)))
+            products_on_vector(group)
             if group + 1 < GROUPS:
                 first_stage(group + 1)
             else:
-                for n, tag in enumerate(("ga", "ub", "ga", "ub")):
-                    last_banks[CHUNKS - 1, n] = psum.tile([P, CHUNK], F32, name="last_bank", tag=tag, bufs=2)
-                    down_pass(CHUNKS - 1, n, 0, last_banks[CHUNKS - 1, n])
-        quantise(GROUPS - 1)
-        free = freed_slices(GROUPS - 1)
-        for unit in to_gather:
-            gather_gate(*unit, free.pop(0))
-        for unit in to_gate:
-            gate_and_store(*unit, last_banks.get(unit))
+                for n, tag in enumerate(("ga", "ub", "ga", "ga")):
+                    last_banks[n] = psum.tile([P, CHUNK], F32, name="last_bank", tag=tag, bufs=4 if tag == "ga" else 2)[:]
+                    down_pass(last, n, 0, last_banks[n])
+            results = [pair_ub[group][:, :CHUNK], pair_ub[group][:, CHUNK:]]
+            if group == GROUPS - 1:
+                results = [results[0], pair_act[group][:, :CHUNK], results[1], pair_act[group][:, CHUNK:]]
+            early = 2
+            for unit, y, res in list(zip(steps, ys, results))[:early]:
+                gate_fused(*unit, y, res)
+            quantise(group)
+        for unit, y, res in list(zip(steps, ys, results))[early:]:
+            gate_fused(*unit, y, res)
+        for n in range(N_TILES):
+            down_pass(last, n, 1, last_banks[n])
+            nc.vector.tensor_tensor(picked[n], last_banks[n], picked[n], MULT)
+            store(last, n, picked[n])

@@ -26,10 +26,10 @@ SUB = 128
 SUBS = CHUNK // SUB
 N_TILES = N // P
 GROUPS = CHUNKS * R_PASSES
-EARLY = J - CHUNK
+EARLY = J // 2
 WD_FIRST = EARLY + 2 * R
 STAGED_BYTES = WD_FIRST + R_PASSES * N
-PLANE_BYTES = STAGED_BYTES + CHUNK
+PLANE_BYTES = STAGED_BYTES + EARLY
 GATE_BYTES = 4 * T
 
 
@@ -48,11 +48,11 @@ def tile_list_gmlpt_gelu_gate_kernel(
 
         tab_rows = held.tile([P, T], U8, name="tab_rows", align_bytes=64)
         nc.vector.memset(tab_rows[:].bitcast(I32), 0)
-        w_rows = shared.tile([P, 2 * R], U8, name="w_rows", align_bytes=64, offset=GATE_BYTES - R)
+        w_rows = held.tile([P, 2 * R], U8, name="w_rows", align_bytes=64)
         nc.gpsimd.memset(w_rows[:].bitcast(I32), 0)
         planes = held.tile([P, PLANE_BYTES], U8, name="planes", align_bytes=64)
         nc.gpsimd.memset(planes[:].bitcast(I32), 0)
-        staged = held.tile([P, STAGED_BYTES], U8, name="staged", tag="gate1", align_bytes=64)
+        staged = shared.tile([P, STAGED_BYTES], U8, name="staged", align_bytes=64, offset=3 * GATE_BYTES - R)
 
         warm = held.tile([P, 1], F32, name="warm")
         nc.vector.memset(warm[:], 0.0)
@@ -61,12 +61,11 @@ def tile_list_gmlpt_gelu_gate_kernel(
 
         raw = {}
 
-        def load_w_words(a):
+        def load_w_words(a, both):
             for i, (name, words) in enumerate((("wg", wg_words), ("wu", wu_words))):
-                tag = "gate%d" % (2 + i) if a else name
-                raw[name, a] = held.tile([P, PASS_ROWS], I32, name="%s_raw%d" % (name, a), tag=tag, align_bytes=64)
+                raw[name, a] = both[i]
                 nc.sync.dma_start(
-                    raw[name, a][:],
+                    raw[name, a],
                     words[0, :, a * PASS_ROWS : (a + 1) * PASS_ROWS, :].rearrange("p n t -> p (n t)").bitcast(I32),
                 )
 
@@ -79,8 +78,7 @@ def tile_list_gmlpt_gelu_gate_kernel(
         )
         tab = held.tile([P, T], U32, name="tab", align_bytes=64)
         nc.sync.dma_start(tab[:].bitcast(I32), tab_words[0].rearrange("p n t -> p (n t)").bitcast(I32))
-        load_w_words(0)
-        load_w_words(1)
+        load_w_words(0, [held.tile([P, PASS_ROWS], I32, name=name, align_bytes=64)[:] for name in ("wg", "wu")])
 
         def chunk_offsets(c, count=1):
             return offsets[:, c * (CHUNK // 16) : (c + count) * (CHUNK // 16)]
@@ -91,15 +89,17 @@ def tile_list_gmlpt_gelu_gate_kernel(
                     plane[32 * q : 32 * q + 4, :].bitcast(I32), rows[32 * q : 32 * q + 32 : 8, :].bitcast(I32)
                 )
 
-        x_rows = held.tile([P, EARLY], U8, name="x_rows", align_bytes=64)
-        nc.vector.tensor_copy(x_rows[:], tab_rows[:].indirect(chunk_offsets(0, CHUNKS - 1)))
-        nc.vector.tensor_copy(staged[:, :EARLY].bitcast(I32), x_rows[:].bitcast(I32))
-        nc.gpsimd.tensor_copy(
+        nc.vector.tensor_copy(
             staged[:, EARLY:WD_FIRST].rearrange("p (a t m) -> p a t m", a=2 * R_PASSES, t=PACK),
             w_rows[:].rearrange("p (a m t) -> p a t m", a=2 * R_PASSES, t=PACK),
         )
+        x_rows = shared.tile([P, EARLY], U8, name="x_rows", align_bytes=64, offset=GATE_BYTES - CHUNK)
+        nc.vector.tensor_copy(x_rows[:], tab_rows[:].indirect(chunk_offsets(0, 2)))
+        nc.vector.tensor_copy(staged[:, :EARLY].bitcast(I32), x_rows[:].bitcast(I32))
         move_rows(planes[:, :STAGED_BYTES], staged[:])
-        x_firsts = [0, CHUNK, 2 * CHUNK, STAGED_BYTES]
+        late_words = shared.tile([P, 2 * PASS_ROWS], I32, name="late_words", align_bytes=64, offset=GATE_BYTES)
+        load_w_words(1, [late_words[:, :PASS_ROWS], late_words[:, PASS_ROWS:]])
+        x_firsts = [0, CHUNK, STAGED_BYTES, STAGED_BYTES + CHUNK]
         x_planes = [planes[:, first : first + CHUNK] for first in x_firsts]
         w_plane, wd_plane = planes[:, EARLY:WD_FIRST], planes[:, WD_FIRST:STAGED_BYTES]
 
@@ -108,29 +108,27 @@ def tile_list_gmlpt_gelu_gate_kernel(
         def deal_words(a):
             for name in ("wg", "wu"):
                 dealt[name, a] = held.tile([P, PASS_ROWS], I32, name="%s%d" % (name, a), align_bytes=64)
-                nc.gpsimd.tensor_copy(
+                nc.vector.tensor_copy(
                     dealt[name, a][:].rearrange("p (t c i) -> p c t i", t=PACK, i=4),
-                    raw[name, a][:].rearrange("p (c i t) -> p c t i", t=PACK, i=4),
+                    raw[name, a].rearrange("p (c i t) -> p c t i", t=PACK, i=4),
                 )
 
         def gather_words(c, tag):
             x_words[c] = held.tile([P, CHUNK], U32, name="x_words%d" % c, tag=tag, align_bytes=64)
             nc.vector.tensor_copy(x_words[c][:], tab[:].indirect(chunk_offsets(c)))
 
-        deal_words(0)
-        deal_words(1)
-        wd = shared.tile([P, R_PASSES, 2 * N], U8, name="wd", align_bytes=64, offset=GATE_BYTES)
+        wd = shared.tile([P, R_PASSES, 2 * N], U8, name="wd", align_bytes=64, offset=3 * GATE_BYTES)
         nc.sync.dma_start(wd[:].bitcast(I32), wd_words.rearrange("a p n -> p a n").bitcast(I32))
         gather_words(0, "x_words0")
-        late_rows = held.tile([P, CHUNK], U8, name="late_rows", tag="wg", align_bytes=64)
-        nc.vector.tensor_copy(late_rows[:], tab_rows[:].indirect(chunk_offsets(CHUNKS - 1)))
-        gather_words(1, "x_words1")
+        deal_words(0)
+        late_rows = held.tile([P, EARLY], U8, name="late_rows", tag="wu", align_bytes=64)
+        deal_words(1)
+        gather_words(1, "wg")
+        nc.vector.tensor_copy(late_rows[:], tab_rows[:].indirect(chunk_offsets(2, 2)))
         gates = []
         for n in range(N_TILES):
-            if n == 0:
-                gate = shared.tile([P, T], F32, name="gate0", align_bytes=64, offset=0)
-            else:
-                gate = held.tile([P, T], F32, name="gate%d" % n, align_bytes=64)
+            first = (0, 2 * GATE_BYTES, 3 * GATE_BYTES + 4 * N, GATE_BYTES)[n]
+            gate = shared.tile([P, T], F32, name="gate%d" % n, align_bytes=64, offset=first)
             nc.sync.dma_start(gate[:], gT[n * P : (n + 1) * P, :])
             gates.append(gate)
             if n == 1:
@@ -144,14 +142,14 @@ def tile_list_gmlpt_gelu_gate_kernel(
         h_codes, h_planes, pair_act, pair_ub, acts, ub_banks, picked, last_banks, ga_banks = {}, {}, {}, {}, {}, {}, {}, {}, {}
 
         def gpsimd_subs(group):
-            return (0, 0, 1, 2, 2, 2, 2, 1)[group]
+            return 2 if group < GROUPS - 2 else 1
 
         def interleaved(ap):
             return ap.rearrange("p (j t) -> p j t", t=PACK)
 
         def first_stage(group):
             c, a = divmod(group, R_PASSES)
-            tag = "x_words3" if group == 1 else "pair_act%d" % group
+            tag = "x_words3" if group == 0 else "pair_act%d" % group
             pair_act[group] = held.tile([P, 2 * CHUNK], F32, name="pair_act%d" % group, tag=tag, align_bytes=64)
             pair_ub[group] = held.tile([P, 2 * CHUNK], F32, name="pair_ub%d" % group, align_bytes=64)
             for s in range(SUBS):
@@ -176,6 +174,10 @@ def tile_list_gmlpt_gelu_gate_kernel(
                 ga_banks[group, s] = ga
                 if s < 2:
                     acts[group, s] = pair_act[group][:, s * CHUNK : (s + 1) * CHUNK]
+                elif s == SUBS - 1 and group <= R_PASSES:
+                    acts[group, s] = h_of(group + 1)[:, : 2 * CHUNK].bitcast(F32)
+                elif (group, s) == (0, 2):
+                    acts[group, s] = held.tile([P, CHUNK], F32, name="first_act", tag="x_words2", align_bytes=64)[:]
                 else:
                     acts[group, s] = ring.tile([P, CHUNK], F32, name="act", align_bytes=64, bufs=4)[:]
                 nc.scalar.activation(interleaved(acts[group, s]), ga[:].rearrange("p t j -> p j t"), GELU)
@@ -241,14 +243,13 @@ def tile_list_gmlpt_gelu_gate_kernel(
                     ys.append(ring.tile([P, CHUNK], F32, name="y", align_bytes=64, bufs=4)[:])
             for i, (unit, y) in enumerate(zip(steps, ys)):
                 down(*unit, y, ga_banks[group, (2 + i) % SUBS][:].rearrange("p t j -> p (t j)"))
-            if gpsimd_subs(group):
-                products_on_gpsimd(group)
+            products_on_gpsimd(group)
             if group == 0:
                 gather_words(2, "x_words2")
-            elif group == 2:
+            elif group == 1:
                 gather_words(3, "x_words3")
-            elif 2 < group < GROUPS - 1:
-                n = group - 3
+            elif group < GROUPS - 2:
+                n = group - 2
                 picked[n] = pair_act[group - 1][:, :CHUNK]
                 nc.vector.tensor_copy(picked[n], gates[n][:].indirect(chunk_offsets(last)))
             products_on_vector(group)
@@ -259,6 +260,8 @@ def tile_list_gmlpt_gelu_gate_kernel(
                     last_banks[n] = psum.tile([P, CHUNK], F32, name="last_bank", tag=tag, bufs=4 if tag == "ga" else 2)[:]
                     down_pass(last, n, 0, last_banks[n])
             results = [pair_ub[group][:, :CHUNK], pair_ub[group][:, CHUNK:]]
+            if group == GROUPS - 2:
+                results = [results[0], pair_act[group][:, :CHUNK]]
             if group == GROUPS - 1:
                 results = [results[0], pair_act[group][:, :CHUNK], results[1], pair_act[group][:, CHUNK:]]
             early = 2

@@ -46,18 +46,13 @@ def tile_list_gmlpt_gelu_gate_kernel(
         offsets = held.tile([P, J // 16], U16, name="offsets")
         nc.sync.dma_start(offsets[:], offs)
 
-        tab_rows = held.tile([P, T], U8, name="tab_rows", align_bytes=64)
+        tab_rows = shared.tile([P, T], U8, name="tab_rows", align_bytes=64, offset=3 * GATE_BYTES - T // 2)
         nc.vector.memset(tab_rows[:].bitcast(I32), 0)
         w_rows = held.tile([P, 2 * R], U8, name="w_rows", align_bytes=64)
         nc.gpsimd.memset(w_rows[:].bitcast(I32), 0)
         planes = held.tile([P, PLANE_BYTES], U8, name="planes", align_bytes=64)
-        nc.gpsimd.memset(planes[:].bitcast(I32), 0)
-        staged = shared.tile([P, STAGED_BYTES], U8, name="staged", align_bytes=64, offset=3 * GATE_BYTES - R)
-
-        warm = held.tile([P, 1], F32, name="warm")
-        nc.vector.memset(warm[:], 0.0)
-        warm_out = held.tile([P, 1], F32, name="warm_out")
-        nc.scalar.activation(warm_out[:], warm[:], GELU)
+        nc.vector.memset(planes[:].bitcast(I32), 0)
+        staged = held.tile([P, STAGED_BYTES], U8, name="staged", align_bytes=64)
 
         raw = {}
 
@@ -78,7 +73,8 @@ def tile_list_gmlpt_gelu_gate_kernel(
         )
         tab = held.tile([P, T], U32, name="tab", align_bytes=64)
         nc.sync.dma_start(tab[:].bitcast(I32), tab_words[0].rearrange("p n t -> p (n t)").bitcast(I32))
-        load_w_words(0, [held.tile([P, PASS_ROWS], I32, name=name, align_bytes=64)[:] for name in ("wg", "wu")])
+        early_words = shared.tile([P, 2 * PASS_ROWS], I32, name="early_words", align_bytes=64, offset=4 * GATE_BYTES)
+        load_w_words(0, [early_words[:, :PASS_ROWS], early_words[:, PASS_ROWS:]])
 
         def chunk_offsets(c, count=1):
             return offsets[:, c * (CHUNK // 16) : (c + count) * (CHUNK // 16)]
@@ -117,21 +113,22 @@ def tile_list_gmlpt_gelu_gate_kernel(
             x_words[c] = held.tile([P, CHUNK], U32, name="x_words%d" % c, tag=tag, align_bytes=64)
             nc.vector.tensor_copy(x_words[c][:], tab[:].indirect(chunk_offsets(c)))
 
-        wd = shared.tile([P, R_PASSES, 2 * N], U8, name="wd", align_bytes=64, offset=3 * GATE_BYTES)
+        wd = held.tile([P, R_PASSES, 2 * N], U8, name="wd", tag="staged", align_bytes=64)
         nc.sync.dma_start(wd[:].bitcast(I32), wd_words.rearrange("a p n -> p a n").bitcast(I32))
         gather_words(0, "x_words0")
         deal_words(0)
-        late_rows = held.tile([P, EARLY], U8, name="late_rows", tag="wu", align_bytes=64)
-        deal_words(1)
-        gather_words(1, "wg")
+        late_rows = shared.tile([P, EARLY], U8, name="late_rows", align_bytes=64, offset=4 * GATE_BYTES)
         nc.vector.tensor_copy(late_rows[:], tab_rows[:].indirect(chunk_offsets(2, 2)))
+        deal_words(1)
+        x_words[1] = shared.tile([P, CHUNK], U32, name="x_words1", align_bytes=64, offset=4 * GATE_BYTES + 4 * CHUNK)
+        nc.vector.tensor_copy(x_words[1][:], tab[:].indirect(chunk_offsets(1)))
         gates = []
         for n in range(N_TILES):
-            first = (0, 2 * GATE_BYTES, 3 * GATE_BYTES + 4 * N, GATE_BYTES)[n]
+            first = (0, 2 * GATE_BYTES, 3 * GATE_BYTES, GATE_BYTES)[n]
             gate = shared.tile([P, T], F32, name="gate%d" % n, align_bytes=64, offset=first)
             nc.sync.dma_start(gate[:], gT[n * P : (n + 1) * P, :])
             gates.append(gate)
-            if n == 1:
+            if n == 0:
                 move_rows(planes[:, STAGED_BYTES:], late_rows[:])
 
         h_tiles = [held.tile([P, SUBS * CHUNK], BF16, name="h%d" % i, align_bytes=64) for i in range(3)]
@@ -142,7 +139,7 @@ def tile_list_gmlpt_gelu_gate_kernel(
         h_codes, h_planes, pair_act, pair_ub, acts, ub_banks, picked, last_banks, ga_banks = {}, {}, {}, {}, {}, {}, {}, {}, {}
 
         def gpsimd_subs(group):
-            return 2 if group < GROUPS - 2 else 1
+            return 2 if group < R_PASSES else 1
 
         def interleaved(ap):
             return ap.rearrange("p (j t) -> p j t", t=PACK)
@@ -151,7 +148,7 @@ def tile_list_gmlpt_gelu_gate_kernel(
             c, a = divmod(group, R_PASSES)
             tag = "x_words3" if group == 0 else "pair_act%d" % group
             pair_act[group] = held.tile([P, 2 * CHUNK], F32, name="pair_act%d" % group, tag=tag, align_bytes=64)
-            pair_ub[group] = held.tile([P, 2 * CHUNK], F32, name="pair_ub%d" % group, align_bytes=64)
+            pair_ub[group] = ring.tile([P, 2 * CHUNK], F32, name="pair_ub", align_bytes=64, bufs=2)
             for s in range(SUBS):
                 cols = slice(s * SUB, (s + 1) * SUB)
                 on_gpsimd = s < gpsimd_subs(group)
@@ -178,8 +175,10 @@ def tile_list_gmlpt_gelu_gate_kernel(
                     acts[group, s] = h_of(group + 1)[:, : 2 * CHUNK].bitcast(F32)
                 elif (group, s) == (0, 2):
                     acts[group, s] = held.tile([P, CHUNK], F32, name="first_act", tag="x_words2", align_bytes=64)[:]
+                elif s == 2:
+                    acts[group, s] = held.tile([P, CHUNK], F32, name="act%d" % group, align_bytes=64)[:]
                 else:
-                    acts[group, s] = ring.tile([P, CHUNK], F32, name="act", align_bytes=64, bufs=4)[:]
+                    acts[group, s] = ring.tile([P, CHUNK], F32, name="act", align_bytes=64, bufs=2)[:]
                 nc.scalar.activation(interleaved(acts[group, s]), ga[:].rearrange("p t j -> p j t"), GELU)
                 if on_gpsimd:
                     nc.scalar.copy(
@@ -228,49 +227,42 @@ def tile_list_gmlpt_gelu_gate_kernel(
             nc.vector.tensor_tensor(res, gates[n][:].indirect(chunk_offsets(c)), y, MULT)
             store(c, n, res)
 
-        last = CHUNKS - 1
-        fused = [(c, n) for c in range(last) for n in range(N_TILES)]
+        def as_y_bank(bank):
+            return bank[:].rearrange("p t j -> p (t j)")
+
+        def fresh_y():
+            return ring.tile([P, CHUNK], F32, name="y", align_bytes=64, bufs=4)[:]
+
+        units = [(c, n) for c in range(CHUNKS) for n in range(N_TILES)]
         first_stage(0)
         for group in range(GROUPS):
-            steps = [fused.pop(0) for i in range(2)] if group > R_PASSES else []
-            if group == GROUPS - 1:
-                steps.extend(fused)
+            steps = [units.pop(0) for i in range(2)] if group > R_PASSES else []
             ys = []
-            for i in range(len(steps)):
-                if i == len(steps) - 1 and group + 1 < GROUPS:
-                    ys.append(h_of(group + 1)[:, : 2 * CHUNK].bitcast(F32))
-                else:
-                    ys.append(ring.tile([P, CHUNK], F32, name="y", align_bytes=64, bufs=4)[:])
+            if steps:
+                ys = [fresh_y(), h_of(group + 1)[:, : 2 * CHUNK].bitcast(F32)]
             for i, (unit, y) in enumerate(zip(steps, ys)):
-                down(*unit, y, ga_banks[group, (2 + i) % SUBS][:].rearrange("p t j -> p (t j)"))
+                down(*unit, y, as_y_bank(ga_banks[group, 2 + i]))
             products_on_gpsimd(group)
-            if group == 0:
-                gather_words(2, "x_words2")
-            elif group == 1:
-                gather_words(3, "x_words3")
-            elif group < GROUPS - 2:
-                n = group - 2
-                picked[n] = pair_act[group - 1][:, :CHUNK]
-                nc.vector.tensor_copy(picked[n], gates[n][:].indirect(chunk_offsets(last)))
+            if group < R_PASSES:
+                gather_words(group + 2, "x_words%d" % (group + 2))
             products_on_vector(group)
             if group + 1 < GROUPS:
                 first_stage(group + 1)
             else:
-                for n, tag in enumerate(("ga", "ub", "ga", "ga")):
-                    last_banks[n] = psum.tile([P, CHUNK], F32, name="last_bank", tag=tag, bufs=4 if tag == "ga" else 2)[:]
-                    down_pass(last, n, 0, last_banks[n])
-            results = [pair_ub[group][:, :CHUNK], pair_ub[group][:, CHUNK:]]
-            if group == GROUPS - 2:
-                results = [results[0], pair_act[group][:, :CHUNK]]
-            if group == GROUPS - 1:
-                results = [results[0], pair_act[group][:, :CHUNK], results[1], pair_act[group][:, CHUNK:]]
-            early = 2
-            for unit, y, res in list(zip(steps, ys, results))[:early]:
+                late_ys = [fresh_y() for unit in units[:2]]
+                for i, (unit, y) in enumerate(zip(units, late_ys)):
+                    down(*unit, y, as_y_bank(ga_banks[group, i]))
+                for unit, tag in zip(units[2:], ("ub", "ga", "ga", "ga")):
+                    bank = psum.tile([P, CHUNK], F32, name="last_bank", tag=tag, bufs=4 if tag == "ga" else 2)
+                    last_banks[unit] = bank[:]
+                    down_pass(*unit, 0, last_banks[unit])
+            for unit, y, res in zip(steps, ys, (acts[group, 1], acts[group, 2])):
                 gate_fused(*unit, y, res)
             quantise(group)
-        for unit, y, res in list(zip(steps, ys, results))[early:]:
-            gate_fused(*unit, y, res)
-        for n in range(N_TILES):
-            down_pass(last, n, 1, last_banks[n])
-            nc.vector.tensor_tensor(picked[n], last_banks[n], picked[n], MULT)
-            store(last, n, picked[n])
+        for unit in units[2:]:
+            down_pass(*unit, 1, last_banks[unit])
+            late_ys.append(ring.tile([P, CHUNK], F32, name="last_y", align_bytes=64, bufs=4)[:])
+            nc.scalar.copy(late_ys[-1], last_banks[unit])
+        for unit, y in zip(units, late_ys):
+            res = ring.tile([P, CHUNK], F32, name="res", align_bytes=64, bufs=6)
+            gate_fused(*unit, y, res[:])

@@ -31,6 +31,7 @@ WD_FIRST = EARLY + 2 * R
 STAGED_BYTES = WD_FIRST + R_PASSES * N
 PLANE_BYTES = STAGED_BYTES + EARLY
 GATE_BYTES = 4 * T
+EXTRA_TOKENS = 32
 
 
 def tile_list_gmlpt_gelu_gate_kernel(
@@ -138,20 +139,21 @@ def tile_list_gmlpt_gelu_gate_kernel(
 
         h_codes, h_planes, pair_act, pair_ub, acts, ub_banks, picked, last_banks, ga_banks = {}, {}, {}, {}, {}, {}, {}, {}, {}
 
-        def gpsimd_subs(group):
-            return 2 if group < R_PASSES else 1
+        def gpsimd_tokens(group, s):
+            share = 2 * SUB if group < R_PASSES else SUB + EXTRA_TOKENS
+            return max(0, min(SUB, share - s * SUB))
 
         def interleaved(ap):
             return ap.rearrange("p (j t) -> p j t", t=PACK)
 
         def first_stage(group):
             c, a = divmod(group, R_PASSES)
-            tag = "x_words3" if group == 0 else "pair_act%d" % group
+            tag = "x_words3" if group == 0 else "pair_act%d" % (group % 2)
             pair_act[group] = held.tile([P, 2 * CHUNK], F32, name="pair_act%d" % group, tag=tag, align_bytes=64)
             pair_ub[group] = ring.tile([P, 2 * CHUNK], F32, name="pair_ub", align_bytes=64, bufs=2)
             for s in range(SUBS):
                 cols = slice(s * SUB, (s + 1) * SUB)
-                on_gpsimd = s < gpsimd_subs(group)
+                tokens = gpsimd_tokens(group, s)
                 banks = []
                 for tag, name, first in (("ga", "wg", 0), ("ub" if s < 2 else "ub_held", "wu", R)):
                     bank = psum.tile([P, PACK, SUB], F32, name=tag, bufs=4 if tag == "ga" else 2)
@@ -175,27 +177,26 @@ def tile_list_gmlpt_gelu_gate_kernel(
                     acts[group, s] = h_of(group + 1)[:, : 2 * CHUNK].bitcast(F32)
                 elif (group, s) == (0, 2):
                     acts[group, s] = held.tile([P, CHUNK], F32, name="first_act", tag="x_words2", align_bytes=64)[:]
-                elif s == 2:
-                    acts[group, s] = held.tile([P, CHUNK], F32, name="act%d" % group, align_bytes=64)[:]
                 else:
-                    acts[group, s] = ring.tile([P, CHUNK], F32, name="act", align_bytes=64, bufs=2)[:]
+                    acts[group, s] = held.tile([P, CHUNK], F32, name="act%d_%d" % (group, s), align_bytes=64)[:]
                 nc.scalar.activation(interleaved(acts[group, s]), ga[:].rearrange("p t j -> p j t"), GELU)
-                if on_gpsimd:
+                if tokens:
                     nc.scalar.copy(
-                        interleaved(pair_ub[group][:, s * CHUNK : (s + 1) * CHUNK]),
-                        ub_banks[group, s][:].rearrange("p t j -> p j t"),
+                        interleaved(pair_ub[group][:, s * CHUNK : s * CHUNK + tokens * PACK]),
+                        ub_banks[group, s][:, :, :tokens].rearrange("p t j -> p j t"),
                     )
 
         def products_on_gpsimd(group):
-            cols = slice(0, gpsimd_subs(group) * CHUNK)
+            cols = slice(0, PACK * sum(gpsimd_tokens(group, s) for s in range(SUBS)))
             nc.gpsimd.tensor_tensor(h_of(group)[:, cols], pair_ub[group][:, cols], pair_act[group][:, cols], MULT)
 
         def products_on_vector(group):
-            for s in range(gpsimd_subs(group), SUBS):
+            for s in [s for s in range(SUBS) if gpsimd_tokens(group, s) < SUB]:
+                done = gpsimd_tokens(group, s)
                 nc.vector.tensor_tensor(
-                    interleaved(h_of(group)[:, s * CHUNK : (s + 1) * CHUNK]),
-                    ub_banks[group, s][:].rearrange("p t j -> p j t"),
-                    interleaved(acts[group, s]),
+                    interleaved(h_of(group)[:, s * CHUNK + done * PACK : (s + 1) * CHUNK]),
+                    ub_banks[group, s][:, :, done:].rearrange("p t j -> p j t"),
+                    interleaved(acts[group, s][:, done * PACK :]),
                     MULT,
                 )
 
@@ -256,13 +257,19 @@ def tile_list_gmlpt_gelu_gate_kernel(
                     bank = psum.tile([P, CHUNK], F32, name="last_bank", tag=tag, bufs=4 if tag == "ga" else 2)
                     last_banks[unit] = bank[:]
                     down_pass(*unit, 0, last_banks[unit])
-            for unit, y, res in zip(steps, ys, (acts[group, 1], acts[group, 2])):
+            for unit, y, res in zip(steps, ys, (acts[group, 2], acts[group, 3])):
                 gate_fused(*unit, y, res)
             quantise(group)
         for unit in units[2:]:
             down_pass(*unit, 1, last_banks[unit])
             late_ys.append(ring.tile([P, CHUNK], F32, name="last_y", align_bytes=64, bufs=4)[:])
             nc.scalar.copy(late_ys[-1], last_banks[unit])
-        for unit, y in zip(units, late_ys):
+        for unit, y in zip(units[:-1], late_ys):
             res = ring.tile([P, CHUNK], F32, name="res", align_bytes=64, bufs=6)
             gate_fused(*unit, y, res[:])
+        c, n = units[-1]
+        res = ring.tile([P, CHUNK], F32, name="res", align_bytes=64, bufs=6)
+        for first, end in ((0, CHUNK - SUB), (CHUNK - SUB, CHUNK)):
+            entries = offsets[:, (c * CHUNK + first) // 16 : (c * CHUNK + end) // 16]
+            nc.vector.tensor_tensor(res[:, first:end], gates[n][:].indirect(entries), late_ys[-1][:, first:end], MULT)
+            nc.sync.dma_start(out[n * P : (n + 1) * P, c * CHUNK + first : c * CHUNK + end], res[:, first:end])

@@ -32,6 +32,7 @@ STAGED_BYTES = WD_FIRST + R_PASSES * N
 PLANE_BYTES = STAGED_BYTES + EARLY
 GATE_BYTES = 4 * T
 EXTRA_TOKENS = 32
+ROWS_FIRST = P - 16
 
 
 def tile_list_gmlpt_gelu_gate_kernel(
@@ -48,9 +49,9 @@ def tile_list_gmlpt_gelu_gate_kernel(
         nc.sync.dma_start(offsets[:], offs)
 
         tab_rows = shared.tile([P, T], U8, name="tab_rows", align_bytes=64, offset=3 * GATE_BYTES - T // 2)
-        nc.vector.memset(tab_rows[:].bitcast(I32), 0)
+        nc.vector.memset(tab_rows[:ROWS_FIRST, :].bitcast(I32), 0)
         w_rows = held.tile([P, 2 * R], U8, name="w_rows", align_bytes=64)
-        nc.gpsimd.memset(w_rows[:].bitcast(I32), 0)
+        nc.gpsimd.memset(w_rows[:ROWS_FIRST, :].bitcast(I32), 0)
         planes = held.tile([P, PLANE_BYTES], U8, name="planes", align_bytes=64)
         nc.vector.memset(planes[:].bitcast(I32), 0)
         staged = held.tile([P, STAGED_BYTES], U8, name="staged", align_bytes=64)
@@ -65,11 +66,11 @@ def tile_list_gmlpt_gelu_gate_kernel(
                     words[0, :, a * PASS_ROWS : (a + 1) * PASS_ROWS, :].rearrange("p n t -> p (n t)").bitcast(I32),
                 )
 
-        nc.sync.dma_start(tab_rows[0:P:8, :].bitcast(I32), tab_scales[0].bitcast(I32))
+        nc.sync.dma_start(tab_rows[ROWS_FIRST:, :].bitcast(I32), tab_scales[0].bitcast(I32))
         for i, scales in enumerate((wg_scales, wu_scales)):
-            nc.sync.dma_start(w_rows[0:P:8, i * R : (i + 1) * R].bitcast(I32), scales[0].bitcast(I32))
+            nc.sync.dma_start(w_rows[ROWS_FIRST:, i * R : (i + 1) * R].bitcast(I32), scales[0].bitcast(I32))
         nc.sync.dma_start(
-            staged[0:P:8, WD_FIRST:].bitcast(I32).rearrange("p (a n) -> p a n", a=R_PASSES),
+            staged[ROWS_FIRST:, WD_FIRST:].bitcast(I32).rearrange("p (a n) -> p a n", a=R_PASSES),
             wd_scales.rearrange("a r n -> r a n").bitcast(I32),
         )
         tab = held.tile([P, T], U32, name="tab", align_bytes=64)
@@ -83,7 +84,7 @@ def tile_list_gmlpt_gelu_gate_kernel(
         def move_rows(plane, rows):
             for q in range(4):
                 nc.sync.dma_start(
-                    plane[32 * q : 32 * q + 4, :].bitcast(I32), rows[32 * q : 32 * q + 32 : 8, :].bitcast(I32)
+                    plane[32 * q : 32 * q + 4, :].bitcast(I32), rows[ROWS_FIRST + 4 * q : ROWS_FIRST + 4 * q + 4, :].bitcast(I32)
                 )
 
         nc.vector.tensor_copy(

@@ -82,10 +82,8 @@ def tile_list_gmlpt_gelu_gate_kernel(
             return offsets[:, c * (CHUNK // 16) : (c + count) * (CHUNK // 16)]
 
         def move_rows(plane, rows):
-            for q in range(4):
-                nc.sync.dma_start(
-                    plane[32 * q : 32 * q + 4, :].bitcast(I32), rows[ROWS_FIRST + 4 * q : ROWS_FIRST + 4 * q + 4, :].bitcast(I32)
-                )
+            for i in range(4):
+                nc.sync.dma_start(plane[i:P:32, :].bitcast(I32), rows[ROWS_FIRST + i : P : 4, :].bitcast(I32))
 
         nc.vector.tensor_copy(
             staged[:, EARLY:WD_FIRST].rearrange("p (a t m) -> p a t m", a=2 * R_PASSES, t=PACK),

@@ -26,11 +26,15 @@ SUB = 128
 SUBS = CHUNK // SUB
 N_TILES = N // P
 GROUPS = CHUNKS * R_PASSES
-EARLY = J // 2
+EARLY = J - CHUNK
 WD_FIRST = EARLY + 2 * R
 STAGED_BYTES = WD_FIRST + R_PASSES * N
-PLANE_BYTES = STAGED_BYTES + EARLY
 GATE_BYTES = 4 * T
+WORDS_BYTES = 8 * PASS_ROWS
+WD_BYTES = R_PASSES * 2 * N
+LATE_WORDS_PLACE = EARLY
+STAGED_PLACE = LATE_WORDS_PLACE + WORDS_BYTES + GATE_BYTES
+GATE_PLACES = (LATE_WORDS_PLACE + WORDS_BYTES,) + tuple(STAGED_PLACE + WD_BYTES + n * GATE_BYTES for n in range(3))
 EXTRA_TOKENS = 32
 ROWS_FIRST = P - 16
 
@@ -48,13 +52,16 @@ def tile_list_gmlpt_gelu_gate_kernel(
         offsets = held.tile([P, J // 16], U16, name="offsets")
         nc.sync.dma_start(offsets[:], offs)
 
-        tab_rows = shared.tile([P, T], U8, name="tab_rows", align_bytes=64, offset=3 * GATE_BYTES - T // 2)
+        tab_rows = held.tile([P, T], U8, name="tab_rows", align_bytes=64)
         nc.vector.memset(tab_rows[:ROWS_FIRST, :].bitcast(I32), 0)
-        w_rows = held.tile([P, 2 * R], U8, name="w_rows", align_bytes=64)
-        nc.gpsimd.memset(w_rows[:ROWS_FIRST, :].bitcast(I32), 0)
-        planes = held.tile([P, PLANE_BYTES], U8, name="planes", align_bytes=64)
-        nc.vector.memset(planes[:].bitcast(I32), 0)
-        staged = held.tile([P, STAGED_BYTES], U8, name="staged", align_bytes=64)
+        wg_rows = held.tile([P, R], U8, name="wg_rows", align_bytes=64)
+        wu_rows = shared.tile([P, R], U8, name="wu_rows", align_bytes=64, offset=GATE_PLACES[0] - CHUNK)
+        w_rows = (wg_rows, wu_rows)
+        for rows in w_rows:
+            nc.gpsimd.memset(rows[:ROWS_FIRST, :].bitcast(I32), 0)
+        planes = held.tile([P, STAGED_BYTES + CHUNK], U8, name="planes", align_bytes=64)
+        nc.gpsimd.memset(planes[:].bitcast(I32), 0)
+        staged = shared.tile([P, STAGED_BYTES], U8, name="staged", align_bytes=64, offset=STAGED_PLACE)
 
         raw = {}
 
@@ -68,14 +75,14 @@ def tile_list_gmlpt_gelu_gate_kernel(
 
         nc.sync.dma_start(tab_rows[ROWS_FIRST:, :].bitcast(I32), tab_scales[0].bitcast(I32))
         for i, scales in enumerate((wg_scales, wu_scales)):
-            nc.sync.dma_start(w_rows[ROWS_FIRST:, i * R : (i + 1) * R].bitcast(I32), scales[0].bitcast(I32))
+            nc.sync.dma_start(w_rows[i][ROWS_FIRST:, :].bitcast(I32), scales[0].bitcast(I32))
         nc.sync.dma_start(
             staged[ROWS_FIRST:, WD_FIRST:].bitcast(I32).rearrange("p (a n) -> p a n", a=R_PASSES),
             wd_scales.rearrange("a r n -> r a n").bitcast(I32),
         )
         tab = held.tile([P, T], U32, name="tab", align_bytes=64)
         nc.sync.dma_start(tab[:].bitcast(I32), tab_words[0].rearrange("p n t -> p (n t)").bitcast(I32))
-        early_words = shared.tile([P, 2 * PASS_ROWS], I32, name="early_words", align_bytes=64, offset=4 * GATE_BYTES)
+        early_words = held.tile([P, 2 * PASS_ROWS], I32, name="early_words", align_bytes=64)
         load_w_words(0, [early_words[:, :PASS_ROWS], early_words[:, PASS_ROWS:]])
 
         def chunk_offsets(c, count=1):
@@ -85,18 +92,23 @@ def tile_list_gmlpt_gelu_gate_kernel(
             for i in range(4):
                 nc.sync.dma_start(plane[i:P:32, :].bitcast(I32), rows[ROWS_FIRST + i : P : 4, :].bitcast(I32))
 
-        nc.vector.tensor_copy(
-            staged[:, EARLY:WD_FIRST].rearrange("p (a t m) -> p a t m", a=2 * R_PASSES, t=PACK),
-            w_rows[:].rearrange("p (a m t) -> p a t m", a=2 * R_PASSES, t=PACK),
-        )
-        x_rows = shared.tile([P, EARLY], U8, name="x_rows", align_bytes=64, offset=GATE_BYTES - CHUNK)
-        nc.vector.tensor_copy(x_rows[:], tab_rows[:].indirect(chunk_offsets(0, 2)))
+        for i, rows in enumerate(w_rows):
+            nc.gpsimd.tensor_copy(
+                staged[:, EARLY + i * R : EARLY + (i + 1) * R].rearrange("p (a t m) -> p a t m", a=R_PASSES, t=PACK),
+                rows[:].rearrange("p (a m t) -> p a t m", a=R_PASSES, t=PACK),
+            )
+        x_rows = shared.tile([P, EARLY], U8, name="x_rows", align_bytes=64, offset=LATE_WORDS_PLACE - CHUNK)
+        nc.vector.tensor_copy(x_rows[:], tab_rows[:].indirect(chunk_offsets(0, CHUNKS - 1)))
         nc.vector.tensor_copy(staged[:, :EARLY].bitcast(I32), x_rows[:].bitcast(I32))
         move_rows(planes[:, :STAGED_BYTES], staged[:])
-        late_words = shared.tile([P, 2 * PASS_ROWS], I32, name="late_words", align_bytes=64, offset=GATE_BYTES)
+        late_words = shared.tile([P, 2 * PASS_ROWS], I32, name="late_words", align_bytes=64, offset=LATE_WORDS_PLACE)
         load_w_words(1, [late_words[:, :PASS_ROWS], late_words[:, PASS_ROWS:]])
-        x_firsts = [0, CHUNK, STAGED_BYTES, STAGED_BYTES + CHUNK]
-        x_planes = [planes[:, first : first + CHUNK] for first in x_firsts]
+        gates = [shared.tile([P, T], F32, name="gate%d" % n, align_bytes=64, offset=GATE_PLACES[n]) for n in range(N_TILES)]
+
+        def load_gates(n):
+            nc.sync.dma_start(gates[n][:], gT[n * P : (n + 1) * P, :])
+
+        load_gates(0)
         w_plane, wd_plane = planes[:, EARLY:WD_FIRST], planes[:, WD_FIRST:STAGED_BYTES]
 
         x_words, dealt = {}, {}
@@ -104,32 +116,27 @@ def tile_list_gmlpt_gelu_gate_kernel(
         def deal_words(a):
             for name in ("wg", "wu"):
                 dealt[name, a] = held.tile([P, PASS_ROWS], I32, name="%s%d" % (name, a), align_bytes=64)
-                nc.vector.tensor_copy(
+                nc.gpsimd.tensor_copy(
                     dealt[name, a][:].rearrange("p (t c i) -> p c t i", t=PACK, i=4),
                     raw[name, a].rearrange("p (c i t) -> p c t i", t=PACK, i=4),
                 )
 
-        def gather_words(c, tag):
-            x_words[c] = held.tile([P, CHUNK], U32, name="x_words%d" % c, tag=tag, align_bytes=64)
+        def gather_words(c):
+            x_words[c] = held.tile([P, CHUNK], U32, name="x_words%d" % c, align_bytes=64)
             nc.vector.tensor_copy(x_words[c][:], tab[:].indirect(chunk_offsets(c)))
 
-        wd = held.tile([P, R_PASSES, 2 * N], U8, name="wd", tag="staged", align_bytes=64)
+        wd = shared.tile([P, R_PASSES, 2 * N], U8, name="wd", align_bytes=64, offset=STAGED_PLACE)
         nc.sync.dma_start(wd[:].bitcast(I32), wd_words.rearrange("a p n -> p a n").bitcast(I32))
-        gather_words(0, "x_words0")
+        load_gates(1)
         deal_words(0)
-        late_rows = shared.tile([P, EARLY], U8, name="late_rows", align_bytes=64, offset=4 * GATE_BYTES)
-        nc.vector.tensor_copy(late_rows[:], tab_rows[:].indirect(chunk_offsets(2, 2)))
         deal_words(1)
-        x_words[1] = shared.tile([P, CHUNK], U32, name="x_words1", align_bytes=64, offset=4 * GATE_BYTES + 4 * CHUNK)
-        nc.vector.tensor_copy(x_words[1][:], tab[:].indirect(chunk_offsets(1)))
-        gates = []
-        for n in range(N_TILES):
-            first = (0, 2 * GATE_BYTES, 3 * GATE_BYTES, GATE_BYTES)[n]
-            gate = shared.tile([P, T], F32, name="gate%d" % n, align_bytes=64, offset=first)
-            nc.sync.dma_start(gate[:], gT[n * P : (n + 1) * P, :])
-            gates.append(gate)
-            if n == 0:
-                move_rows(planes[:, STAGED_BYTES:], late_rows[:])
+        for c in range(CHUNKS):
+            gather_words(c)
+        late_rows = shared.tile([P, CHUNK], U8, name="late_rows", align_bytes=64, offset=LATE_WORDS_PLACE)
+        nc.vector.tensor_copy(late_rows[:], tab_rows[:].indirect(chunk_offsets(CHUNKS - 1)))
+        move_rows(planes[:, STAGED_BYTES:], late_rows[:])
+        x_planes = [planes[:, c * CHUNK : (c + 1) * CHUNK] for c in range(CHUNKS - 1)] + [planes[:, STAGED_BYTES:]]
+        first_ub = shared.tile([P, 2 * CHUNK], F32, name="first_ub", align_bytes=64, offset=GATE_PLACES[3] - 4 * CHUNK)
 
         h_tiles = [held.tile([P, SUBS * CHUNK], BF16, name="h%d" % i, align_bytes=64) for i in range(3)]
 
@@ -139,7 +146,7 @@ def tile_list_gmlpt_gelu_gate_kernel(
         h_codes, h_planes, pair_act, pair_ub, acts, ub_banks, picked, last_banks, ga_banks = {}, {}, {}, {}, {}, {}, {}, {}, {}
 
         def gpsimd_tokens(group, s):
-            share = 2 * SUB if group < R_PASSES else SUB + EXTRA_TOKENS
+            share = SUB if group in (1, 2) else SUB + EXTRA_TOKENS if group else 2 * SUB
             return max(0, min(SUB, share - s * SUB))
 
         def interleaved(ap):
@@ -147,9 +154,9 @@ def tile_list_gmlpt_gelu_gate_kernel(
 
         def first_stage(group):
             c, a = divmod(group, R_PASSES)
-            tag = "x_words3" if group == 0 else "pair_act%d" % (group % 2)
+            tag = "pair_act%d" % (group % 2)
             pair_act[group] = held.tile([P, 2 * CHUNK], F32, name="pair_act%d" % group, tag=tag, align_bytes=64)
-            pair_ub[group] = ring.tile([P, 2 * CHUNK], F32, name="pair_ub", align_bytes=64, bufs=2)
+            pair_ub[group] = first_ub if group == 0 else ring.tile([P, 2 * CHUNK], F32, name="pair_ub", align_bytes=64, bufs=2)
             for s in range(SUBS):
                 cols = slice(s * SUB, (s + 1) * SUB)
                 tokens = gpsimd_tokens(group, s)
@@ -174,8 +181,6 @@ def tile_list_gmlpt_gelu_gate_kernel(
                     acts[group, s] = pair_act[group][:, s * CHUNK : (s + 1) * CHUNK]
                 elif s == SUBS - 1 and group <= R_PASSES:
                     acts[group, s] = h_of(group + 1)[:, : 2 * CHUNK].bitcast(F32)
-                elif (group, s) == (0, 2):
-                    acts[group, s] = held.tile([P, CHUNK], F32, name="first_act", tag="x_words2", align_bytes=64)[:]
                 else:
                     acts[group, s] = held.tile([P, CHUNK], F32, name="act%d_%d" % (group, s), align_bytes=64)[:]
                 nc.scalar.activation(interleaved(acts[group, s]), ga[:].rearrange("p t j -> p j t"), GELU)
@@ -243,8 +248,9 @@ def tile_list_gmlpt_gelu_gate_kernel(
             for i, (unit, y) in enumerate(zip(steps, ys)):
                 down(*unit, y, as_y_bank(ga_banks[group, 2 + i]))
             products_on_gpsimd(group)
-            if group < R_PASSES:
-                gather_words(group + 2, "x_words%d" % (group + 2))
+            if group == 0:
+                load_gates(2)
+                load_gates(3)
             products_on_vector(group)
             if group + 1 < GROUPS:
                 first_stage(group + 1)

@@ -31,10 +31,10 @@ WD_FIRST = EARLY + 2 * R
 STAGED_BYTES = WD_FIRST + R_PASSES * N
 GATE_BYTES = 4 * T
 WORDS_BYTES = 8 * PASS_ROWS
-WD_BYTES = R_PASSES * 2 * N
 LATE_WORDS_PLACE = EARLY
 STAGED_PLACE = LATE_WORDS_PLACE + WORDS_BYTES + GATE_BYTES
-GATE_PLACES = (LATE_WORDS_PLACE + WORDS_BYTES,) + tuple(STAGED_PLACE + WD_BYTES + n * GATE_BYTES for n in range(3))
+GATE_PLACES = (LATE_WORDS_PLACE + WORDS_BYTES,) + tuple(STAGED_PLACE + n * GATE_BYTES for n in range(3))
+HOLD_FIRST = CHUNK + 64
 EXTRA_TOKENS = 32
 ROWS_FIRST = P - 16
 
@@ -85,6 +85,9 @@ def tile_list_gmlpt_gelu_gate_kernel(
         early_words = held.tile([P, 2 * PASS_ROWS], I32, name="early_words", align_bytes=64)
         load_w_words(0, [early_words[:, :PASS_ROWS], early_words[:, PASS_ROWS:]])
 
+        wd = held.tile([P, R_PASSES, 2 * N], U8, name="wd", align_bytes=64)
+        nc.sync.dma_start(wd[:].bitcast(I32), wd_words.rearrange("a p n -> p a n").bitcast(I32))
+
         def chunk_offsets(c, count=1):
             return offsets[:, c * (CHUNK // 16) : (c + count) * (CHUNK // 16)]
 
@@ -125,8 +128,6 @@ def tile_list_gmlpt_gelu_gate_kernel(
             x_words[c] = held.tile([P, CHUNK], U32, name="x_words%d" % c, align_bytes=64)
             nc.vector.tensor_copy(x_words[c][:], tab[:].indirect(chunk_offsets(c)))
 
-        wd = shared.tile([P, R_PASSES, 2 * N], U8, name="wd", align_bytes=64, offset=STAGED_PLACE)
-        nc.sync.dma_start(wd[:].bitcast(I32), wd_words.rearrange("a p n -> p a n").bitcast(I32))
         load_gates(1)
         deal_words(0)
         deal_words(1)
@@ -146,7 +147,7 @@ def tile_list_gmlpt_gelu_gate_kernel(
         h_codes, h_planes, pair_act, pair_ub, acts, ub_banks, picked, last_banks, ga_banks = {}, {}, {}, {}, {}, {}, {}, {}, {}
 
         def gpsimd_tokens(group, s):
-            share = SUB if group in (1, 2) else SUB + EXTRA_TOKENS if group else 2 * SUB
+            share = SUB // 2 if group in (1, 2) else SUB + EXTRA_TOKENS if group else 2 * SUB
             return max(0, min(SUB, share - s * SUB))
 
         def interleaved(ap):
@@ -244,7 +245,7 @@ def tile_list_gmlpt_gelu_gate_kernel(
             steps = [units.pop(0) for i in range(2)] if group > R_PASSES else []
             ys = []
             if steps:
-                ys = [fresh_y(), h_of(group + 1)[:, : 2 * CHUNK].bitcast(F32)]
+                ys = [fresh_y(), h_of(group + 1)[:, HOLD_FIRST : HOLD_FIRST + 2 * CHUNK].bitcast(F32)]
             for i, (unit, y) in enumerate(zip(steps, ys)):
                 down(*unit, y, as_y_bank(ga_banks[group, 2 + i]))
             products_on_gpsimd(group)

@@ -25,7 +25,6 @@ CHUNKS = J // CHUNK
 SUB = 128
 SUBS = CHUNK // SUB
 N_TILES = N // P
-GROUPS = CHUNKS * R_PASSES
 EARLY = J - CHUNK
 WD_FIRST = EARLY + 2 * R
 STAGED_BYTES = WD_FIRST + R_PASSES * N
@@ -34,8 +33,10 @@ WORDS_BYTES = 8 * PASS_ROWS
 LATE_WORDS_PLACE = EARLY
 STAGED_PLACE = LATE_WORDS_PLACE + WORDS_BYTES + GATE_BYTES
 GATE_PLACES = (LATE_WORDS_PLACE + WORDS_BYTES,) + tuple(STAGED_PLACE + n * GATE_BYTES for n in range(3))
-HOLD_FIRST = CHUNK + 64
-EXTRA_TOKENS = 32
+BLOCKS = R_PASSES * SUBS
+GPSIMD_TOKENS = (320, 192, 320, 320)
+PAIR_BLOCKS = 3
+STEPS = (0, 3, 4, 4)
 ROWS_FIRST = P - 16
 
 
@@ -45,7 +46,6 @@ def tile_list_gmlpt_gelu_gate_kernel(
     nc = tc.nc
     with ExitStack() as ctx:
         held = ctx.enter_context(tc.tile_pool(name="held", bufs=1))
-        ring = ctx.enter_context(tc.tile_pool(name="ring", bufs=3))
         shared = ctx.enter_context(tc.tile_pool(name="shared", bufs=1))
         psum = ctx.enter_context(tc.psum_pool(name="psum", bufs=1))
 
@@ -137,33 +137,26 @@ def tile_list_gmlpt_gelu_gate_kernel(
         nc.vector.tensor_copy(late_rows[:], tab_rows[:].indirect(chunk_offsets(CHUNKS - 1)))
         move_rows(planes[:, STAGED_BYTES:], late_rows[:])
         x_planes = [planes[:, c * CHUNK : (c + 1) * CHUNK] for c in range(CHUNKS - 1)] + [planes[:, STAGED_BYTES:]]
-        first_ub = shared.tile([P, 2 * CHUNK], F32, name="first_ub", align_bytes=64, offset=GATE_PLACES[3] - 4 * CHUNK)
+        first_ub = shared.tile([P, PAIR_BLOCKS * CHUNK], F32, name="first_ub", align_bytes=64, offset=GATE_PLACES[3] - 4 * CHUNK)
+        h_tiles = [held.tile([P, BLOCKS * CHUNK], BF16, name="h%d" % i, align_bytes=64) for i in range(2)]
+        h_codes, h_planes, pair_act, pair_ub, acts, ub_banks, ga_banks = {}, {}, {}, {}, {}, {}, {}
 
-        h_tiles = [held.tile([P, SUBS * CHUNK], BF16, name="h%d" % i, align_bytes=64) for i in range(3)]
-
-        def h_of(group):
-            return h_tiles[group % 3]
-
-        h_codes, h_planes, pair_act, pair_ub, acts, ub_banks, picked, last_banks, ga_banks = {}, {}, {}, {}, {}, {}, {}, {}, {}
-
-        def gpsimd_tokens(group, s):
-            share = SUB // 2 if group in (1, 2) else SUB + EXTRA_TOKENS if group else 2 * SUB
-            return max(0, min(SUB, share - s * SUB))
+        def gpsimd_tokens(c, b):
+            return max(0, min(SUB, GPSIMD_TOKENS[c] - b * SUB))
 
         def interleaved(ap):
             return ap.rearrange("p (j t) -> p j t", t=PACK)
 
-        def first_stage(group):
-            c, a = divmod(group, R_PASSES)
-            tag = "pair_act%d" % (group % 2)
-            pair_act[group] = held.tile([P, 2 * CHUNK], F32, name="pair_act%d" % group, tag=tag, align_bytes=64)
-            pair_ub[group] = first_ub if group == 0 else ring.tile([P, 2 * CHUNK], F32, name="pair_ub", align_bytes=64, bufs=2)
-            for s in range(SUBS):
+        def first_stage(c):
+            pair_act[c] = held.tile([P, PAIR_BLOCKS * CHUNK], F32, name="pair_act%d" % (c % 2), align_bytes=64)
+            pair_ub[c] = first_ub if c == 0 else held.tile([P, PAIR_BLOCKS * CHUNK], F32, name="pair_ub", align_bytes=64)
+            for b in range(BLOCKS):
+                a, s = divmod(b, SUBS)
                 cols = slice(s * SUB, (s + 1) * SUB)
-                tokens = gpsimd_tokens(group, s)
+                tokens = gpsimd_tokens(c, b)
                 banks = []
-                for tag, name, first in (("ga", "wg", 0), ("ub" if s < 2 else "ub_held", "wu", R)):
-                    bank = psum.tile([P, PACK, SUB], F32, name=tag, bufs=4 if tag == "ga" else 2)
+                for tag, name, first in (("ga", "wg", 0), ("ub", "wu", R)):
+                    bank = psum.tile([P, PACK, SUB], F32, name=tag, bufs=4)
                     for t in range(PACK):
                         w_cols = slice(first + a * PASS_ROWS + t * P, first + a * PASS_ROWS + (t + 1) * P)
                         nc.tensor.matmul_mx(
@@ -176,106 +169,80 @@ def tile_list_gmlpt_gelu_gate_kernel(
                             stop=True,
                         )
                     banks.append(bank)
-                ga, ub_banks[group, s] = banks
-                ga_banks[group, s] = ga
-                if s < 2:
-                    acts[group, s] = pair_act[group][:, s * CHUNK : (s + 1) * CHUNK]
-                elif s == SUBS - 1 and group <= R_PASSES:
-                    acts[group, s] = h_of(group + 1)[:, : 2 * CHUNK].bitcast(F32)
+                ga_banks[c, b], ub_banks[c, b] = banks
+                if b < PAIR_BLOCKS:
+                    acts[c, b] = pair_act[c][:, b * CHUNK : (b + 1) * CHUNK]
                 else:
-                    acts[group, s] = held.tile([P, CHUNK], F32, name="act%d_%d" % (group, s), align_bytes=64)[:]
-                nc.scalar.activation(interleaved(acts[group, s]), ga[:].rearrange("p t j -> p j t"), GELU)
+                    acts[c, b] = held.tile([P, CHUNK], F32, name="act%d_%d" % (c % 2, b), align_bytes=64)[:]
+                nc.scalar.activation(interleaved(acts[c, b]), ga_banks[c, b][:].rearrange("p t j -> p j t"), GELU)
                 if tokens:
                     nc.scalar.copy(
-                        interleaved(pair_ub[group][:, s * CHUNK : s * CHUNK + tokens * PACK]),
-                        ub_banks[group, s][:, :, :tokens].rearrange("p t j -> p j t"),
+                        interleaved(pair_ub[c][:, b * CHUNK : b * CHUNK + tokens * PACK]),
+                        ub_banks[c, b][:, :, :tokens].rearrange("p t j -> p j t"),
                     )
 
-        def products_on_gpsimd(group):
-            cols = slice(0, PACK * sum(gpsimd_tokens(group, s) for s in range(SUBS)))
-            nc.gpsimd.tensor_tensor(h_of(group)[:, cols], pair_ub[group][:, cols], pair_act[group][:, cols], MULT)
-
-        def products_on_vector(group):
-            for s in [s for s in range(SUBS) if gpsimd_tokens(group, s) < SUB]:
-                done = gpsimd_tokens(group, s)
+        def products(c):
+            h = h_tiles[c % 2]
+            cols = slice(0, PACK * GPSIMD_TOKENS[c])
+            nc.gpsimd.tensor_tensor(h[:, cols], pair_ub[c][:, cols], pair_act[c][:, cols], MULT)
+            for b in [b for b in range(BLOCKS) if gpsimd_tokens(c, b) < SUB]:
+                done = gpsimd_tokens(c, b)
                 nc.vector.tensor_tensor(
-                    interleaved(h_of(group)[:, s * CHUNK + done * PACK : (s + 1) * CHUNK]),
-                    ub_banks[group, s][:, :, done:].rearrange("p t j -> p j t"),
-                    interleaved(acts[group, s][:, done * PACK :]),
+                    interleaved(h[:, b * CHUNK + done * PACK : (b + 1) * CHUNK]),
+                    ub_banks[c, b][:, :, done:].rearrange("p t j -> p j t"),
+                    interleaved(acts[c, b][:, done * PACK :]),
                     MULT,
                 )
 
-        def quantise(group):
-            h_codes[group] = held.tile([P, CHUNK], U32, name="h_codes%d" % group, align_bytes=64)
-            h_planes[group] = held.tile([P, CHUNK], U8, name="h_plane%d" % group, align_bytes=64)
-            nc.vector.quantize_mx(out=h_codes[group][:].bitcast(FP8X4), scales=h_planes[group][:], in_=h_of(group)[:])
-
-        def down_pass(c, n, a, bank):
-            nc.tensor.matmul_mx(
-                out=bank,
-                lhsT=wd[:, a, 2 * n * P : 2 * (n + 1) * P].bitcast(FP4X4),
-                lhsT_scale=wd_plane[:, a * N + n * P : a * N + (n + 1) * P],
-                rhs=h_codes[c * R_PASSES + a][:].bitcast(FP8X4),
-                rhs_scale=h_planes[c * R_PASSES + a][:],
-                start=(a == 0),
-                stop=(a == R_PASSES - 1),
-            )
+        def quantise(c):
+            h_codes[c] = held.tile([P, R_PASSES * CHUNK], U32, name="h_codes%d" % c, align_bytes=64)
+            h_planes[c] = held.tile([P, R_PASSES * CHUNK], U8, name="h_plane%d" % c, align_bytes=64)
+            nc.vector.quantize_mx(out=h_codes[c][:].bitcast(FP8X4), scales=h_planes[c][:], in_=h_tiles[c % 2][:])
 
         def down(c, n, y, bank):
             for a in range(R_PASSES):
-                down_pass(c, n, a, bank)
+                nc.tensor.matmul_mx(
+                    out=bank,
+                    lhsT=wd[:, a, 2 * n * P : 2 * (n + 1) * P].bitcast(FP4X4),
+                    lhsT_scale=wd_plane[:, a * N + n * P : a * N + (n + 1) * P],
+                    rhs=h_codes[c][:, a * CHUNK : (a + 1) * CHUNK].bitcast(FP8X4),
+                    rhs_scale=h_planes[c][:, a * CHUNK : (a + 1) * CHUNK],
+                    start=(a == 0),
+                    stop=(a == R_PASSES - 1),
+                )
             nc.scalar.copy(y, bank)
 
-        def store(c, n, res):
-            nc.sync.dma_start(out[n * P : (n + 1) * P, c * CHUNK : (c + 1) * CHUNK], res)
+        def gate_step(c, n, y, res, first=0, end=CHUNK):
+            entries = offsets[:, (c * CHUNK + first) // 16 : (c * CHUNK + end) // 16]
+            nc.vector.tensor_tensor(res[:, first:end], gates[n][:].indirect(entries), y[:, first:end], MULT)
+            nc.sync.dma_start(out[n * P : (n + 1) * P, c * CHUNK + first : c * CHUNK + end], res[:, first:end])
 
-        def gate_fused(c, n, y, res):
-            nc.vector.tensor_tensor(res, gates[n][:].indirect(chunk_offsets(c)), y, MULT)
-            store(c, n, res)
-
-        def as_y_bank(bank):
-            return bank[:].rearrange("p t j -> p (t j)")
-
-        def fresh_y():
-            return ring.tile([P, CHUNK], F32, name="y", align_bytes=64, bufs=4)[:]
+        def y_place(c, i):
+            first = (i + 2) % N_TILES * 2 * CHUNK
+            return h_tiles[(c + 1) % 2][:, first : first + 2 * CHUNK].bitcast(F32)
 
         units = [(c, n) for c in range(CHUNKS) for n in range(N_TILES)]
         first_stage(0)
-        for group in range(GROUPS):
-            steps = [units.pop(0) for i in range(2)] if group > R_PASSES else []
-            ys = []
-            if steps:
-                ys = [fresh_y(), h_of(group + 1)[:, HOLD_FIRST : HOLD_FIRST + 2 * CHUNK].bitcast(F32)]
-            for i, (unit, y) in enumerate(zip(steps, ys)):
-                down(*unit, y, as_y_bank(ga_banks[group, 2 + i]))
-            products_on_gpsimd(group)
-            if group == 0:
+        for c in range(CHUNKS):
+            last = c + 1 == CHUNKS
+            steps = [(i, units.pop(0)) for i in range(N_TILES - STEPS[c], N_TILES)]
+            for i, unit in steps:
+                down(*unit, y_place(c, i), ga_banks[c, SUBS + i][:].rearrange("p t j -> p (t j)"))
+            products(c)
+            if c == 0:
                 load_gates(2)
                 load_gates(3)
-            products_on_vector(group)
-            if group + 1 < GROUPS:
-                first_stage(group + 1)
+            if last:
+                quantise(c)
             else:
-                late_ys = [fresh_y() for unit in units[:2]]
-                for i, (unit, y) in enumerate(zip(units, late_ys)):
-                    down(*unit, y, as_y_bank(ga_banks[group, i]))
-                for unit, tag in zip(units[2:], ("ub", "ga", "ga", "ga")):
-                    bank = psum.tile([P, CHUNK], F32, name="last_bank", tag=tag, bufs=4 if tag == "ga" else 2)
-                    last_banks[unit] = bank[:]
-                    down_pass(*unit, 0, last_banks[unit])
-            for unit, y, res in zip(steps, ys, (acts[group, 2], acts[group, 3])):
-                gate_fused(*unit, y, res)
-            quantise(group)
-        for unit in units[2:]:
-            down_pass(*unit, 1, last_banks[unit])
-            late_ys.append(ring.tile([P, CHUNK], F32, name="last_y", align_bytes=64, bufs=4)[:])
-            nc.scalar.copy(late_ys[-1], last_banks[unit])
-        for unit, y in zip(units[:-1], late_ys):
-            res = ring.tile([P, CHUNK], F32, name="res", align_bytes=64, bufs=6)
-            gate_fused(*unit, y, res[:])
-        c, n = units[-1]
-        res = ring.tile([P, CHUNK], F32, name="res", align_bytes=64, bufs=6)
-        for first, end in ((0, CHUNK - SUB), (CHUNK - SUB, CHUNK)):
-            entries = offsets[:, (c * CHUNK + first) // 16 : (c * CHUNK + end) // 16]
-            nc.vector.tensor_tensor(res[:, first:end], gates[n][:].indirect(entries), late_ys[-1][:, first:end], MULT)
-            nc.sync.dma_start(out[n * P : (n + 1) * P, c * CHUNK + first : c * CHUNK + end], res[:, first:end])
+                first_stage(c + 1)
+            for i, unit in steps:
+                gate_step(*unit, y_place(c, i), acts[c, SUBS + i])
+            if not last:
+                quantise(c)
+        for i, unit in enumerate(units):
+            y = held.tile([P, CHUNK], F32, name="last_y%d" % i, align_bytes=64)
+            down(*unit, y[:], psum.tile([P, CHUNK], F32, name="last_bank", tag="ub", bufs=4)[:])
+            res = held.tile([P, CHUNK], F32, name="last_res%d" % i, align_bytes=64)
+            for first, end in ((0, CHUNK),) if i + 1 < len(units) else ((0, CHUNK - SUB), (CHUNK - SUB, CHUNK)):
+                gate_step(*unit, y[:], res[:], first, end)

@@ -34,7 +34,7 @@ LATE_WORDS_PLACE = EARLY
 STAGED_PLACE = LATE_WORDS_PLACE + WORDS_BYTES + GATE_BYTES
 GATE_PLACES = (LATE_WORDS_PLACE + WORDS_BYTES,) + tuple(STAGED_PLACE + n * GATE_BYTES for n in range(3))
 BLOCKS = R_PASSES * SUBS
-GPSIMD_TOKENS = (320, 192, 320, 320)
+GPSIMD_TOKENS = (320, 128, 336, 336)
 PAIR_BLOCKS = 3
 STEPS = (0, 3, 4, 4)
 ROWS_FIRST = P - 16

@@ -29,13 +29,13 @@ EARLY = J - CHUNK
 WD_FIRST = EARLY + 2 * R
 STAGED_BYTES = WD_FIRST + R_PASSES * N
 GATE_BYTES = 4 * T
-WORDS_BYTES = 8 * PASS_ROWS
-LATE_WORDS_PLACE = EARLY
-STAGED_PLACE = LATE_WORDS_PLACE + WORDS_BYTES + GATE_BYTES
-GATE_PLACES = (LATE_WORDS_PLACE + WORDS_BYTES,) + tuple(STAGED_PLACE + n * GATE_BYTES for n in range(3))
+WD_BYTES = R_PASSES * 2 * N
+STAGED_PLACE = GATE_BYTES
+GATE_PLACES = (0,) + tuple(STAGED_PLACE + WD_BYTES + n * GATE_BYTES for n in range(3))
 BLOCKS = R_PASSES * SUBS
-GPSIMD_TOKENS = (320, 128, 336, 336)
-PAIR_BLOCKS = 3
+GPSIMD_TOKENS = (256, 128, 256, 256)
+PAIR_BLOCKS = 2
+RUNS = 4
 STEPS = (0, 3, 4, 4)
 ROWS_FIRST = P - 16
 
@@ -55,23 +55,13 @@ def tile_list_gmlpt_gelu_gate_kernel(
         tab_rows = held.tile([P, T], U8, name="tab_rows", align_bytes=64)
         nc.vector.memset(tab_rows[:ROWS_FIRST, :].bitcast(I32), 0)
         wg_rows = held.tile([P, R], U8, name="wg_rows", align_bytes=64)
-        wu_rows = shared.tile([P, R], U8, name="wu_rows", align_bytes=64, offset=GATE_PLACES[0] - CHUNK)
+        wu_rows = shared.tile([P, R], U8, name="wu_rows", align_bytes=64, offset=GATE_PLACES[0])
         w_rows = (wg_rows, wu_rows)
         for rows in w_rows:
             nc.gpsimd.memset(rows[:ROWS_FIRST, :].bitcast(I32), 0)
         planes = held.tile([P, STAGED_BYTES + CHUNK], U8, name="planes", align_bytes=64)
         nc.gpsimd.memset(planes[:].bitcast(I32), 0)
         staged = shared.tile([P, STAGED_BYTES], U8, name="staged", align_bytes=64, offset=STAGED_PLACE)
-
-        raw = {}
-
-        def load_w_words(a, both):
-            for i, (name, words) in enumerate((("wg", wg_words), ("wu", wu_words))):
-                raw[name, a] = both[i]
-                nc.sync.dma_start(
-                    raw[name, a],
-                    words[0, :, a * PASS_ROWS : (a + 1) * PASS_ROWS, :].rearrange("p n t -> p (n t)").bitcast(I32),
-                )
 
         nc.sync.dma_start(tab_rows[ROWS_FIRST:, :].bitcast(I32), tab_scales[0].bitcast(I32))
         for i, scales in enumerate((wg_scales, wu_scales)):
@@ -82,11 +72,10 @@ def tile_list_gmlpt_gelu_gate_kernel(
         )
         tab = held.tile([P, T], U32, name="tab", align_bytes=64)
         nc.sync.dma_start(tab[:].bitcast(I32), tab_words[0].rearrange("p n t -> p (n t)").bitcast(I32))
-        early_words = held.tile([P, 2 * PASS_ROWS], I32, name="early_words", align_bytes=64)
-        load_w_words(0, [early_words[:, :PASS_ROWS], early_words[:, PASS_ROWS:]])
-
-        wd = held.tile([P, R_PASSES, 2 * N], U8, name="wd", align_bytes=64)
-        nc.sync.dma_start(wd[:].bitcast(I32), wd_words.rearrange("a p n -> p a n").bitcast(I32))
+        raw = {}
+        for name, words in (("wg", wg_words), ("wu", wu_words)):
+            raw[name] = held.tile([P, R], I32, name="raw_%s" % name, align_bytes=64)
+            nc.sync.dma_start(raw[name][:], words[0].rearrange("p n t -> p (n t)").bitcast(I32))
 
         def chunk_offsets(c, count=1):
             return offsets[:, c * (CHUNK // 16) : (c + count) * (CHUNK // 16)]
@@ -100,12 +89,10 @@ def tile_list_gmlpt_gelu_gate_kernel(
                 staged[:, EARLY + i * R : EARLY + (i + 1) * R].rearrange("p (a t m) -> p a t m", a=R_PASSES, t=PACK),
                 rows[:].rearrange("p (a m t) -> p a t m", a=R_PASSES, t=PACK),
             )
-        x_rows = shared.tile([P, EARLY], U8, name="x_rows", align_bytes=64, offset=LATE_WORDS_PLACE - CHUNK)
+        x_rows = shared.tile([P, EARLY], U8, name="x_rows", align_bytes=64, offset=GATE_PLACES[0] + R)
         nc.vector.tensor_copy(x_rows[:], tab_rows[:].indirect(chunk_offsets(0, CHUNKS - 1)))
         nc.vector.tensor_copy(staged[:, :EARLY].bitcast(I32), x_rows[:].bitcast(I32))
         move_rows(planes[:, :STAGED_BYTES], staged[:])
-        late_words = shared.tile([P, 2 * PASS_ROWS], I32, name="late_words", align_bytes=64, offset=LATE_WORDS_PLACE)
-        load_w_words(1, [late_words[:, :PASS_ROWS], late_words[:, PASS_ROWS:]])
         gates = [shared.tile([P, T], F32, name="gate%d" % n, align_bytes=64, offset=GATE_PLACES[n]) for n in range(N_TILES)]
 
         def load_gates(n):
@@ -121,7 +108,7 @@ def tile_list_gmlpt_gelu_gate_kernel(
                 dealt[name, a] = held.tile([P, PASS_ROWS], I32, name="%s%d" % (name, a), align_bytes=64)
                 nc.gpsimd.tensor_copy(
                     dealt[name, a][:].rearrange("p (t c i) -> p c t i", t=PACK, i=4),
-                    raw[name, a].rearrange("p (c i t) -> p c t i", t=PACK, i=4),
+                    raw[name][:, a * PASS_ROWS : (a + 1) * PASS_ROWS].rearrange("p (c i t) -> p c t i", t=PACK, i=4),
                 )
 
         def gather_words(c):
@@ -129,11 +116,13 @@ def tile_list_gmlpt_gelu_gate_kernel(
             nc.vector.tensor_copy(x_words[c][:], tab[:].indirect(chunk_offsets(c)))
 
         load_gates(1)
+        wd = shared.tile([P, R_PASSES, 2 * N], U8, name="wd", align_bytes=64, offset=STAGED_PLACE)
+        nc.sync.dma_start(wd[:].bitcast(I32), wd_words.rearrange("a p n -> p a n").bitcast(I32))
         deal_words(0)
         deal_words(1)
         for c in range(CHUNKS):
             gather_words(c)
-        late_rows = shared.tile([P, CHUNK], U8, name="late_rows", align_bytes=64, offset=LATE_WORDS_PLACE)
+        late_rows = held.tile([P, CHUNK], U8, name="late_rows", tag="raw_wu", align_bytes=64)
         nc.vector.tensor_copy(late_rows[:], tab_rows[:].indirect(chunk_offsets(CHUNKS - 1)))
         move_rows(planes[:, STAGED_BYTES:], late_rows[:])
         x_planes = [planes[:, c * CHUNK : (c + 1) * CHUNK] for c in range(CHUNKS - 1)] + [planes[:, STAGED_BYTES:]]
@@ -182,15 +171,15 @@ def tile_list_gmlpt_gelu_gate_kernel(
                     )
 
         def products(c):
-            h = h_tiles[c % 2]
-            cols = slice(0, PACK * GPSIMD_TOKENS[c])
-            nc.gpsimd.tensor_tensor(h[:, cols], pair_ub[c][:, cols], pair_act[c][:, cols], MULT)
-            for b in [b for b in range(BLOCKS) if gpsimd_tokens(c, b) < SUB]:
-                done = gpsimd_tokens(c, b)
+            h = h_tiles[c % 2][:].rearrange("p (a k s w) -> p a s k w", a=R_PASSES, k=RUNS, s=SUBS)
+            blocks = GPSIMD_TOKENS[c] // SUB
+            ub, act = [t[:, : blocks * CHUNK].rearrange("p (s k w) -> p s k w", s=blocks, k=RUNS) for t in (pair_ub[c], pair_act[c])]
+            nc.gpsimd.tensor_tensor(h[:, 0, :blocks], ub, act, MULT)
+            for b in range(blocks, BLOCKS):
                 nc.vector.tensor_tensor(
-                    interleaved(h[:, b * CHUNK + done * PACK : (b + 1) * CHUNK]),
-                    ub_banks[c, b][:, :, done:].rearrange("p t j -> p j t"),
-                    interleaved(acts[c, b][:, done * PACK :]),
+                    h[:, b // SUBS, b % SUBS].rearrange("p k (j t) -> p k j t", t=PACK),
+                    ub_banks[c, b][:].rearrange("p t (k j) -> p k j t", k=RUNS),
+                    acts[c, b].rearrange("p (k j t) -> p k j t", k=RUNS, t=PACK),
                     MULT,
                 )
 
@@ -210,18 +199,25 @@ def tile_list_gmlpt_gelu_gate_kernel(
                     start=(a == 0),
                     stop=(a == R_PASSES - 1),
                 )
-            nc.scalar.copy(y, bank)
+            nc.scalar.copy(
+                y.rearrange("p (s k j) -> p s k j", s=SUBS, k=RUNS), bank.rearrange("p (k s j) -> p s k j", s=SUBS, k=RUNS)
+            )
 
         def gate_step(c, n, y, res, first=0, end=CHUNK):
             entries = offsets[:, (c * CHUNK + first) // 16 : (c * CHUNK + end) // 16]
             nc.vector.tensor_tensor(res[:, first:end], gates[n][:].indirect(entries), y[:, first:end], MULT)
             nc.sync.dma_start(out[n * P : (n + 1) * P, c * CHUNK + first : c * CHUNK + end], res[:, first:end])
 
+        first_y = held.tile([P, CHUNK], F32, name="first_y", align_bytes=64)
+
         def y_place(c, i):
-            first = (i + 2) % N_TILES * 2 * CHUNK
+            if i == 0:
+                return first_y[:]
+            first = (5, 1, 3)[i - 1] * CHUNK
             return h_tiles[(c + 1) % 2][:, first : first + 2 * CHUNK].bitcast(F32)
 
         units = [(c, n) for c in range(CHUNKS) for n in range(N_TILES)]
+        units.insert(2 * N_TILES - 2, units.pop(N_TILES - 1))
         first_stage(0)
         for c in range(CHUNKS):
             last = c + 1 == CHUNKS

@@ -33,9 +33,10 @@ WD_BYTES = R_PASSES * 2 * N
 STAGED_PLACE = GATE_BYTES
 GATE_PLACES = (0,) + tuple(STAGED_PLACE + WD_BYTES + n * GATE_BYTES for n in range(3))
 BLOCKS = R_PASSES * SUBS
-GPSIMD_TOKENS = (256, 128, 256, 256)
-PAIR_BLOCKS = 2
 RUNS = 4
+RUN = SUB // RUNS
+GPSIMD_TOKENS = (64, 32, 80, 80)
+PAIR_BLOCKS = 3
 STEPS = (0, 3, 4, 4)
 ROWS_FIRST = P - 16
 
@@ -128,13 +129,16 @@ def tile_list_gmlpt_gelu_gate_kernel(
         x_planes = [planes[:, c * CHUNK : (c + 1) * CHUNK] for c in range(CHUNKS - 1)] + [planes[:, STAGED_BYTES:]]
         first_ub = shared.tile([P, PAIR_BLOCKS * CHUNK], F32, name="first_ub", align_bytes=64, offset=GATE_PLACES[3] - 4 * CHUNK)
         h_tiles = [held.tile([P, BLOCKS * CHUNK], BF16, name="h%d" % i, align_bytes=64) for i in range(2)]
-        h_codes, h_planes, pair_act, pair_ub, acts, ub_banks, ga_banks = {}, {}, {}, {}, {}, {}, {}
+        h_codes, h_planes, pair_act, pair_ub, acts, ub_banks, ga_banks, act_runs = {}, {}, {}, {}, {}, {}, {}, {}
 
         def gpsimd_tokens(c, b):
-            return max(0, min(SUB, GPSIMD_TOKENS[c] - b * SUB))
+            return max(0, min(RUN, GPSIMD_TOKENS[c] - b * RUN))
 
-        def interleaved(ap):
-            return ap.rearrange("p (j t) -> p j t", t=PACK)
+        def in_runs(ap):
+            return ap.rearrange("p (k j t) -> p k j t", k=RUNS, t=PACK)
+
+        def bank_in_runs(bank):
+            return bank[:].rearrange("p t (k j) -> p k j t", k=RUNS)
 
         def first_stage(c):
             pair_act[c] = held.tile([P, PAIR_BLOCKS * CHUNK], F32, name="pair_act%d" % (c % 2), align_bytes=64)
@@ -160,26 +164,28 @@ def tile_list_gmlpt_gelu_gate_kernel(
                     banks.append(bank)
                 ga_banks[c, b], ub_banks[c, b] = banks
                 if b < PAIR_BLOCKS:
-                    acts[c, b] = pair_act[c][:, b * CHUNK : (b + 1) * CHUNK]
+                    act_runs[c, b] = in_runs(pair_act[c][:])[:, :, b * RUN : (b + 1) * RUN]
                 else:
                     acts[c, b] = held.tile([P, CHUNK], F32, name="act%d_%d" % (c % 2, b), align_bytes=64)[:]
-                nc.scalar.activation(interleaved(acts[c, b]), ga_banks[c, b][:].rearrange("p t j -> p j t"), GELU)
+                    act_runs[c, b] = in_runs(acts[c, b])
+                nc.scalar.activation(act_runs[c, b], bank_in_runs(ga_banks[c, b]), GELU)
                 if tokens:
                     nc.scalar.copy(
-                        interleaved(pair_ub[c][:, b * CHUNK : b * CHUNK + tokens * PACK]),
-                        ub_banks[c, b][:, :, :tokens].rearrange("p t j -> p j t"),
+                        in_runs(pair_ub[c][:])[:, :, b * RUN : b * RUN + tokens], bank_in_runs(ub_banks[c, b])[:, :, :tokens]
                     )
 
         def products(c):
-            h = h_tiles[c % 2][:].rearrange("p (a k s w) -> p a s k w", a=R_PASSES, k=RUNS, s=SUBS)
-            blocks = GPSIMD_TOKENS[c] // SUB
-            ub, act = [t[:, : blocks * CHUNK].rearrange("p (s k w) -> p s k w", s=blocks, k=RUNS) for t in (pair_ub[c], pair_act[c])]
-            nc.gpsimd.tensor_tensor(h[:, 0, :blocks], ub, act, MULT)
-            for b in range(blocks, BLOCKS):
+            h = [in_runs(h_tiles[c % 2][:, a * SUBS * CHUNK : (a + 1) * SUBS * CHUNK]) for a in range(R_PASSES)]
+            tokens = GPSIMD_TOKENS[c]
+            ub, act = in_runs(pair_ub[c][:]), in_runs(pair_act[c][:])
+            nc.gpsimd.tensor_tensor(h[0][:, :, :tokens], ub[:, :, :tokens], act[:, :, :tokens], MULT)
+            for b in [b for b in range(BLOCKS) if gpsimd_tokens(c, b) < RUN]:
+                a, s = divmod(b, SUBS)
+                done = gpsimd_tokens(c, b)
                 nc.vector.tensor_tensor(
-                    h[:, b // SUBS, b % SUBS].rearrange("p k (j t) -> p k j t", t=PACK),
-                    ub_banks[c, b][:].rearrange("p t (k j) -> p k j t", k=RUNS),
-                    acts[c, b].rearrange("p (k j t) -> p k j t", k=RUNS, t=PACK),
+                    h[a][:, :, s * RUN + done : (s + 1) * RUN],
+                    bank_in_runs(ub_banks[c, b])[:, :, done:],
+                    act_runs[c, b][:, :, done:],
                     MULT,
                 )
 

@@ -24,21 +24,29 @@ CHUNK = 512
 CHUNKS = J // CHUNK
 SUB = 128
 SUBS = CHUNK // SUB
-N_TILES = N // P
-EARLY = J - CHUNK
-WD_FIRST = EARLY + 2 * R
-STAGED_BYTES = WD_FIRST + R_PASSES * N
-GATE_BYTES = 4 * T
-WD_BYTES = R_PASSES * 2 * N
-STAGED_PLACE = GATE_BYTES
-GATE_PLACES = (0,) + tuple(STAGED_PLACE + WD_BYTES + n * GATE_BYTES for n in range(3))
 BLOCKS = R_PASSES * SUBS
+BLOCK = SUB * PACK
+N_TILES = N // P
+ROWS_FIRST = P - 16
+KB = 1024
+EARLY_BYTES = CHUNK + 2 * PASS_ROWS
+LATE_X = J - CHUNK
+LATE_WD = LATE_X + 2 * PASS_ROWS
+LATE_BYTES = LATE_WD + R_PASSES * N
+GATE_BYTES = 4 * T
+WD_PLACE = 0
+GATE_PLACES = tuple(2 * KB + n * GATE_BYTES for n in range(N_TILES))
+LATE_X_PLACE = GATE_PLACES[0] - LATE_X // 2
+LATE_PLACE = GATE_PLACES[3] - 2 * KB
+RAW_U0_PLACE = GATE_PLACES[3] + GATE_BYTES
+RAW_1_PLACE = RAW_U0_PLACE + 2 * KB
+W_ROWS_PLACE = RAW_1_PLACE - KB
 RUNS = 4
 RUN = SUB // RUNS
-GPSIMD_TOKENS = (64, 32, 80, 80)
+GPSIMD_TOKENS = (32, 48, 80, 80)
 PAIR_BLOCKS = 3
-STEPS = (0, 3, 4, 4)
-ROWS_FIRST = P - 16
+RING = 4
+RES_BLOCKS = (6, 7, 5, 4)
 
 
 def tile_list_gmlpt_gelu_gate_kernel(
@@ -50,201 +58,264 @@ def tile_list_gmlpt_gelu_gate_kernel(
         shared = ctx.enter_context(tc.tile_pool(name="shared", bufs=1))
         psum = ctx.enter_context(tc.psum_pool(name="psum", bufs=1))
 
+        def own(shape, dtype, name):
+            return held.tile(shape, dtype, name=name, align_bytes=64)
+
+        def placed(shape, dtype, name, offset):
+            return shared.tile(shape, dtype, name=name, align_bytes=64, offset=offset)
+
         offsets = held.tile([P, J // 16], U16, name="offsets")
         nc.sync.dma_start(offsets[:], offs)
 
-        tab_rows = held.tile([P, T], U8, name="tab_rows", align_bytes=64)
+        tab_rows = own([P, T], U8, "tab_rows")
         nc.vector.memset(tab_rows[:ROWS_FIRST, :].bitcast(I32), 0)
-        wg_rows = held.tile([P, R], U8, name="wg_rows", align_bytes=64)
-        wu_rows = shared.tile([P, R], U8, name="wu_rows", align_bytes=64, offset=GATE_PLACES[0])
-        w_rows = (wg_rows, wu_rows)
-        for rows in w_rows:
-            nc.gpsimd.memset(rows[:ROWS_FIRST, :].bitcast(I32), 0)
-        planes = held.tile([P, STAGED_BYTES + CHUNK], U8, name="planes", align_bytes=64)
-        nc.gpsimd.memset(planes[:].bitcast(I32), 0)
-        staged = shared.tile([P, STAGED_BYTES], U8, name="staged", align_bytes=64, offset=STAGED_PLACE)
+        w_rows = placed([P, 2 * R], U8, "w_rows", W_ROWS_PLACE)
+        nc.gpsimd.memset(w_rows[:ROWS_FIRST, :].bitcast(I32), 0)
+        early_planes = own([P, EARLY_BYTES], U8, "early_planes")
+        late_planes = own([P, LATE_BYTES], U8, "late_planes")
+        nc.gpsimd.memset(early_planes[:].bitcast(I32), 0)
+        nc.gpsimd.memset(late_planes[:].bitcast(I32), 0)
+        early = own([P, EARLY_BYTES], U8, "early")
+        late = placed([P, LATE_BYTES], U8, "late", LATE_PLACE)
 
         nc.sync.dma_start(tab_rows[ROWS_FIRST:, :].bitcast(I32), tab_scales[0].bitcast(I32))
         for i, scales in enumerate((wg_scales, wu_scales)):
-            nc.sync.dma_start(w_rows[i][ROWS_FIRST:, :].bitcast(I32), scales[0].bitcast(I32))
+            nc.sync.dma_start(w_rows[ROWS_FIRST:, i * R : (i + 1) * R].bitcast(I32), scales[0].bitcast(I32))
         nc.sync.dma_start(
-            staged[ROWS_FIRST:, WD_FIRST:].bitcast(I32).rearrange("p (a n) -> p a n", a=R_PASSES),
+            late[ROWS_FIRST:, LATE_WD:].bitcast(I32).rearrange("p (a n) -> p a n", a=R_PASSES),
             wd_scales.rearrange("a r n -> r a n").bitcast(I32),
         )
-        tab = held.tile([P, T], U32, name="tab", align_bytes=64)
-        nc.sync.dma_start(tab[:].bitcast(I32), tab_words[0].rearrange("p n t -> p (n t)").bitcast(I32))
-        raw = {}
-        for name, words in (("wg", wg_words), ("wu", wu_words)):
-            raw[name] = held.tile([P, R], I32, name="raw_%s" % name, align_bytes=64)
-            nc.sync.dma_start(raw[name][:], words[0].rearrange("p n t -> p (n t)").bitcast(I32))
 
-        def chunk_offsets(c, count=1):
-            return offsets[:, c * (CHUNK // 16) : (c + count) * (CHUNK // 16)]
+        def words_of(words, a):
+            return words[0].rearrange("p n t -> p (n t)").bitcast(I32)[:, a * PASS_ROWS : (a + 1) * PASS_ROWS]
+
+        raw_g0 = own([P, PASS_ROWS], I32, "raw_g0")
+        nc.sync.dma_start(raw_g0[:], words_of(wg_words, 0))
+        tab = placed([P, T], U32, "tab", GATE_PLACES[1])
+        nc.sync.dma_start(tab[:].bitcast(I32), tab_words[0].rearrange("p n t -> p (n t)").bitcast(I32))
+
+        def entries(first, end):
+            return offsets[:, first // 16 : end // 16]
 
         def move_rows(plane, rows):
             for i in range(4):
                 nc.sync.dma_start(plane[i:P:32, :].bitcast(I32), rows[ROWS_FIRST + i : P : 4, :].bitcast(I32))
 
-        for i, rows in enumerate(w_rows):
+        def deal_scales(to, a):
             nc.gpsimd.tensor_copy(
-                staged[:, EARLY + i * R : EARLY + (i + 1) * R].rearrange("p (a t m) -> p a t m", a=R_PASSES, t=PACK),
-                rows[:].rearrange("p (a m t) -> p a t m", a=R_PASSES, t=PACK),
+                to.rearrange("p (w t m) -> p w t m", w=2, t=PACK),
+                w_rows[:].rearrange("p (w a m t) -> p a w t m", w=2, a=R_PASSES, t=PACK)[:, a],
             )
-        x_rows = shared.tile([P, EARLY], U8, name="x_rows", align_bytes=64, offset=GATE_PLACES[0] + R)
-        nc.vector.tensor_copy(x_rows[:], tab_rows[:].indirect(chunk_offsets(0, CHUNKS - 1)))
-        nc.vector.tensor_copy(staged[:, :EARLY].bitcast(I32), x_rows[:].bitcast(I32))
-        move_rows(planes[:, :STAGED_BYTES], staged[:])
-        gates = [shared.tile([P, T], F32, name="gate%d" % n, align_bytes=64, offset=GATE_PLACES[n]) for n in range(N_TILES)]
+
+        dealt = {}
+
+        def deal_words(name, a, raw):
+            dealt[name, a] = own([P, PASS_ROWS], I32, "%s%d" % (name, a))
+            nc.gpsimd.tensor_copy(
+                dealt[name, a][:].rearrange("p (t c i) -> p c t i", t=PACK, i=4),
+                raw.rearrange("p (c i t) -> p c t i", t=PACK, i=4),
+            )
+
+        early_x = own([P, CHUNK], U8, "early_x")
+        nc.vector.tensor_copy(early_x[:], tab_rows[:].indirect(entries(0, CHUNK)))
+        nc.vector.tensor_copy(early[:, :CHUNK].bitcast(I32), early_x[:].bitcast(I32))
+        deal_scales(early[:, CHUNK:], 0)
+        move_rows(early_planes, early)
+        deal_scales(late[:, LATE_X:LATE_WD], 1)
+        deal_words("wg", 0, raw_g0[:])
+        raw_u0 = placed([P, PASS_ROWS], I32, "raw_u0", RAW_U0_PLACE)
+        nc.sync.dma_start(raw_u0[:], words_of(wu_words, 0))
+        raw_1 = placed([P, 2, PASS_ROWS], I32, "raw_1", RAW_1_PLACE)
+        nc.sync.dma_start(raw_1[:, 0, :], words_of(wg_words, 1))
+        nc.sync.dma_start(raw_1[:, 1, :], words_of(wu_words, 1))
+        late_x = placed([P, LATE_X], U8, "late_x", LATE_X_PLACE)
+        nc.vector.tensor_copy(late_x[:, :CHUNK], tab_rows[:].indirect(entries(CHUNK, 2 * CHUNK)))
+        nc.vector.tensor_copy(late_x[:, CHUNK:], tab_rows[:].indirect(entries(2 * CHUNK, J)))
+        nc.vector.tensor_copy(late[:, :LATE_X].bitcast(I32), late_x[:].bitcast(I32))
+        move_rows(late_planes, late)
+        wd = placed([P, R_PASSES, 2 * N], U8, "wd", WD_PLACE)
+        nc.sync.dma_start(wd[:].bitcast(I32), wd_words.rearrange("a p n -> p a n").bitcast(I32))
+        gates = [placed([P, T], F32, "gate%d" % n, GATE_PLACES[n]) for n in range(N_TILES)]
 
         def load_gates(n):
             nc.sync.dma_start(gates[n][:], gT[n * P : (n + 1) * P, :])
 
         load_gates(0)
-        w_plane, wd_plane = planes[:, EARLY:WD_FIRST], planes[:, WD_FIRST:STAGED_BYTES]
+        deal_words("wu", 0, raw_u0[:])
+        deal_words("wg", 1, raw_1[:, 0, :])
+        deal_words("wu", 1, raw_1[:, 1, :])
 
-        x_words, dealt = {}, {}
+        x_words = {}
+        for first, end in ((0, 2 * SUB), (2 * SUB, CHUNK)) + tuple((c * CHUNK, (c + 1) * CHUNK) for c in range(1, CHUNKS)):
+            words = own([P, end - first], U32, "x_words%d" % first)
+            nc.vector.tensor_copy(words[:], tab[:].indirect(entries(first, end)))
+            for j in range(first, end, SUB):
+                x_words[j // SUB] = words[:, j - first : j - first + SUB]
+        for n in range(1, N_TILES):
+            load_gates(n)
 
-        def deal_words(a):
-            for name in ("wg", "wu"):
-                dealt[name, a] = held.tile([P, PASS_ROWS], I32, name="%s%d" % (name, a), align_bytes=64)
-                nc.gpsimd.tensor_copy(
-                    dealt[name, a][:].rearrange("p (t c i) -> p c t i", t=PACK, i=4),
-                    raw[name][:, a * PASS_ROWS : (a + 1) * PASS_ROWS].rearrange("p (c i t) -> p c t i", t=PACK, i=4),
-                )
+        def x_plane(c, s):
+            plane, first = (early_planes, 0) if c == 0 else (late_planes, (c - 1) * CHUNK)
+            return plane[:, first + s * SUB : first + (s + 1) * SUB]
 
-        def gather_words(c):
-            x_words[c] = held.tile([P, CHUNK], U32, name="x_words%d" % c, align_bytes=64)
-            nc.vector.tensor_copy(x_words[c][:], tab[:].indirect(chunk_offsets(c)))
+        def w_plane(name, a, t):
+            plane, first = (early_planes, CHUNK) if a == 0 else (late_planes, LATE_X)
+            first = first + (PASS_ROWS if name == "wu" else 0) + t * P
+            return plane[:, first : first + P]
 
-        load_gates(1)
-        wd = shared.tile([P, R_PASSES, 2 * N], U8, name="wd", align_bytes=64, offset=STAGED_PLACE)
-        nc.sync.dma_start(wd[:].bitcast(I32), wd_words.rearrange("a p n -> p a n").bitcast(I32))
-        deal_words(0)
-        deal_words(1)
-        for c in range(CHUNKS):
-            gather_words(c)
-        late_rows = held.tile([P, CHUNK], U8, name="late_rows", tag="raw_wu", align_bytes=64)
-        nc.vector.tensor_copy(late_rows[:], tab_rows[:].indirect(chunk_offsets(CHUNKS - 1)))
-        move_rows(planes[:, STAGED_BYTES:], late_rows[:])
-        x_planes = [planes[:, c * CHUNK : (c + 1) * CHUNK] for c in range(CHUNKS - 1)] + [planes[:, STAGED_BYTES:]]
-        first_ub = shared.tile([P, PAIR_BLOCKS * CHUNK], F32, name="first_ub", align_bytes=64, offset=GATE_PLACES[3] - 4 * CHUNK)
-        h_tiles = [held.tile([P, BLOCKS * CHUNK], BF16, name="h%d" % i, align_bytes=64) for i in range(2)]
-        h_codes, h_planes, pair_act, pair_ub, acts, ub_banks, ga_banks, act_runs = {}, {}, {}, {}, {}, {}, {}, {}
+        scalar_banks = [psum.tile([P, BLOCK], F32, name="scalar_bank%d" % i) for i in range(RING)]
+        vector_banks = [psum.tile([P, BLOCK], F32, name="vector_bank%d" % i) for i in range(RING)]
+        act_tiles = {(i, b): own([P, BLOCK], F32, "act%d_%d" % (i, b)) for i in range(2) for b in range(1 + i, BLOCKS)}
+        y_ring = [own([P, CHUNK], F32, "y%d" % i) for i in range(RING)]
+        pair_act = [own([P, PAIR_BLOCKS * BLOCK], F32, "pair_act%d" % i) for i in range(2)]
+        pair_ub = [own([P, PAIR_BLOCKS * BLOCK], F32, "pair_ub%d" % i) for i in range(2)]
+        h_tiles = [own([P, BLOCKS * BLOCK], BF16, "h%d" % i) for i in range(2)]
+        h_codes = [own([P, R_PASSES * CHUNK], U32, "h_codes%d" % c) for c in range(CHUNKS)]
+        h_planes = [own([P, R_PASSES * CHUNK], U8, "h_plane%d" % c) for c in range(CHUNKS)]
 
-        def gpsimd_tokens(c, b):
-            return max(0, min(RUN, GPSIMD_TOKENS[c] - b * RUN))
+        def turn(ring):
+            ring.append(ring.pop(0))
+            return ring[-1]
 
         def in_runs(ap):
             return ap.rearrange("p (k j t) -> p k j t", k=RUNS, t=PACK)
 
         def bank_in_runs(bank):
-            return bank[:].rearrange("p t (k j) -> p k j t", k=RUNS)
+            return bank[:].rearrange("p (t k j) -> p k j t", t=PACK, k=RUNS)
 
-        def first_stage(c):
-            pair_act[c] = held.tile([P, PAIR_BLOCKS * CHUNK], F32, name="pair_act%d" % (c % 2), align_bytes=64)
-            pair_ub[c] = first_ub if c == 0 else held.tile([P, PAIR_BLOCKS * CHUNK], F32, name="pair_ub", align_bytes=64)
-            for b in range(BLOCKS):
-                a, s = divmod(b, SUBS)
-                cols = slice(s * SUB, (s + 1) * SUB)
-                tokens = gpsimd_tokens(c, b)
-                banks = []
-                for tag, name, first in (("ga", "wg", 0), ("ub", "wu", R)):
-                    bank = psum.tile([P, PACK, SUB], F32, name=tag, bufs=4)
-                    for t in range(PACK):
-                        w_cols = slice(first + a * PASS_ROWS + t * P, first + a * PASS_ROWS + (t + 1) * P)
-                        nc.tensor.matmul_mx(
-                            out=bank[:, t, :],
-                            lhsT=dealt[name, a][:, t * P : (t + 1) * P].bitcast(FP8X4),
-                            lhsT_scale=w_plane[:, w_cols],
-                            rhs=x_words[c][:, cols].bitcast(FP8X4),
-                            rhs_scale=x_planes[c][:, cols],
-                            start=True,
-                            stop=True,
-                        )
-                    banks.append(bank)
-                ga_banks[c, b], ub_banks[c, b] = banks
-                if b < PAIR_BLOCKS:
-                    act_runs[c, b] = in_runs(pair_act[c][:])[:, :, b * RUN : (b + 1) * RUN]
-                else:
-                    acts[c, b] = held.tile([P, CHUNK], F32, name="act%d_%d" % (c % 2, b), align_bytes=64)[:]
-                    act_runs[c, b] = in_runs(acts[c, b])
-                nc.scalar.activation(act_runs[c, b], bank_in_runs(ga_banks[c, b]), GELU)
-                if tokens:
-                    nc.scalar.copy(
-                        in_runs(pair_ub[c][:])[:, :, b * RUN : b * RUN + tokens], bank_in_runs(ub_banks[c, b])[:, :, :tokens]
-                    )
+        def gpsimd_tokens(c, b):
+            return max(0, min(RUN, GPSIMD_TOKENS[c] - b * RUN))
 
-        def products(c):
-            h = [in_runs(h_tiles[c % 2][:, a * SUBS * CHUNK : (a + 1) * SUBS * CHUNK]) for a in range(R_PASSES)]
-            tokens = GPSIMD_TOKENS[c]
-            ub, act = in_runs(pair_ub[c][:]), in_runs(pair_act[c][:])
-            nc.gpsimd.tensor_tensor(h[0][:, :, :tokens], ub[:, :, :tokens], act[:, :, :tokens], MULT)
-            for b in [b for b in range(BLOCKS) if gpsimd_tokens(c, b) < RUN]:
-                a, s = divmod(b, SUBS)
-                done = gpsimd_tokens(c, b)
-                nc.vector.tensor_tensor(
-                    h[a][:, :, s * RUN + done : (s + 1) * RUN],
-                    bank_in_runs(ub_banks[c, b])[:, :, done:],
-                    act_runs[c, b][:, :, done:],
-                    MULT,
+        def first_product(name, c, b, bank):
+            a, s = divmod(b, SUBS)
+            for t in range(PACK):
+                nc.tensor.matmul_mx(
+                    out=bank[:, t * SUB : (t + 1) * SUB],
+                    lhsT=dealt[name, a][:, t * P : (t + 1) * P].bitcast(FP8X4),
+                    lhsT_scale=w_plane(name, a, t),
+                    rhs=x_words[c * SUBS + s].bitcast(FP8X4),
+                    rhs_scale=x_plane(c, s),
+                    start=True,
+                    stop=True,
                 )
 
+        acts, ub_banks, ys = {}, {}, {}
+
+        def block_runs(tile, b):
+            return in_runs(tile)[:, :, b * RUN : (b + 1) * RUN]
+
+        def gelu(c, b):
+            acts[c, b] = block_runs(pair_act[c % 2][:], b) if gpsimd_tokens(c, b) else in_runs(act_tiles[c % 2, b][:])
+            bank = turn(scalar_banks)
+            first_product("wg", c, b, bank)
+            nc.scalar.activation(acts[c, b], bank_in_runs(bank), GELU)
+
+        def ub_for_vector(c, b):
+            ub_banks[c, b] = turn(vector_banks)
+            first_product("wu", c, b, ub_banks[c, b])
+
+        def ub_for_gpsimd(c, b):
+            tokens = gpsimd_tokens(c, b)
+            if tokens == RUN:
+                bank = turn(scalar_banks)
+                first_product("wu", c, b, bank)
+            else:
+                ub_for_vector(c, b)
+                bank = ub_banks[c, b]
+            nc.scalar.copy(block_runs(pair_ub[c % 2][:], b)[:, :, :tokens], bank_in_runs(bank)[:, :, :tokens])
+
+        def h_pass(c, a):
+            return h_tiles[c % 2][:, a * SUBS * BLOCK : (a + 1) * SUBS * BLOCK]
+
+        def gpsimd_product(c):
+            h, ub, act = (in_runs(ap)[:, :, : GPSIMD_TOKENS[c]] for ap in (h_pass(c, 0), pair_ub[c % 2][:], pair_act[c % 2][:]))
+            nc.gpsimd.tensor_tensor(h, ub, act, MULT)
+
+        def vector_product(c, b):
+            done = gpsimd_tokens(c, b)
+            h = block_runs(h_pass(c, b // SUBS), b % SUBS)
+            nc.vector.tensor_tensor(h[:, :, done:], bank_in_runs(ub_banks[c, b])[:, :, done:], acts[c, b][:, :, done:], MULT)
+
+        def vector_block(c, b):
+            gelu(c, b)
+            ub_for_vector(c, b)
+            vector_product(c, b)
+
         def quantise(c):
-            h_codes[c] = held.tile([P, R_PASSES * CHUNK], U32, name="h_codes%d" % c, align_bytes=64)
-            h_planes[c] = held.tile([P, R_PASSES * CHUNK], U8, name="h_plane%d" % c, align_bytes=64)
             nc.vector.quantize_mx(out=h_codes[c][:].bitcast(FP8X4), scales=h_planes[c][:], in_=h_tiles[c % 2][:])
 
-        def down(c, n, y, bank):
+        def down(c, n, y):
+            bank = turn(scalar_banks)
             for a in range(R_PASSES):
                 nc.tensor.matmul_mx(
-                    out=bank,
+                    out=bank[:],
                     lhsT=wd[:, a, 2 * n * P : 2 * (n + 1) * P].bitcast(FP4X4),
-                    lhsT_scale=wd_plane[:, a * N + n * P : a * N + (n + 1) * P],
+                    lhsT_scale=late_planes[:, LATE_WD + a * N + n * P : LATE_WD + a * N + (n + 1) * P],
                     rhs=h_codes[c][:, a * CHUNK : (a + 1) * CHUNK].bitcast(FP8X4),
                     rhs_scale=h_planes[c][:, a * CHUNK : (a + 1) * CHUNK],
                     start=(a == 0),
                     stop=(a == R_PASSES - 1),
                 )
             nc.scalar.copy(
-                y.rearrange("p (s k j) -> p s k j", s=SUBS, k=RUNS), bank.rearrange("p (k s j) -> p s k j", s=SUBS, k=RUNS)
+                y.rearrange("p (s k j) -> p s k j", s=SUBS, k=RUNS), bank[:].rearrange("p (k s j) -> p s k j", s=SUBS, k=RUNS)
             )
 
-        def gate_step(c, n, y, res, first=0, end=CHUNK):
-            entries = offsets[:, (c * CHUNK + first) // 16 : (c * CHUNK + end) // 16]
-            nc.vector.tensor_tensor(res[:, first:end], gates[n][:].indirect(entries), y[:, first:end], MULT)
-            nc.sync.dma_start(out[n * P : (n + 1) * P, c * CHUNK + first : c * CHUNK + end], res[:, first:end])
+        def gate_step(c, n, res, y=None, cuts=(0, CHUNK)):
+            y = turn(y_ring)[:] if y is None else y
+            down(c, n, y)
+            ys[c, n] = y
+            for first, end in zip(cuts, cuts[1:]):
+                picked = gates[n][:].indirect(entries(c * CHUNK + first, c * CHUNK + end))
+                nc.vector.tensor_tensor(res[:, first:end], picked, y[:, first:end], MULT)
+                nc.sync.dma_start(out[n * P : (n + 1) * P, c * CHUNK + first : c * CHUNK + end], res[:, first:end])
 
-        first_y = held.tile([P, CHUNK], F32, name="first_y", align_bytes=64)
+        for b in (1, 2, 0):
+            gelu(0, b)
+        ub_for_gpsimd(0, 0)
+        gpsimd_product(0)
+        for b in (1, 2):
+            ub_for_vector(0, b)
+            vector_product(0, b)
+        for b in range(3, BLOCKS):
+            vector_block(0, b)
+        quantise(0)
+        vector_block(1, 2)
+        vector_block(1, 3)
+        for b in range(2):
+            gelu(1, b)
+            ub_for_gpsimd(1, b)
+        gpsimd_product(1)
+        vector_product(1, 1)
+        for b in range(4, BLOCKS):
+            vector_block(1, b)
 
-        def y_place(c, i):
-            if i == 0:
-                return first_y[:]
-            first = (5, 1, 3)[i - 1] * CHUNK
-            return h_tiles[(c + 1) % 2][:, first : first + 2 * CHUNK].bitcast(F32)
+        def cycle(c, first_units, pairs_ahead, last_units):
+            res = [act_tiles[(c - 1) % 2, b][:] for b in RES_BLOCKS]
+            gate_step(*first_units[0], res.pop(0))
+            quantise(c - 1)
+            for i, unit in enumerate(first_units[1:]):
+                gate_step(*unit, res.pop(0) if i else h_tiles[(c - 1) % 2][:, : 2 * BLOCK].bitcast(F32))
+            for b in range(pairs_ahead):
+                gelu(c, b)
+                ub_for_gpsimd(c, b)
+            gate_step(*last_units[0], res.pop(0))
+            pinned = h_tiles[c % 2][:, 3 * BLOCK : 5 * BLOCK].bitcast(F32)
+            gate_step(*last_units[1], ys[first_units[-1]], pinned)
+            for b in range(pairs_ahead, PAIR_BLOCKS):
+                gelu(c, b)
+                ub_for_gpsimd(c, b)
+            gpsimd_product(c)
+            vector_product(c, 2)
+            for b in range(PAIR_BLOCKS, BLOCKS):
+                vector_block(c, b)
 
-        units = [(c, n) for c in range(CHUNKS) for n in range(N_TILES)]
-        units.insert(2 * N_TILES - 2, units.pop(N_TILES - 1))
-        first_stage(0)
-        for c in range(CHUNKS):
-            last = c + 1 == CHUNKS
-            steps = [(i, units.pop(0)) for i in range(N_TILES - STEPS[c], N_TILES)]
-            for i, unit in steps:
-                down(*unit, y_place(c, i), ga_banks[c, SUBS + i][:].rearrange("p t j -> p (t j)"))
-            products(c)
-            if c == 0:
-                load_gates(2)
-                load_gates(3)
-            if last:
-                quantise(c)
-            else:
-                first_stage(c + 1)
-            for i, unit in steps:
-                gate_step(*unit, y_place(c, i), acts[c, SUBS + i])
-            if not last:
-                quantise(c)
-        for i, unit in enumerate(units):
-            y = held.tile([P, CHUNK], F32, name="last_y%d" % i, align_bytes=64)
-            down(*unit, y[:], psum.tile([P, CHUNK], F32, name="last_bank", tag="ub", bufs=4)[:])
-            res = held.tile([P, CHUNK], F32, name="last_res%d" % i, align_bytes=64)
-            for first, end in ((0, CHUNK),) if i + 1 < len(units) else ((0, CHUNK - SUB), (CHUNK - SUB, CHUNK)):
-                gate_step(*unit, y[:], res[:], first, end)
+        cycle(2, [(0, 0), (0, 1), (0, 2)], 1, [(1, 0), (1, 1)])
+        cycle(3, [(1, 2)], 0, [(0, 3), (1, 3)])
+        gate_step(2, 0, act_tiles[1, 6])
+        quantise(3)
+        gate_step(2, 1, act_tiles[1, 7])
+        gate_step(2, 2, h_tiles[1][:, : 2 * BLOCK].bitcast(F32))
+        gate_step(2, 3, act_tiles[1, 5])
+        for n, res in enumerate((act_tiles[1, 4], act_tiles[0, 4], act_tiles[0, 3], act_tiles[0, 6])):
+            cuts = (0, CHUNK) if n + 1 < N_TILES else (0, CHUNK - SUB, CHUNK)
+            gate_step(3, n, res, None, cuts)

@@ -29,24 +29,25 @@ BLOCK = SUB * PACK
 N_TILES = N // P
 ROWS_FIRST = P - 16
 KB = 1024
-EARLY_BYTES = CHUNK + 2 * PASS_ROWS
+WD_FIRST = CHUNK + 2 * R
+EARLY_BYTES = WD_FIRST + R_PASSES * N
 LATE_X = J - CHUNK
-LATE_WD = LATE_X + 2 * PASS_ROWS
-LATE_BYTES = LATE_WD + R_PASSES * N
 GATE_BYTES = 4 * T
-WD_PLACE = 0
-GATE_PLACES = tuple(2 * KB + n * GATE_BYTES for n in range(N_TILES))
-LATE_X_PLACE = GATE_PLACES[0] - LATE_X // 2
-LATE_PLACE = GATE_PLACES[3] - 2 * KB
+WD_PLACE = GATE_BYTES
+GATE_PLACES = (0,) + tuple(2 * KB + n * GATE_BYTES for n in range(1, N_TILES))
+TAB_ROWS_PLACE = WD_PLACE - KB
+LATE_PLACE = GATE_PLACES[3]
 RAW_U0_PLACE = GATE_PLACES[3] + GATE_BYTES
 RAW_1_PLACE = RAW_U0_PLACE + 2 * KB
 W_ROWS_PLACE = RAW_1_PLACE - KB
 RUNS = 4
 RUN = SUB // RUNS
 GPSIMD_TOKENS = (32, 48, 80, 80)
+H_TILE = (0, 0, 1, 0)
 PAIR_BLOCKS = 3
 RING = 4
-RES_BLOCKS = (6, 7, 5, 4)
+FEED = 4
+RESULTS = 5
 
 
 def tile_list_gmlpt_gelu_gate_kernel(
@@ -67,22 +68,21 @@ def tile_list_gmlpt_gelu_gate_kernel(
         offsets = held.tile([P, J // 16], U16, name="offsets")
         nc.sync.dma_start(offsets[:], offs)
 
-        tab_rows = own([P, T], U8, "tab_rows")
+        tab_rows = placed([P, T], U8, "tab_rows", TAB_ROWS_PLACE)
         nc.vector.memset(tab_rows[:ROWS_FIRST, :].bitcast(I32), 0)
         w_rows = placed([P, 2 * R], U8, "w_rows", W_ROWS_PLACE)
         nc.gpsimd.memset(w_rows[:ROWS_FIRST, :].bitcast(I32), 0)
         early_planes = own([P, EARLY_BYTES], U8, "early_planes")
-        late_planes = own([P, LATE_BYTES], U8, "late_planes")
         nc.gpsimd.memset(early_planes[:].bitcast(I32), 0)
-        nc.gpsimd.memset(late_planes[:].bitcast(I32), 0)
+        late_x_plane = own([P, LATE_X], U8, "late_x_plane")
+        nc.gpsimd.memset(late_x_plane[:].bitcast(I32), 0)
         early = own([P, EARLY_BYTES], U8, "early")
-        late = placed([P, LATE_BYTES], U8, "late", LATE_PLACE)
 
         nc.sync.dma_start(tab_rows[ROWS_FIRST:, :].bitcast(I32), tab_scales[0].bitcast(I32))
         for i, scales in enumerate((wg_scales, wu_scales)):
-            nc.sync.dma_start(w_rows[ROWS_FIRST:, i * R : (i + 1) * R].bitcast(I32), scales[0].bitcast(I32))
-        nc.sync.dma_start(
-            late[ROWS_FIRST:, LATE_WD:].bitcast(I32).rearrange("p (a n) -> p a n", a=R_PASSES),
+            nc.scalar.dma_start(w_rows[ROWS_FIRST:, i * R : (i + 1) * R].bitcast(I32), scales[0].bitcast(I32))
+        nc.scalar.dma_start(
+            early[ROWS_FIRST:, WD_FIRST:].bitcast(I32).rearrange("p (a n) -> p a n", a=R_PASSES),
             wd_scales.rearrange("a r n -> r a n").bitcast(I32),
         )
 
@@ -91,7 +91,7 @@ def tile_list_gmlpt_gelu_gate_kernel(
 
         raw_g0 = own([P, PASS_ROWS], I32, "raw_g0")
         nc.sync.dma_start(raw_g0[:], words_of(wg_words, 0))
-        tab = placed([P, T], U32, "tab", GATE_PLACES[1])
+        tab = placed([P, T], U32, "tab", GATE_PLACES[2])
         nc.sync.dma_start(tab[:].bitcast(I32), tab_words[0].rearrange("p n t -> p (n t)").bitcast(I32))
 
         def entries(first, end):
@@ -119,20 +119,19 @@ def tile_list_gmlpt_gelu_gate_kernel(
         early_x = own([P, CHUNK], U8, "early_x")
         nc.vector.tensor_copy(early_x[:], tab_rows[:].indirect(entries(0, CHUNK)))
         nc.vector.tensor_copy(early[:, :CHUNK].bitcast(I32), early_x[:].bitcast(I32))
-        deal_scales(early[:, CHUNK:], 0)
+        for a in range(R_PASSES):
+            deal_scales(early[:, CHUNK + a * R : CHUNK + (a + 1) * R], a)
         move_rows(early_planes, early)
-        deal_scales(late[:, LATE_X:LATE_WD], 1)
         deal_words("wg", 0, raw_g0[:])
         raw_u0 = placed([P, PASS_ROWS], I32, "raw_u0", RAW_U0_PLACE)
         nc.sync.dma_start(raw_u0[:], words_of(wu_words, 0))
         raw_1 = placed([P, 2, PASS_ROWS], I32, "raw_1", RAW_1_PLACE)
         nc.sync.dma_start(raw_1[:, 0, :], words_of(wg_words, 1))
         nc.sync.dma_start(raw_1[:, 1, :], words_of(wu_words, 1))
-        late_x = placed([P, LATE_X], U8, "late_x", LATE_X_PLACE)
+        late_x = placed([P, LATE_X], U8, "late_x", LATE_PLACE)
         nc.vector.tensor_copy(late_x[:, :CHUNK], tab_rows[:].indirect(entries(CHUNK, 2 * CHUNK)))
         nc.vector.tensor_copy(late_x[:, CHUNK:], tab_rows[:].indirect(entries(2 * CHUNK, J)))
-        nc.vector.tensor_copy(late[:, :LATE_X].bitcast(I32), late_x[:].bitcast(I32))
-        move_rows(late_planes, late)
+        move_rows(late_x_plane, late_x)
         wd = placed([P, R_PASSES, 2 * N], U8, "wd", WD_PLACE)
         nc.sync.dma_start(wd[:].bitcast(I32), wd_words.rearrange("a p n -> p a n").bitcast(I32))
         gates = [placed([P, T], F32, "gate%d" % n, GATE_PLACES[n]) for n in range(N_TILES)]
@@ -141,6 +140,7 @@ def tile_list_gmlpt_gelu_gate_kernel(
             nc.sync.dma_start(gates[n][:], gT[n * P : (n + 1) * P, :])
 
         load_gates(0)
+        load_gates(1)
         deal_words("wu", 0, raw_u0[:])
         deal_words("wg", 1, raw_1[:, 0, :])
         deal_words("wu", 1, raw_1[:, 1, :])
@@ -151,22 +151,21 @@ def tile_list_gmlpt_gelu_gate_kernel(
             nc.vector.tensor_copy(words[:], tab[:].indirect(entries(first, end)))
             for j in range(first, end, SUB):
                 x_words[j // SUB] = words[:, j - first : j - first + SUB]
-        for n in range(1, N_TILES):
+        for n in range(2, N_TILES):
             load_gates(n)
 
         def x_plane(c, s):
-            plane, first = (early_planes, 0) if c == 0 else (late_planes, (c - 1) * CHUNK)
+            plane, first = (early_planes, 0) if c == 0 else (late_x_plane, (c - 1) * CHUNK)
             return plane[:, first + s * SUB : first + (s + 1) * SUB]
 
         def w_plane(name, a, t):
-            plane, first = (early_planes, CHUNK) if a == 0 else (late_planes, LATE_X)
-            first = first + (PASS_ROWS if name == "wu" else 0) + t * P
-            return plane[:, first : first + P]
+            first = CHUNK + a * R + (PASS_ROWS if name == "wu" else 0) + t * P
+            return early_planes[:, first : first + P]
 
         scalar_banks = [psum.tile([P, BLOCK], F32, name="scalar_bank%d" % i) for i in range(RING)]
         vector_banks = [psum.tile([P, BLOCK], F32, name="vector_bank%d" % i) for i in range(RING)]
-        act_tiles = {(i, b): own([P, BLOCK], F32, "act%d_%d" % (i, b)) for i in range(2) for b in range(1 + i, BLOCKS)}
-        y_ring = [own([P, CHUNK], F32, "y%d" % i) for i in range(RING)]
+        feed_ring = [own([P, BLOCK], F32, "feed%d" % i) for i in range(FEED)]
+        res_ring = [own([P, CHUNK], F32, "res%d" % i) for i in range(RESULTS)]
         pair_act = [own([P, PAIR_BLOCKS * BLOCK], F32, "pair_act%d" % i) for i in range(2)]
         pair_ub = [own([P, PAIR_BLOCKS * BLOCK], F32, "pair_ub%d" % i) for i in range(2)]
         h_tiles = [own([P, BLOCKS * BLOCK], BF16, "h%d" % i) for i in range(2)]
@@ -199,13 +198,13 @@ def tile_list_gmlpt_gelu_gate_kernel(
                     stop=True,
                 )
 
-        acts, ub_banks, ys = {}, {}, {}
+        acts, ub_banks = {}, {}
 
         def block_runs(tile, b):
             return in_runs(tile)[:, :, b * RUN : (b + 1) * RUN]
 
         def gelu(c, b):
-            acts[c, b] = block_runs(pair_act[c % 2][:], b) if gpsimd_tokens(c, b) else in_runs(act_tiles[c % 2, b][:])
+            acts[c, b] = block_runs(pair_act[c % 2][:], b) if gpsimd_tokens(c, b) else in_runs(turn(feed_ring)[:])
             bank = turn(scalar_banks)
             first_product("wg", c, b, bank)
             nc.scalar.activation(acts[c, b], bank_in_runs(bank), GELU)
@@ -225,7 +224,7 @@ def tile_list_gmlpt_gelu_gate_kernel(
             nc.scalar.copy(block_runs(pair_ub[c % 2][:], b)[:, :, :tokens], bank_in_runs(bank)[:, :, :tokens])
 
         def h_pass(c, a):
-            return h_tiles[c % 2][:, a * SUBS * BLOCK : (a + 1) * SUBS * BLOCK]
+            return h_tiles[H_TILE[c]][:, a * SUBS * BLOCK : (a + 1) * SUBS * BLOCK]
 
         def gpsimd_product(c):
             h, ub, act = (in_runs(ap)[:, :, : GPSIMD_TOKENS[c]] for ap in (h_pass(c, 0), pair_ub[c % 2][:], pair_act[c % 2][:]))
@@ -242,7 +241,7 @@ def tile_list_gmlpt_gelu_gate_kernel(
             vector_product(c, b)
 
         def quantise(c):
-            nc.vector.quantize_mx(out=h_codes[c][:].bitcast(FP8X4), scales=h_planes[c][:], in_=h_tiles[c % 2][:])
+            nc.vector.quantize_mx(out=h_codes[c][:].bitcast(FP8X4), scales=h_planes[c][:], in_=h_tiles[H_TILE[c]][:])
 
         def down(c, n, y):
             bank = turn(scalar_banks)
@@ -250,7 +249,7 @@ def tile_list_gmlpt_gelu_gate_kernel(
                 nc.tensor.matmul_mx(
                     out=bank[:],
                     lhsT=wd[:, a, 2 * n * P : 2 * (n + 1) * P].bitcast(FP4X4),
-                    lhsT_scale=late_planes[:, LATE_WD + a * N + n * P : LATE_WD + a * N + (n + 1) * P],
+                    lhsT_scale=early_planes[:, WD_FIRST + a * N + n * P : WD_FIRST + a * N + (n + 1) * P],
                     rhs=h_codes[c][:, a * CHUNK : (a + 1) * CHUNK].bitcast(FP8X4),
                     rhs_scale=h_planes[c][:, a * CHUNK : (a + 1) * CHUNK],
                     start=(a == 0),
@@ -260,10 +259,10 @@ def tile_list_gmlpt_gelu_gate_kernel(
                 y.rearrange("p (s k j) -> p s k j", s=SUBS, k=RUNS), bank[:].rearrange("p (k s j) -> p s k j", s=SUBS, k=RUNS)
             )
 
-        def gate_step(c, n, res, y=None, cuts=(0, CHUNK)):
-            y = turn(y_ring)[:] if y is None else y
+        def gate_step(c, n, res=None, y=None, cuts=(0, CHUNK)):
+            y = turn(feed_ring)[:] if y is None else y
+            res = turn(res_ring)[:] if res is None else res
             down(c, n, y)
-            ys[c, n] = y
             for first, end in zip(cuts, cuts[1:]):
                 picked = gates[n][:].indirect(entries(c * CHUNK + first, c * CHUNK + end))
                 nc.vector.tensor_tensor(res[:, first:end], picked, y[:, first:end], MULT)
@@ -290,17 +289,16 @@ def tile_list_gmlpt_gelu_gate_kernel(
             vector_block(1, b)
 
         def cycle(c, first_units, pairs_ahead, last_units):
-            res = [act_tiles[(c - 1) % 2, b][:] for b in RES_BLOCKS]
-            gate_step(*first_units[0], res.pop(0))
+            gate_step(*first_units[0])
             quantise(c - 1)
-            for i, unit in enumerate(first_units[1:]):
-                gate_step(*unit, res.pop(0) if i else h_tiles[(c - 1) % 2][:, : 2 * BLOCK].bitcast(F32))
+            for unit in first_units[1:]:
+                gate_step(*unit, h_tiles[H_TILE[c - 1]][:, : 2 * BLOCK].bitcast(F32))
             for b in range(pairs_ahead):
                 gelu(c, b)
                 ub_for_gpsimd(c, b)
-            gate_step(*last_units[0], res.pop(0))
-            pinned = h_tiles[c % 2][:, 3 * BLOCK : 5 * BLOCK].bitcast(F32)
-            gate_step(*last_units[1], ys[first_units[-1]], pinned)
+            for unit in last_units[:-1]:
+                gate_step(*unit)
+            gate_step(*last_units[-1], None, h_tiles[H_TILE[c]][:, 3 * BLOCK : 5 * BLOCK].bitcast(F32))
             for b in range(pairs_ahead, PAIR_BLOCKS):
                 gelu(c, b)
                 ub_for_gpsimd(c, b)
@@ -309,13 +307,12 @@ def tile_list_gmlpt_gelu_gate_kernel(
             for b in range(PAIR_BLOCKS, BLOCKS):
                 vector_block(c, b)
 
-        cycle(2, [(0, 0), (0, 1), (0, 2)], 1, [(1, 0), (1, 1)])
+        cycle(2, [(0, 0), (0, 1)], 2, [(1, 0), (1, 1), (0, 2)])
         cycle(3, [(1, 2)], 0, [(0, 3), (1, 3)])
-        gate_step(2, 0, act_tiles[1, 6])
+        gate_step(2, 0)
         quantise(3)
-        gate_step(2, 1, act_tiles[1, 7])
-        gate_step(2, 2, h_tiles[1][:, : 2 * BLOCK].bitcast(F32))
-        gate_step(2, 3, act_tiles[1, 5])
-        for n, res in enumerate((act_tiles[1, 4], act_tiles[0, 4], act_tiles[0, 3], act_tiles[0, 6])):
-            cuts = (0, CHUNK) if n + 1 < N_TILES else (0, CHUNK - SUB, CHUNK)
-            gate_step(3, n, res, None, cuts)
+        gate_step(2, 1)
+        gate_step(2, 2, h_tiles[H_TILE[3]][:, : 2 * BLOCK].bitcast(F32))
+        gate_step(2, 3)
+        for n in range(N_TILES):
+            gate_step(3, n, None, None, (0, CHUNK) if n + 1 < N_TILES else (0, CHUNK - SUB, CHUNK))

@@ -29,21 +29,21 @@ BLOCK = SUB * PACK
 N_TILES = N // P
 ROWS_FIRST = P - 16
 KB = 1024
-WD_FIRST = CHUNK + 2 * R
-EARLY_BYTES = WD_FIRST + R_PASSES * N
+EARLY_BYTES = CHUNK + 2 * PASS_ROWS
 LATE_X = J - CHUNK
+LATE_WD = LATE_X + 2 * PASS_ROWS
+LATE_BYTES = LATE_WD + R_PASSES * N
 GATE_BYTES = 4 * T
-WD_PLACE = GATE_BYTES
-GATE_PLACES = (0,) + tuple(2 * KB + n * GATE_BYTES for n in range(1, N_TILES))
-TAB_ROWS_PLACE = WD_PLACE - KB
-LATE_PLACE = GATE_PLACES[3]
+WD_PLACE = 0
+GATE_PLACES = tuple(2 * KB + n * GATE_BYTES for n in range(N_TILES))
+LATE_X_PLACE = GATE_PLACES[0] - LATE_X // 2
+LATE_PLACE = GATE_PLACES[3] - 2 * KB
 RAW_U0_PLACE = GATE_PLACES[3] + GATE_BYTES
 RAW_1_PLACE = RAW_U0_PLACE + 2 * KB
 W_ROWS_PLACE = RAW_1_PLACE - KB
 RUNS = 4
 RUN = SUB // RUNS
 GPSIMD_TOKENS = (32, 48, 80, 80)
-H_TILE = (0, 0, 1, 0)
 PAIR_BLOCKS = 3
 RING = 4
 FEED = 4
@@ -68,21 +68,22 @@ def tile_list_gmlpt_gelu_gate_kernel(
         offsets = held.tile([P, J // 16], U16, name="offsets")
         nc.sync.dma_start(offsets[:], offs)
 
-        tab_rows = placed([P, T], U8, "tab_rows", TAB_ROWS_PLACE)
+        tab_rows = own([P, T], U8, "tab_rows")
         nc.vector.memset(tab_rows[:ROWS_FIRST, :].bitcast(I32), 0)
         w_rows = placed([P, 2 * R], U8, "w_rows", W_ROWS_PLACE)
         nc.gpsimd.memset(w_rows[:ROWS_FIRST, :].bitcast(I32), 0)
         early_planes = own([P, EARLY_BYTES], U8, "early_planes")
+        late_planes = own([P, LATE_BYTES], U8, "late_planes")
         nc.gpsimd.memset(early_planes[:].bitcast(I32), 0)
-        late_x_plane = own([P, LATE_X], U8, "late_x_plane")
-        nc.gpsimd.memset(late_x_plane[:].bitcast(I32), 0)
+        nc.gpsimd.memset(late_planes[:].bitcast(I32), 0)
         early = own([P, EARLY_BYTES], U8, "early")
+        late = placed([P, LATE_BYTES], U8, "late", LATE_PLACE)
 
         nc.sync.dma_start(tab_rows[ROWS_FIRST:, :].bitcast(I32), tab_scales[0].bitcast(I32))
         for i, scales in enumerate((wg_scales, wu_scales)):
-            nc.scalar.dma_start(w_rows[ROWS_FIRST:, i * R : (i + 1) * R].bitcast(I32), scales[0].bitcast(I32))
-        nc.scalar.dma_start(
-            early[ROWS_FIRST:, WD_FIRST:].bitcast(I32).rearrange("p (a n) -> p a n", a=R_PASSES),
+            nc.sync.dma_start(w_rows[ROWS_FIRST:, i * R : (i + 1) * R].bitcast(I32), scales[0].bitcast(I32))
+        nc.sync.dma_start(
+            late[ROWS_FIRST:, LATE_WD:].bitcast(I32).rearrange("p (a n) -> p a n", a=R_PASSES),
             wd_scales.rearrange("a r n -> r a n").bitcast(I32),
         )
 
@@ -91,7 +92,7 @@ def tile_list_gmlpt_gelu_gate_kernel(
 
         raw_g0 = own([P, PASS_ROWS], I32, "raw_g0")
         nc.sync.dma_start(raw_g0[:], words_of(wg_words, 0))
-        tab = placed([P, T], U32, "tab", GATE_PLACES[2])
+        tab = placed([P, T], U32, "tab", GATE_PLACES[1])
         nc.sync.dma_start(tab[:].bitcast(I32), tab_words[0].rearrange("p n t -> p (n t)").bitcast(I32))
 
         def entries(first, end):
@@ -119,19 +120,20 @@ def tile_list_gmlpt_gelu_gate_kernel(
         early_x = own([P, CHUNK], U8, "early_x")
         nc.vector.tensor_copy(early_x[:], tab_rows[:].indirect(entries(0, CHUNK)))
         nc.vector.tensor_copy(early[:, :CHUNK].bitcast(I32), early_x[:].bitcast(I32))
-        for a in range(R_PASSES):
-            deal_scales(early[:, CHUNK + a * R : CHUNK + (a + 1) * R], a)
+        deal_scales(early[:, CHUNK:], 0)
         move_rows(early_planes, early)
+        deal_scales(late[:, LATE_X:LATE_WD], 1)
         deal_words("wg", 0, raw_g0[:])
         raw_u0 = placed([P, PASS_ROWS], I32, "raw_u0", RAW_U0_PLACE)
         nc.sync.dma_start(raw_u0[:], words_of(wu_words, 0))
         raw_1 = placed([P, 2, PASS_ROWS], I32, "raw_1", RAW_1_PLACE)
         nc.sync.dma_start(raw_1[:, 0, :], words_of(wg_words, 1))
         nc.sync.dma_start(raw_1[:, 1, :], words_of(wu_words, 1))
-        late_x = placed([P, LATE_X], U8, "late_x", LATE_PLACE)
+        late_x = placed([P, LATE_X], U8, "late_x", LATE_X_PLACE)
         nc.vector.tensor_copy(late_x[:, :CHUNK], tab_rows[:].indirect(entries(CHUNK, 2 * CHUNK)))
         nc.vector.tensor_copy(late_x[:, CHUNK:], tab_rows[:].indirect(entries(2 * CHUNK, J)))
-        move_rows(late_x_plane, late_x)
+        nc.vector.tensor_copy(late[:, :LATE_X].bitcast(I32), late_x[:].bitcast(I32))
+        move_rows(late_planes, late)
         wd = placed([P, R_PASSES, 2 * N], U8, "wd", WD_PLACE)
         nc.sync.dma_start(wd[:].bitcast(I32), wd_words.rearrange("a p n -> p a n").bitcast(I32))
         gates = [placed([P, T], F32, "gate%d" % n, GATE_PLACES[n]) for n in range(N_TILES)]
@@ -140,7 +142,6 @@ def tile_list_gmlpt_gelu_gate_kernel(
             nc.sync.dma_start(gates[n][:], gT[n * P : (n + 1) * P, :])
 
         load_gates(0)
-        load_gates(1)
         deal_words("wu", 0, raw_u0[:])
         deal_words("wg", 1, raw_1[:, 0, :])
         deal_words("wu", 1, raw_1[:, 1, :])
@@ -151,16 +152,17 @@ def tile_list_gmlpt_gelu_gate_kernel(
             nc.vector.tensor_copy(words[:], tab[:].indirect(entries(first, end)))
             for j in range(first, end, SUB):
                 x_words[j // SUB] = words[:, j - first : j - first + SUB]
-        for n in range(2, N_TILES):
+        for n in range(1, N_TILES):
             load_gates(n)
 
         def x_plane(c, s):
-            plane, first = (early_planes, 0) if c == 0 else (late_x_plane, (c - 1) * CHUNK)
+            plane, first = (early_planes, 0) if c == 0 else (late_planes, (c - 1) * CHUNK)
             return plane[:, first + s * SUB : first + (s + 1) * SUB]
 
         def w_plane(name, a, t):
-            first = CHUNK + a * R + (PASS_ROWS if name == "wu" else 0) + t * P
-            return early_planes[:, first : first + P]
+            plane, first = (early_planes, CHUNK) if a == 0 else (late_planes, LATE_X)
+            first = first + (PASS_ROWS if name == "wu" else 0) + t * P
+            return plane[:, first : first + P]
 
         scalar_banks = [psum.tile([P, BLOCK], F32, name="scalar_bank%d" % i) for i in range(RING)]
         vector_banks = [psum.tile([P, BLOCK], F32, name="vector_bank%d" % i) for i in range(RING)]
@@ -168,7 +170,9 @@ def tile_list_gmlpt_gelu_gate_kernel(
         res_ring = [own([P, CHUNK], F32, "res%d" % i) for i in range(RESULTS)]
         pair_act = [own([P, PAIR_BLOCKS * BLOCK], F32, "pair_act%d" % i) for i in range(2)]
         pair_ub = [own([P, PAIR_BLOCKS * BLOCK], F32, "pair_ub%d" % i) for i in range(2)]
-        h_tiles = [own([P, BLOCKS * BLOCK], BF16, "h%d" % i) for i in range(2)]
+        h_long = own([P, 3 * SUBS * BLOCK], BF16, "h_long")
+        h_short = own([P, BLOCKS * BLOCK], BF16, "h_short")
+        h_of = [h_long[:, SUBS * BLOCK :], h_long[:, : BLOCKS * BLOCK], h_short[:], h_long[:, : BLOCKS * BLOCK]]
         h_codes = [own([P, R_PASSES * CHUNK], U32, "h_codes%d" % c) for c in range(CHUNKS)]
         h_planes = [own([P, R_PASSES * CHUNK], U8, "h_plane%d" % c) for c in range(CHUNKS)]
 
@@ -224,7 +228,7 @@ def tile_list_gmlpt_gelu_gate_kernel(
             nc.scalar.copy(block_runs(pair_ub[c % 2][:], b)[:, :, :tokens], bank_in_runs(bank)[:, :, :tokens])
 
         def h_pass(c, a):
-            return h_tiles[H_TILE[c]][:, a * SUBS * BLOCK : (a + 1) * SUBS * BLOCK]
+            return h_of[c][:, a * SUBS * BLOCK : (a + 1) * SUBS * BLOCK]
 
         def gpsimd_product(c):
             h, ub, act = (in_runs(ap)[:, :, : GPSIMD_TOKENS[c]] for ap in (h_pass(c, 0), pair_ub[c % 2][:], pair_act[c % 2][:]))
@@ -241,7 +245,7 @@ def tile_list_gmlpt_gelu_gate_kernel(
             vector_product(c, b)
 
         def quantise(c):
-            nc.vector.quantize_mx(out=h_codes[c][:].bitcast(FP8X4), scales=h_planes[c][:], in_=h_tiles[H_TILE[c]][:])
+            nc.vector.quantize_mx(out=h_codes[c][:].bitcast(FP8X4), scales=h_planes[c][:], in_=h_of[c])
 
         def down(c, n, y):
             bank = turn(scalar_banks)
@@ -249,7 +253,7 @@ def tile_list_gmlpt_gelu_gate_kernel(
                 nc.tensor.matmul_mx(
                     out=bank[:],
                     lhsT=wd[:, a, 2 * n * P : 2 * (n + 1) * P].bitcast(FP4X4),
-                    lhsT_scale=early_planes[:, WD_FIRST + a * N + n * P : WD_FIRST + a * N + (n + 1) * P],
+                    lhsT_scale=late_planes[:, LATE_WD + a * N + n * P : LATE_WD + a * N + (n + 1) * P],
                     rhs=h_codes[c][:, a * CHUNK : (a + 1) * CHUNK].bitcast(FP8X4),
                     rhs_scale=h_planes[c][:, a * CHUNK : (a + 1) * CHUNK],
                     start=(a == 0),
@@ -288,18 +292,13 @@ def tile_list_gmlpt_gelu_gate_kernel(
         for b in range(4, BLOCKS):
             vector_block(1, b)
 
-        def cycle(c, first_units, pairs_ahead, last_units):
-            gate_step(*first_units[0])
+        def cycle(c, units):
+            gate_step(*units[0])
             quantise(c - 1)
-            for unit in first_units[1:]:
-                gate_step(*unit, h_tiles[H_TILE[c - 1]][:, : 2 * BLOCK].bitcast(F32))
-            for b in range(pairs_ahead):
-                gelu(c, b)
-                ub_for_gpsimd(c, b)
-            for unit in last_units[:-1]:
+            for unit in units[1:-1]:
                 gate_step(*unit)
-            gate_step(*last_units[-1], None, h_tiles[H_TILE[c]][:, 3 * BLOCK : 5 * BLOCK].bitcast(F32))
-            for b in range(pairs_ahead, PAIR_BLOCKS):
+            gate_step(*units[-1], None, h_of[c][:, 3 * BLOCK : 5 * BLOCK].bitcast(F32))
+            for b in range(PAIR_BLOCKS):
                 gelu(c, b)
                 ub_for_gpsimd(c, b)
             gpsimd_product(c)
@@ -307,12 +306,13 @@ def tile_list_gmlpt_gelu_gate_kernel(
             for b in range(PAIR_BLOCKS, BLOCKS):
                 vector_block(c, b)
 
-        cycle(2, [(0, 0), (0, 1)], 2, [(1, 0), (1, 1), (0, 2)])
-        cycle(3, [(1, 2)], 0, [(0, 3), (1, 3)])
-        gate_step(2, 0)
+        cycle(2, [(0, 0), (0, 1), (0, 2)])
+        cycle(3, [(1, 0), (1, 1), (1, 2), (0, 3)])
+        gate_step(1, 3)
         quantise(3)
+        gate_step(2, 0)
         gate_step(2, 1)
-        gate_step(2, 2, h_tiles[H_TILE[3]][:, : 2 * BLOCK].bitcast(F32))
+        gate_step(2, 2, h_of[3][:, : 2 * BLOCK].bitcast(F32))
         gate_step(2, 3)
         for n in range(N_TILES):
             gate_step(3, n, None, None, (0, CHUNK) if n + 1 < N_TILES else (0, CHUNK - SUB, CHUNK))

@@ -43,7 +43,7 @@ RAW_1_PLACE = RAW_U0_PLACE + 2 * KB
 W_ROWS_PLACE = RAW_1_PLACE - KB
 RUNS = 4
 RUN = SUB // RUNS
-GPSIMD_TOKENS = (32, 48, 80, 80)
+GPSIMD_TOKENS = (32, 32, 64, 64)
 PAIR_BLOCKS = 3
 RING = 4
 FEED = 4
@@ -276,20 +276,18 @@ def tile_list_gmlpt_gelu_gate_kernel(
             gelu(0, b)
         ub_for_gpsimd(0, 0)
         gpsimd_product(0)
-        for b in (1, 2):
+        for b in range(1, BLOCKS):
+            if b + 2 < BLOCKS:
+                gelu(0, b + 2)
             ub_for_vector(0, b)
             vector_product(0, b)
-        for b in range(3, BLOCKS):
-            vector_block(0, b)
         quantise(0)
+        vector_block(1, 1)
         vector_block(1, 2)
-        vector_block(1, 3)
-        for b in range(2):
-            gelu(1, b)
-            ub_for_gpsimd(1, b)
+        gelu(1, 0)
+        ub_for_gpsimd(1, 0)
         gpsimd_product(1)
-        vector_product(1, 1)
-        for b in range(4, BLOCKS):
+        for b in range(3, BLOCKS):
             vector_block(1, b)
 
         def cycle(c, units):
@@ -298,12 +296,14 @@ def tile_list_gmlpt_gelu_gate_kernel(
             for unit in units[1:-1]:
                 gate_step(*unit)
             gate_step(*units[-1], None, h_of[c][:, 3 * BLOCK : 5 * BLOCK].bitcast(F32))
-            for b in range(PAIR_BLOCKS):
+            paired = [b for b in range(BLOCKS) if gpsimd_tokens(c, b)]
+            for b in paired:
                 gelu(c, b)
                 ub_for_gpsimd(c, b)
             gpsimd_product(c)
-            vector_product(c, 2)
-            for b in range(PAIR_BLOCKS, BLOCKS):
+            if gpsimd_tokens(c, paired[-1]) < RUN:
+                vector_product(c, paired[-1])
+            for b in range(len(paired), BLOCKS):
                 vector_block(c, b)
 
         cycle(2, [(0, 0), (0, 1), (0, 2)])

@@ -82,10 +82,6 @@ def tile_list_gmlpt_gelu_gate_kernel(
         nc.sync.dma_start(tab_rows[ROWS_FIRST:, :].bitcast(I32), tab_scales[0].bitcast(I32))
         for i, scales in enumerate((wg_scales, wu_scales)):
             nc.sync.dma_start(w_rows[ROWS_FIRST:, i * R : (i + 1) * R].bitcast(I32), scales[0].bitcast(I32))
-        nc.sync.dma_start(
-            late[ROWS_FIRST:, LATE_WD:].bitcast(I32).rearrange("p (a n) -> p a n", a=R_PASSES),
-            wd_scales.rearrange("a r n -> r a n").bitcast(I32),
-        )
 
         def words_of(words, a):
             return words[0].rearrange("p n t -> p (n t)").bitcast(I32)[:, a * PASS_ROWS : (a + 1) * PASS_ROWS]
@@ -117,11 +113,15 @@ def tile_list_gmlpt_gelu_gate_kernel(
                 raw.rearrange("p (c i t) -> p c t i", t=PACK, i=4),
             )
 
-        early_x = own([P, CHUNK], U8, "early_x")
+        early_x = placed([P, CHUNK], U8, "early_x", LATE_PLACE)
         nc.vector.tensor_copy(early_x[:], tab_rows[:].indirect(entries(0, CHUNK)))
         nc.vector.tensor_copy(early[:, :CHUNK].bitcast(I32), early_x[:].bitcast(I32))
         deal_scales(early[:, CHUNK:], 0)
         move_rows(early_planes, early)
+        nc.sync.dma_start(
+            late[ROWS_FIRST:, LATE_WD:].bitcast(I32).rearrange("p (a n) -> p a n", a=R_PASSES),
+            wd_scales.rearrange("a r n -> r a n").bitcast(I32),
+        )
         deal_scales(late[:, LATE_X:LATE_WD], 1)
         deal_words("wg", 0, raw_g0[:])
         raw_u0 = placed([P, PASS_ROWS], I32, "raw_u0", RAW_U0_PLACE)
@@ -290,29 +290,33 @@ def tile_list_gmlpt_gelu_gate_kernel(
         for b in range(3, BLOCKS):
             vector_block(1, b)
 
+        def in_h(c, first):
+            return h_of[c][:, first : first + 2 * BLOCK].bitcast(F32)
+
         def cycle(c, units):
+            paired = [b for b in range(BLOCKS) if gpsimd_tokens(c, b)]
             gate_step(*units[0])
             quantise(c - 1)
             for unit in units[1:-1]:
-                gate_step(*unit)
-            gate_step(*units[-1], None, h_of[c][:, 3 * BLOCK : 5 * BLOCK].bitcast(F32))
-            paired = [b for b in range(BLOCKS) if gpsimd_tokens(c, b)]
+                gate_step(*unit, in_h(2, 0) if unit == (1, 1) else None)
+            if c == 2:
+                gate_step(*units[-1], None, in_h(c, 3 * BLOCK))
             for b in paired:
                 gelu(c, b)
                 ub_for_gpsimd(c, b)
+            if c == 3:
+                gate_step(*units[-1], None, in_h(c, 3 * BLOCK))
             gpsimd_product(c)
-            if gpsimd_tokens(c, paired[-1]) < RUN:
-                vector_product(c, paired[-1])
             for b in range(len(paired), BLOCKS):
                 vector_block(c, b)
 
         cycle(2, [(0, 0), (0, 1), (0, 2)])
-        cycle(3, [(1, 0), (1, 1), (1, 2), (0, 3)])
-        gate_step(1, 3)
-        quantise(3)
-        gate_step(2, 0)
+        cycle(3, [(1, 0), (1, 1), (1, 2), (2, 0)])
         gate_step(2, 1)
-        gate_step(2, 2, h_of[3][:, : 2 * BLOCK].bitcast(F32))
+        quantise(3)
+        gate_step(2, 2)
+        gate_step(0, 3)
+        gate_step(1, 3, in_h(3, 0))
         gate_step(2, 3)
         for n in range(N_TILES):
             gate_step(3, n, None, None, (0, CHUNK) if n + 1 < N_TILES else (0, CHUNK - SUB, CHUNK))

@@ -74,8 +74,8 @@ def tile_list_gmlpt_gelu_gate_kernel(
         nc.gpsimd.memset(w_rows[:ROWS_FIRST, :].bitcast(I32), 0)
         early_planes = own([P, EARLY_BYTES], U8, "early_planes")
         late_planes = own([P, LATE_BYTES], U8, "late_planes")
-        nc.gpsimd.memset(early_planes[:].bitcast(I32), 0)
-        nc.gpsimd.memset(late_planes[:].bitcast(I32), 0)
+        nc.vector.memset(early_planes[:].bitcast(I32), 0)
+        nc.vector.memset(late_planes[:].bitcast(I32), 0)
         early = own([P, EARLY_BYTES], U8, "early")
         late = placed([P, LATE_BYTES], U8, "late", LATE_PLACE)
 
@@ -294,29 +294,24 @@ def tile_list_gmlpt_gelu_gate_kernel(
             return h_of[c][:, first : first + 2 * BLOCK].bitcast(F32)
 
         def cycle(c, units):
-            paired = [b for b in range(BLOCKS) if gpsimd_tokens(c, b)]
             gate_step(*units[0])
             quantise(c - 1)
             for unit in units[1:-1]:
-                gate_step(*unit, in_h(2, 0) if unit == (1, 1) else None)
-            if c == 2:
-                gate_step(*units[-1], None, in_h(c, 3 * BLOCK))
+                gate_step(*unit)
+            gate_step(*units[-1], None, in_h(c, 3 * BLOCK))
+            paired = [b for b in range(BLOCKS) if gpsimd_tokens(c, b)]
             for b in paired:
                 gelu(c, b)
                 ub_for_gpsimd(c, b)
-            if c == 3:
-                gate_step(*units[-1], None, in_h(c, 3 * BLOCK))
             gpsimd_product(c)
             for b in range(len(paired), BLOCKS):
                 vector_block(c, b)
 
-        cycle(2, [(0, 0), (0, 1), (0, 2)])
-        cycle(3, [(1, 0), (1, 1), (1, 2), (2, 0)])
-        gate_step(2, 1)
+        cycle(2, [(0, 0), (0, 1)])
+        cycle(3, [(1, 0), (1, 1), (0, 2), (1, 2)])
+        gate_step(2, 0)
         quantise(3)
-        gate_step(2, 2)
-        gate_step(0, 3)
-        gate_step(1, 3, in_h(3, 0))
-        gate_step(2, 3)
+        for unit in ((2, 1), (2, 2), (0, 3), (1, 3), (2, 3)):
+            gate_step(*unit)
         for n in range(N_TILES):
             gate_step(3, n, None, None, (0, CHUNK) if n + 1 < N_TILES else (0, CHUNK - SUB, CHUNK))

@@ -38,9 +38,8 @@ WD_PLACE = 0
 GATE_PLACES = tuple(2 * KB + n * GATE_BYTES for n in range(N_TILES))
 LATE_X_PLACE = GATE_PLACES[0] - LATE_X // 2
 LATE_PLACE = GATE_PLACES[3] - 2 * KB
-RAW_U0_PLACE = GATE_PLACES[3] + GATE_BYTES
-RAW_1_PLACE = RAW_U0_PLACE + 2 * KB
-W_ROWS_PLACE = RAW_1_PLACE - KB
+RAW_PLACE = LATE_PLACE + LATE_BYTES
+EARLY_X_PLACE = RAW_PLACE - CHUNK // 2
 RUNS = 4
 RUN = SUB // RUNS
 GPSIMD_TOKENS = (32, 32, 64, 64)
@@ -70,7 +69,7 @@ def tile_list_gmlpt_gelu_gate_kernel(
 
         tab_rows = own([P, T], U8, "tab_rows")
         nc.vector.memset(tab_rows[:ROWS_FIRST, :].bitcast(I32), 0)
-        w_rows = placed([P, 2 * R], U8, "w_rows", W_ROWS_PLACE)
+        w_rows = own([P, 2 * R], U8, "w_rows")
         nc.gpsimd.memset(w_rows[:ROWS_FIRST, :].bitcast(I32), 0)
         early_planes = own([P, EARLY_BYTES], U8, "early_planes")
         late_planes = own([P, LATE_BYTES], U8, "late_planes")
@@ -94,9 +93,9 @@ def tile_list_gmlpt_gelu_gate_kernel(
         def entries(first, end):
             return offsets[:, first // 16 : end // 16]
 
-        def move_rows(plane, rows):
+        def move_rows(plane, rows, queue):
             for i in range(4):
-                nc.sync.dma_start(plane[i:P:32, :].bitcast(I32), rows[ROWS_FIRST + i : P : 4, :].bitcast(I32))
+                queue.dma_start(plane[i:P:32, :].bitcast(I32), rows[ROWS_FIRST + i : P : 4, :].bitcast(I32))
 
         def deal_scales(to, a):
             nc.gpsimd.tensor_copy(
@@ -113,27 +112,26 @@ def tile_list_gmlpt_gelu_gate_kernel(
                 raw.rearrange("p (c i t) -> p c t i", t=PACK, i=4),
             )
 
-        early_x = placed([P, CHUNK], U8, "early_x", LATE_PLACE)
+        early_x = placed([P, CHUNK], U8, "early_x", EARLY_X_PLACE)
         nc.vector.tensor_copy(early_x[:], tab_rows[:].indirect(entries(0, CHUNK)))
         nc.vector.tensor_copy(early[:, :CHUNK].bitcast(I32), early_x[:].bitcast(I32))
         deal_scales(early[:, CHUNK:], 0)
-        move_rows(early_planes, early)
+        move_rows(early_planes, early, nc.scalar)
         nc.sync.dma_start(
             late[ROWS_FIRST:, LATE_WD:].bitcast(I32).rearrange("p (a n) -> p a n", a=R_PASSES),
             wd_scales.rearrange("a r n -> r a n").bitcast(I32),
         )
         deal_scales(late[:, LATE_X:LATE_WD], 1)
         deal_words("wg", 0, raw_g0[:])
-        raw_u0 = placed([P, PASS_ROWS], I32, "raw_u0", RAW_U0_PLACE)
-        nc.sync.dma_start(raw_u0[:], words_of(wu_words, 0))
-        raw_1 = placed([P, 2, PASS_ROWS], I32, "raw_1", RAW_1_PLACE)
-        nc.sync.dma_start(raw_1[:, 0, :], words_of(wg_words, 1))
-        nc.sync.dma_start(raw_1[:, 1, :], words_of(wu_words, 1))
+        raw = placed([P, 3, PASS_ROWS], I32, "raw", RAW_PLACE)
+        later_words = (("wu", wu_words, 0), ("wg", wg_words, 1), ("wu", wu_words, 1))
+        for i, (name, words, a) in enumerate(later_words):
+            nc.sync.dma_start(raw[:, i, :], words_of(words, a))
         late_x = placed([P, LATE_X], U8, "late_x", LATE_X_PLACE)
         nc.vector.tensor_copy(late_x[:, :CHUNK], tab_rows[:].indirect(entries(CHUNK, 2 * CHUNK)))
         nc.vector.tensor_copy(late_x[:, CHUNK:], tab_rows[:].indirect(entries(2 * CHUNK, J)))
         nc.vector.tensor_copy(late[:, :LATE_X].bitcast(I32), late_x[:].bitcast(I32))
-        move_rows(late_planes, late)
+        move_rows(late_planes, late, nc.sync)
         wd = placed([P, R_PASSES, 2 * N], U8, "wd", WD_PLACE)
         nc.sync.dma_start(wd[:].bitcast(I32), wd_words.rearrange("a p n -> p a n").bitcast(I32))
         gates = [placed([P, T], F32, "gate%d" % n, GATE_PLACES[n]) for n in range(N_TILES)]
@@ -142,9 +140,8 @@ def tile_list_gmlpt_gelu_gate_kernel(
             nc.sync.dma_start(gates[n][:], gT[n * P : (n + 1) * P, :])
 
         load_gates(0)
-        deal_words("wu", 0, raw_u0[:])
-        deal_words("wg", 1, raw_1[:, 0, :])
-        deal_words("wu", 1, raw_1[:, 1, :])
+        for i, (name, words, a) in enumerate(later_words):
+            deal_words(name, a, raw[:, i, :])
 
         x_words = {}
         for first, end in ((0, 2 * SUB), (2 * SUB, CHUNK)) + tuple((c * CHUNK, (c + 1) * CHUNK) for c in range(1, CHUNKS)):

@@ -42,8 +42,8 @@ RAW_PLACE = LATE_PLACE + LATE_BYTES
 EARLY_X_PLACE = RAW_PLACE - CHUNK // 2
 RUNS = 4
 RUN = SUB // RUNS
-GPSIMD_TOKENS = (32, 32, 64, 64)
-PAIR_BLOCKS = 3
+GPSIMD_BLOCKS = (1, 1, 2, 2)
+PAIR_BLOCKS = max(GPSIMD_BLOCKS)
 RING = 4
 FEED = 4
 RESULTS = 5
@@ -183,8 +183,8 @@ def tile_list_gmlpt_gelu_gate_kernel(
         def bank_in_runs(bank):
             return bank[:].rearrange("p (t k j) -> p k j t", t=PACK, k=RUNS)
 
-        def gpsimd_tokens(c, b):
-            return max(0, min(RUN, GPSIMD_TOKENS[c] - b * RUN))
+        def paired(c):
+            return range(SUBS - GPSIMD_BLOCKS[c], SUBS)
 
         def first_product(name, c, b, bank):
             a, s = divmod(b, SUBS)
@@ -205,7 +205,10 @@ def tile_list_gmlpt_gelu_gate_kernel(
             return in_runs(tile)[:, :, b * RUN : (b + 1) * RUN]
 
         def gelu(c, b):
-            acts[c, b] = block_runs(pair_act[c % 2][:], b) if gpsimd_tokens(c, b) else in_runs(turn(feed_ring)[:])
+            if b in paired(c):
+                acts[c, b] = block_runs(pair_act[c % 2][:], b - paired(c)[0])
+            else:
+                acts[c, b] = in_runs(turn(feed_ring)[:])
             bank = turn(scalar_banks)
             first_product("wg", c, b, bank)
             nc.scalar.activation(acts[c, b], bank_in_runs(bank), GELU)
@@ -215,26 +218,24 @@ def tile_list_gmlpt_gelu_gate_kernel(
             first_product("wu", c, b, ub_banks[c, b])
 
         def ub_for_gpsimd(c, b):
-            tokens = gpsimd_tokens(c, b)
-            if tokens == RUN:
-                bank = turn(scalar_banks)
-                first_product("wu", c, b, bank)
-            else:
-                ub_for_vector(c, b)
-                bank = ub_banks[c, b]
-            nc.scalar.copy(block_runs(pair_ub[c % 2][:], b)[:, :, :tokens], bank_in_runs(bank)[:, :, :tokens])
+            bank = turn(scalar_banks)
+            first_product("wu", c, b, bank)
+            nc.scalar.copy(block_runs(pair_ub[c % 2][:], b - paired(c)[0]), bank_in_runs(bank))
 
         def h_pass(c, a):
             return h_of[c][:, a * SUBS * BLOCK : (a + 1) * SUBS * BLOCK]
 
         def gpsimd_product(c):
-            h, ub, act = (in_runs(ap)[:, :, : GPSIMD_TOKENS[c]] for ap in (h_pass(c, 0), pair_ub[c % 2][:], pair_act[c % 2][:]))
-            nc.gpsimd.tensor_tensor(h, ub, act, MULT)
+            for b in paired(c):
+                gelu(c, b)
+                ub_for_gpsimd(c, b)
+            tokens = GPSIMD_BLOCKS[c] * RUN
+            ub, act = (in_runs(tile[c % 2][:])[:, :, :tokens] for tile in (pair_ub, pair_act))
+            nc.gpsimd.tensor_tensor(in_runs(h_pass(c, 0))[:, :, SUB - tokens :], ub, act, MULT)
 
         def vector_product(c, b):
-            done = gpsimd_tokens(c, b)
             h = block_runs(h_pass(c, b // SUBS), b % SUBS)
-            nc.vector.tensor_tensor(h[:, :, done:], bank_in_runs(ub_banks[c, b])[:, :, done:], acts[c, b][:, :, done:], MULT)
+            nc.vector.tensor_tensor(h, bank_in_runs(ub_banks[c, b]), acts[c, b], MULT)
 
         def vector_block(c, b):
             gelu(c, b)
@@ -269,39 +270,35 @@ def tile_list_gmlpt_gelu_gate_kernel(
                 nc.vector.tensor_tensor(res[:, first:end], picked, y[:, first:end], MULT)
                 nc.sync.dma_start(out[n * P : (n + 1) * P, c * CHUNK + first : c * CHUNK + end], res[:, first:end])
 
-        for b in (1, 2, 0):
+        def vector_blocks(c):
+            return [b for b in range(BLOCKS) if b not in paired(c)]
+
+        blocks = vector_blocks(0)
+        for b in blocks[:2]:
             gelu(0, b)
-        ub_for_gpsimd(0, 0)
         gpsimd_product(0)
-        for b in range(1, BLOCKS):
-            if b + 2 < BLOCKS:
-                gelu(0, b + 2)
+        for i, b in enumerate(blocks):
+            for ahead in blocks[i + 2 : i + 3]:
+                gelu(0, ahead)
             ub_for_vector(0, b)
             vector_product(0, b)
         quantise(0)
-        vector_block(1, 1)
-        vector_block(1, 2)
-        gelu(1, 0)
-        ub_for_gpsimd(1, 0)
-        gpsimd_product(1)
-        for b in range(3, BLOCKS):
+        blocks = vector_blocks(1)
+        for b in blocks[:2]:
             vector_block(1, b)
-
-        def in_h(c, first):
-            return h_of[c][:, first : first + 2 * BLOCK].bitcast(F32)
+        gpsimd_product(1)
+        for b in blocks[2:]:
+            vector_block(1, b)
 
         def cycle(c, units):
             gate_step(*units[0])
             quantise(c - 1)
             for unit in units[1:-1]:
                 gate_step(*unit)
-            gate_step(*units[-1], None, in_h(c, 3 * BLOCK))
-            paired = [b for b in range(BLOCKS) if gpsimd_tokens(c, b)]
-            for b in paired:
-                gelu(c, b)
-                ub_for_gpsimd(c, b)
+            first = 3 * BLOCK + PACK * RUN
+            gate_step(*units[-1], None, h_of[c][:, first : first + 2 * BLOCK].bitcast(F32))
             gpsimd_product(c)
-            for b in range(len(paired), BLOCKS):
+            for b in vector_blocks(c):
                 vector_block(c, b)
 
         cycle(2, [(0, 0), (0, 1)])

from contextlib import ExitStack

import concourse.mybir as mybir

K, R, N, T, J = 512, 1024, 512, 4096, 2048
FLOPS = 2 * K * R * J * 2 + 2 * R * N * J

F32 = mybir.dt.float32
BF16 = mybir.dt.bfloat16
I32 = mybir.dt.int32
U32 = mybir.dt.uint32
U16 = mybir.dt.uint16
U8 = mybir.dt.uint8
FP8X4 = mybir.dt.float8_e4m3fn_x4
FP4X4 = mybir.dt.float4_e2m1fn_x4
MULT = mybir.AluOpType.mult
GELU = mybir.ActivationFunctionType.Gelu_apprx_tanh

P = 128
PACK = 4
PASS_ROWS = P * PACK
R_PASSES = R // PASS_ROWS
CHUNK = 512
CHUNKS = J // CHUNK
SUB = 128
SUBS = CHUNK // SUB
BLOCKS = R_PASSES * SUBS
BLOCK = SUB * PACK
N_TILES = N // P
ROWS_FIRST = P - 16
KB = 1024
EARLY_BYTES = CHUNK + 2 * PASS_ROWS
LATE_X = J - CHUNK
LATE_WD = LATE_X + 2 * PASS_ROWS
LATE_BYTES = LATE_WD + R_PASSES * N
GATE_BYTES = 4 * T
WD_PLACE = 0
GATE_PLACES = tuple(2 * KB + n * GATE_BYTES for n in range(N_TILES))
LATE_X_PLACE = GATE_PLACES[0] - LATE_X // 2
LATE_PLACE = GATE_PLACES[3] - 2 * KB
RAW_PLACE = LATE_PLACE + LATE_BYTES
EARLY_X_PLACE = RAW_PLACE - CHUNK // 2
RUNS = 4
RUN = SUB // RUNS
GPSIMD_BLOCKS = (1, 1, 2, 2)
PAIR_BLOCKS = max(GPSIMD_BLOCKS)
RING = 4
FEED = 4
RESULTS = 5


def tile_list_gmlpt_gelu_gate_kernel(
    tc, tab_words, tab_scales, wg_words, wg_scales, wu_words, wu_scales, wd_words, wd_scales, gT, offs, out
):
    nc = tc.nc
    with ExitStack() as ctx:
        held = ctx.enter_context(tc.tile_pool(name="held", bufs=1))
        shared = ctx.enter_context(tc.tile_pool(name="shared", bufs=1))
        psum = ctx.enter_context(tc.psum_pool(name="psum", bufs=1))

        def own(shape, dtype, name):
            return held.tile(shape, dtype, name=name, align_bytes=64)

        def placed(shape, dtype, name, offset):
            return shared.tile(shape, dtype, name=name, align_bytes=64, offset=offset)

        offsets = held.tile([P, J // 16], U16, name="offsets")
        nc.sync.dma_start(offsets[:], offs)

        tab_rows = own([P, T], U8, "tab_rows")
        nc.vector.memset(tab_rows[:ROWS_FIRST, :].bitcast(I32), 0)
        w_rows = own([P, 2 * R], U8, "w_rows")
        nc.gpsimd.memset(w_rows[:ROWS_FIRST, :].bitcast(I32), 0)
        early_planes = own([P, EARLY_BYTES], U8, "early_planes")
        late_planes = own([P, LATE_BYTES], U8, "late_planes")
        nc.vector.memset(early_planes[:].bitcast(I32), 0)
        nc.vector.memset(late_planes[:].bitcast(I32), 0)
        early = own([P, EARLY_BYTES], U8, "early")
        late = placed([P, LATE_BYTES], U8, "late", LATE_PLACE)

        nc.sync.dma_start(tab_rows[ROWS_FIRST:, :].bitcast(I32), tab_scales[0].bitcast(I32))
        for i, scales in enumerate((wg_scales, wu_scales)):
            nc.sync.dma_start(w_rows[ROWS_FIRST:, i * R : (i + 1) * R].bitcast(I32), scales[0].bitcast(I32))

        def words_of(words, a):
            return words[0].rearrange("p n t -> p (n t)").bitcast(I32)[:, a * PASS_ROWS : (a + 1) * PASS_ROWS]

        raw_g0 = own([P, PASS_ROWS], I32, "raw_g0")
        nc.sync.dma_start(raw_g0[:], words_of(wg_words, 0))
        tab = placed([P, T], U32, "tab", GATE_PLACES[1])
        nc.sync.dma_start(tab[:].bitcast(I32), tab_words[0].rearrange("p n t -> p (n t)").bitcast(I32))

        def entries(first, end):
            return offsets[:, first // 16 : end // 16]

        def move_rows(plane, rows, queue):
            for i in range(4):
                queue.dma_start(plane[i:P:32, :].bitcast(I32), rows[ROWS_FIRST + i : P : 4, :].bitcast(I32))

        def deal_scales(to, a):
            nc.gpsimd.tensor_copy(
                to.rearrange("p (w t m) -> p w t m", w=2, t=PACK),
                w_rows[:].rearrange("p (w a m t) -> p a w t m", w=2, a=R_PASSES, t=PACK)[:, a],
            )

        dealt = {}

        def deal_words(name, a, raw):
            dealt[name, a] = own([P, PASS_ROWS], I32, "%s%d" % (name, a))
            nc.gpsimd.tensor_copy(
                dealt[name, a][:].rearrange("p (t c i) -> p c t i", t=PACK, i=4),
                raw.rearrange("p (c i t) -> p c t i", t=PACK, i=4),
            )

        early_x = placed([P, CHUNK], U8, "early_x", EARLY_X_PLACE)
        nc.vector.tensor_copy(early_x[:], tab_rows[:].indirect(entries(0, CHUNK)))
        nc.vector.tensor_copy(early[:, :CHUNK].bitcast(I32), early_x[:].bitcast(I32))
        deal_scales(early[:, CHUNK:], 0)
        move_rows(early_planes, early, nc.scalar)
        nc.sync.dma_start(
            late[ROWS_FIRST:, LATE_WD:].bitcast(I32).rearrange("p (a n) -> p a n", a=R_PASSES),
            wd_scales.rearrange("a r n -> r a n").bitcast(I32),
        )
        deal_scales(late[:, LATE_X:LATE_WD], 1)
        deal_words("wg", 0, raw_g0[:])
        raw = placed([P, 3, PASS_ROWS], I32, "raw", RAW_PLACE)
        later_words = (("wu", wu_words, 0), ("wg", wg_words, 1), ("wu", wu_words, 1))
        for i, (name, words, a) in enumerate(later_words):
            nc.sync.dma_start(raw[:, i, :], words_of(words, a))
        late_x = placed([P, LATE_X], U8, "late_x", LATE_X_PLACE)
        nc.vector.tensor_copy(late_x[:, :CHUNK], tab_rows[:].indirect(entries(CHUNK, 2 * CHUNK)))
        nc.vector.tensor_copy(late_x[:, CHUNK:], tab_rows[:].indirect(entries(2 * CHUNK, J)))
        nc.vector.tensor_copy(late[:, :LATE_X].bitcast(I32), late_x[:].bitcast(I32))
        move_rows(late_planes, late, nc.sync)
        wd = placed([P, R_PASSES, 2 * N], U8, "wd", WD_PLACE)
        nc.sync.dma_start(wd[:].bitcast(I32), wd_words.rearrange("a p n -> p a n").bitcast(I32))
        gates = [placed([P, T], F32, "gate%d" % n, GATE_PLACES[n]) for n in range(N_TILES)]

        def load_gates(n):
            nc.sync.dma_start(gates[n][:], gT[n * P : (n + 1) * P, :])

        load_gates(0)
        for i, (name, words, a) in enumerate(later_words):
            deal_words(name, a, raw[:, i, :])

        x_words = {}
        for first, end in ((0, 2 * SUB), (2 * SUB, CHUNK)) + tuple((c * CHUNK, (c + 1) * CHUNK) for c in range(1, CHUNKS)):
            words = own([P, end - first], U32, "x_words%d" % first)
            nc.vector.tensor_copy(words[:], tab[:].indirect(entries(first, end)))
            for j in range(first, end, SUB):
                x_words[j // SUB] = words[:, j - first : j - first + SUB]
        for n in range(1, N_TILES):
            load_gates(n)

        def x_plane(c, s):
            plane, first = (early_planes, 0) if c == 0 else (late_planes, (c - 1) * CHUNK)
            return plane[:, first + s * SUB : first + (s + 1) * SUB]

        def w_plane(name, a, t):
            plane, first = (early_planes, CHUNK) if a == 0 else (late_planes, LATE_X)
            first = first + (PASS_ROWS if name == "wu" else 0) + t * P
            return plane[:, first : first + P]

        scalar_banks = [psum.tile([P, BLOCK], F32, name="scalar_bank%d" % i) for i in range(RING)]
        vector_banks = [psum.tile([P, BLOCK], F32, name="vector_bank%d" % i) for i in range(RING)]
        feed_ring = [own([P, BLOCK], F32, "feed%d" % i) for i in range(FEED)]
        res_ring = [own([P, CHUNK], F32, "res%d" % i) for i in range(RESULTS)]
        pair_act = [own([P, PAIR_BLOCKS * BLOCK], F32, "pair_act%d" % i) for i in range(2)]
        pair_ub = [own([P, PAIR_BLOCKS * BLOCK], F32, "pair_ub%d" % i) for i in range(2)]
        h_long = own([P, 3 * SUBS * BLOCK], BF16, "h_long")
        h_short = own([P, BLOCKS * BLOCK], BF16, "h_short")
        h_of = [h_long[:, SUBS * BLOCK :], h_long[:, : BLOCKS * BLOCK], h_short[:], h_long[:, : BLOCKS * BLOCK]]
        h_codes = [own([P, R_PASSES * CHUNK], U32, "h_codes%d" % c) for c in range(CHUNKS)]
        h_planes = [own([P, R_PASSES * CHUNK], U8, "h_plane%d" % c) for c in range(CHUNKS)]

        def turn(ring):
            ring.append(ring.pop(0))
            return ring[-1]

        def in_runs(ap):
            return ap.rearrange("p (k j t) -> p k j t", k=RUNS, t=PACK)

        def bank_in_runs(bank):
            return bank[:].rearrange("p (t k j) -> p k j t", t=PACK, k=RUNS)

        def paired(c):
            return range(SUBS - GPSIMD_BLOCKS[c], SUBS)

        def first_product(name, c, b, bank):
            a, s = divmod(b, SUBS)
            for t in range(PACK):
                nc.tensor.matmul_mx(
                    out=bank[:, t * SUB : (t + 1) * SUB],
                    lhsT=dealt[name, a][:, t * P : (t + 1) * P].bitcast(FP8X4),
                    lhsT_scale=w_plane(name, a, t),
                    rhs=x_words[c * SUBS + s].bitcast(FP8X4),
                    rhs_scale=x_plane(c, s),
                    start=True,
                    stop=True,
                )

        acts, ub_banks = {}, {}

        def block_runs(tile, b):
            return in_runs(tile)[:, :, b * RUN : (b + 1) * RUN]

        def gelu(c, b):
            if b in paired(c):
                acts[c, b] = block_runs(pair_act[c % 2][:], b - paired(c)[0])
            else:
                acts[c, b] = in_runs(turn(feed_ring)[:])
            bank = turn(scalar_banks)
            first_product("wg", c, b, bank)
            nc.scalar.activation(acts[c, b], bank_in_runs(bank), GELU)

        def ub_for_vector(c, b):
            ub_banks[c, b] = turn(vector_banks)
            first_product("wu", c, b, ub_banks[c, b])

        def ub_for_gpsimd(c, b):
            bank = turn(scalar_banks)
            first_product("wu", c, b, bank)
            nc.scalar.copy(block_runs(pair_ub[c % 2][:], b - paired(c)[0]), bank_in_runs(bank))

        def h_pass(c, a):
            return h_of[c][:, a * SUBS * BLOCK : (a + 1) * SUBS * BLOCK]

        def gpsimd_product(c):
            for b in paired(c):
                gelu(c, b)
                ub_for_gpsimd(c, b)
            tokens = GPSIMD_BLOCKS[c] * RUN
            ub, act = (in_runs(tile[c % 2][:])[:, :, :tokens] for tile in (pair_ub, pair_act))
            nc.gpsimd.tensor_tensor(in_runs(h_pass(c, 0))[:, :, SUB - tokens :], ub, act, MULT)

        def vector_product(c, b):
            h = block_runs(h_pass(c, b // SUBS), b % SUBS)
            nc.vector.tensor_tensor(h, bank_in_runs(ub_banks[c, b]), acts[c, b], MULT)

        def vector_block(c, b):
            gelu(c, b)
            ub_for_vector(c, b)
            vector_product(c, b)

        def quantise(c):
            nc.vector.quantize_mx(out=h_codes[c][:].bitcast(FP8X4), scales=h_planes[c][:], in_=h_of[c])

        def down(c, n, y):
            bank = turn(scalar_banks)
            for a in range(R_PASSES):
                nc.tensor.matmul_mx(
                    out=bank[:],
                    lhsT=wd[:, a, 2 * n * P : 2 * (n + 1) * P].bitcast(FP4X4),
                    lhsT_scale=late_planes[:, LATE_WD + a * N + n * P : LATE_WD + a * N + (n + 1) * P],
                    rhs=h_codes[c][:, a * CHUNK : (a + 1) * CHUNK].bitcast(FP8X4),
                    rhs_scale=h_planes[c][:, a * CHUNK : (a + 1) * CHUNK],
                    start=(a == 0),
                    stop=(a == R_PASSES - 1),
                )
            nc.scalar.copy(
                y.rearrange("p (s k j) -> p s k j", s=SUBS, k=RUNS), bank[:].rearrange("p (k s j) -> p s k j", s=SUBS, k=RUNS)
            )

        def gate_step(c, n, res=None, y=None, cuts=(0, CHUNK)):
            y = turn(feed_ring)[:] if y is None else y
            res = turn(res_ring)[:] if res is None else res
            down(c, n, y)
            for first, end in zip(cuts, cuts[1:]):
                picked = gates[n][:].indirect(entries(c * CHUNK + first, c * CHUNK + end))
                nc.vector.tensor_tensor(res[:, first:end], picked, y[:, first:end], MULT)
                nc.sync.dma_start(out[n * P : (n + 1) * P, c * CHUNK + first : c * CHUNK + end], res[:, first:end])

        def vector_blocks(c):
            return [b for b in range(BLOCKS) if b not in paired(c)]

        blocks = vector_blocks(0)
        for b in blocks[:2]:
            gelu(0, b)
        gpsimd_product(0)
        for i, b in enumerate(blocks):
            for ahead in blocks[i + 2 : i + 3]:
                gelu(0, ahead)
            ub_for_vector(0, b)
            vector_product(0, b)
        quantise(0)
        blocks = vector_blocks(1)
        for b in blocks[:2]:
            vector_block(1, b)
        gpsimd_product(1)
        for b in blocks[2:]:
            vector_block(1, b)

        def cycle(c, units):
            gate_step(*units[0])
            quantise(c - 1)
            for unit in units[1:-1]:
                gate_step(*unit)
            first = 3 * BLOCK + PACK * RUN
            gate_step(*units[-1], None, h_of[c][:, first : first + 2 * BLOCK].bitcast(F32))
            gpsimd_product(c)
            for b in vector_blocks(c):
                vector_block(c, b)

        cycle(2, [(0, 0), (0, 1)])
        cycle(3, [(1, 0), (1, 1), (0, 2), (1, 2)])
        gate_step(2, 0)
        quantise(3)
        for unit in ((2, 1), (2, 2), (0, 3), (1, 3), (2, 3)):
            gate_step(*unit)
        for n in range(N_TILES):
            gate_step(3, n, None, None, (0, CHUNK) if n + 1 < N_TILES else (0, CHUNK - SUB, CHUNK))
